import numpy as np
import ml_dtypes


def mxq(x, axis, fmt="e4m3"):
    dtype, down = {"e4m3": (ml_dtypes.float8_e4m3fn, 7), "e5m2": (ml_dtypes.float8_e5m2, 14)}[fmt]
    v = np.moveaxis(np.asarray(x, np.float32).astype(ml_dtypes.bfloat16).astype(np.float64), axis, -1)
    blocks = v.reshape(v.shape[:-1] + (-1, 32))
    amax = np.abs(blocks).max(-1, keepdims=True)
    byte = np.maximum(np.where(amax > 0, np.frexp(amax)[1] - 1 + 127, 0) - down, 1)
    scale = np.exp2(byte - 127.0)
    codes = (blocks / scale).astype(np.float32).astype(dtype).astype(np.float64)
    return np.moveaxis((codes * scale).reshape(v.shape), -1, axis)


WIDE = False


def mx_kscale(k):
    if not WIDE:
        return np.ones(k)
    levels = np.array([10, -10, 5, -5, 0])
    if k % 512:
        return np.exp2(np.random.permutation(np.resize(levels, k // 32))).repeat(32)
    a = np.empty((k // 512, 16))
    for p in range(k // 512):
        a[p, :8] = np.random.permutation(np.resize(levels, 8))
        for g in range(8):
            far = levels[np.abs(levels - a[p, g]) >= 10]
            a[p, g + 8] = far[np.random.randint(len(far))]
    return np.exp2(a.ravel()).repeat(32)


def f64(x):
    return np.asarray(x).astype(np.float64)


def striped(idx):
    return np.tile(np.asarray(idx).reshape(-1, 16).T, (8, 1)).astype(np.uint16)


def unstriped(offs):
    return offs[:16].T.reshape(-1).astype(np.int64)


E2M1 = np.array([0.0, 0.5, 1.0, 1.5, 2.0, 3.0, 4.0, 6.0, -0.0, -0.5, -1.0, -1.5, -2.0, -3.0, -4.0, -6.0])


def pack_weight(w, fmt):
    k, n = w.shape
    w = f64(np.asarray(w, np.float32).astype(ml_dtypes.bfloat16)).reshape(k // 32, 32, n)
    amax = np.abs(w).max(1)
    if fmt == "e4m3":
        byte = np.frexp(amax)[1] - 1 + 127 - 7
    else:
        mant, ex = np.frexp(amax / 6.0)
        byte = np.where(mant > 0.5, ex, ex - 1) + 127
    byte = np.clip(np.where(amax > 0, byte, 1), 1, 254)
    scaled = (w * np.exp2(127.0 - byte)[:, None, :]).reshape(k, n).astype(np.float32)
    by_word = np.ascontiguousarray(scaled.reshape(k // 512, 128, 4, n).transpose(0, 1, 3, 2))
    if fmt == "e4m3":
        words = by_word.astype(ml_dtypes.float8_e4m3fn).view(np.uint8)
    else:
        c = by_word.astype(ml_dtypes.float4_e2m1fn).view(np.uint8) & 0xF
        words = (c[..., 0::2] | (c[..., 1::2] << 4)).reshape(k // 512, 128, 2 * n)
    return np.ascontiguousarray(words), np.ascontiguousarray(byte.astype(np.uint8).reshape(k // 512, 16, n))


def unpack_weight(words, scales, fmt):
    g, _, n = scales.shape
    words = np.ascontiguousarray(words).reshape(g, 128, n, -1)
    if fmt == "e4m3":
        vals = words.view(ml_dtypes.float8_e4m3fn).astype(np.float64)
    else:
        nib = np.empty((g, 128, n, 4), np.uint8)
        nib[..., 0::2] = words & 0xF
        nib[..., 1::2] = words >> 4
        vals = E2M1[nib]
    vals = vals * np.repeat(np.exp2(scales.astype(np.float64) - 127.0), 8, axis=1)[..., None]
    return vals.transpose(0, 1, 3, 2).reshape(g * 512, n)


B, N, T, D, DV, NQ = 1, 1024, 4096, 1024, 128, 256
PAGE = 512


def setup_inputs():
    n = np.random.standard_normal
    pages = np.random.permutation(T // PAGE)[:B * N // PAGE]
    idx = (pages[:, None] * PAGE + np.arange(PAGE)[None, :]).reshape(-1)
    s = mx_kscale(D)[:, None]
    u = np.ones(T)
    u[idx] = mx_kscale(B * N)
    r = np.random.uniform(0.5, 2.0, T)
    qp = [pack_weight(x, "e4m3") for x in n((B, D, NQ)) * s * (1.00 / np.sqrt(D))]
    k = n((D, T)) / s
    v = n((DV, T)) / (u * r)
    kp = pack_weight(k, "e2m1")
    vp = pack_weight(v.T, "e4m3")
    return {
        "q_words": np.stack([x[0] for x in qp]),
        "q_scales": np.stack([x[1] for x in qp]),
        "k_words": np.ascontiguousarray(kp[0].reshape(D // 1024, 2, 128, T, 2).transpose(0, 2, 3, 1, 4)).reshape(D // 1024, 128, T, 4),
        "k_scales": kp[1],
        "v_words": vp[0],
        "v_scales": vp[1],
        "vs": np.tile(u * r, (128, 1)).astype(np.float32),
        "og": n((B, NQ, DV)).astype(np.float32),
        "offs": striped(idx),
        "voffs": striped((pages[:, None] * DV + np.arange(DV)[None, :]).reshape(-1)),
    }


def reference(q_words, q_scales, k_words, k_scales, v_words, v_scales, vs, og, offs, voffs):
    idx = unstriped(offs)
    k = unpack_weight(k_words.reshape(D // 1024, 128, T, 2, 2).transpose(0, 3, 1, 2, 4).reshape(D // 512, 128, 2 * T), k_scales, "e2m1")
    v = unpack_weight(v_words, v_scales, "e4m3")
    v = v.reshape(T // 512, 512, DV)[unstriped(voffs)[::DV] // DV].reshape(B, N, DV)
    pick = lambda x: x[:, idx].reshape(x.shape[0], B, N).transpose(1, 0, 2)
    q = np.stack([unpack_weight(q_words[b], q_scales[b], "e4m3") for b in range(B)])
    score = q.transpose(0, 2, 1) @ pick(k)
    p = score / (1.0 + np.exp(-score))
    w = p * pick(f64(vs))[:, :1, :]
    y = mxq(w, 2, "e4m3") @ v
    y = y / 16.0
    y = y / (1.0 + np.exp(-f64(og)))
    return y

@@ -1,0 +1,183 @@
+from contextlib import ExitStack
+
+import concourse.mybir as mybir
+from concourse.masks import make_identity
+
+F32 = mybir.dt.float32
+BF16 = mybir.dt.bfloat16
+I32 = mybir.dt.int32
+U32 = mybir.dt.uint32
+U16 = mybir.dt.uint16
+U8 = mybir.dt.uint8
+FP8X4 = mybir.dt.float8_e4m3fn_x4
+FP4X4 = mybir.dt.float4_e2m1fn_x4
+ACT = mybir.ActivationFunctionType
+ALU = mybir.AluOpType
+
+P = 128
+PACK = 4
+PAGE = P * PACK
+T = 4096
+N = 1024
+NQ = 256
+DV = 128
+PASSES = 2
+PAGES = N // PAGE
+POOL_PAGES = T // PAGE
+Q_TILES = NQ // P
+QUAD = 32
+SECOND = 16
+VS_ROW = P - 1
+
+FLOPS = 2 * NQ * N * (PASSES * PAGE + DV)
+
+
+def tile_attend_pkv4q_silu_gate_kernel(
+    tc, q_words, q_scales, k_words, k_scales, v_words, v_scales, vs, og, offs, voffs, out
+):
+    nc = tc.nc
+    with ExitStack() as ctx:
+        sb = ctx.enter_context(tc.tile_pool(name="sb", bufs=1))
+        ps = ctx.enter_context(tc.psum_pool(name="ps", bufs=1))
+
+        offs_t = sb.tile([P, N // 16], U16, name="offs_t")
+        voffs_t = sb.tile([P, PAGES * DV // 16], U16, name="voffs_t")
+        k_pool = sb.tile([P, T], U32, name="k_pool", align_bytes=64)
+        ks_pool = sb.tile([P, T], U8, name="ks_pool", align_bytes=64)
+        vs_pool = sb.tile([P, T], F32, name="vs_pool", align_bytes=64)
+        v_pool = sb.tile([P, POOL_PAGES * DV], U32, name="v_pool", align_bytes=64)
+        vsc_pool = sb.tile([P, POOL_PAGES * DV], U8, name="vsc_pool", align_bytes=64)
+        q_codes = sb.tile([P, PASSES * NQ], U32, name="q_codes", align_bytes=64)
+        q_plane = sb.tile([P, PASSES * NQ], U8, name="q_plane", align_bytes=64)
+        ks_second = sb.tile([P, N], U8, name="ks_second", align_bytes=64)
+        og_t = sb.tile([P, Q_TILES, DV], F32, name="og_t")
+        ident = sb.tile([P, P], F32, name="ident")
+
+        nc.vector.memset(q_plane[:].bitcast(I32), 0)
+        nc.vector.memset(ks_pool[:].bitcast(I32), 0)
+        nc.vector.memset(vsc_pool[:].bitcast(I32), 0)
+        nc.vector.memset(vs_pool[0:VS_ROW, :], 0.0)
+
+        nc.sync.dma_start(offs_t[:], offs)
+        nc.scalar.dma_start(out=vs_pool[VS_ROW:P, :], in_=vs[0:1, :])
+        nc.sync.dma_start(voffs_t[:], voffs)
+        nc.scalar.dma_start(out=og_t[:], in_=og[0].rearrange("(h p) e -> p h e", p=P))
+        nc.sync.dma_start(out=k_pool[:].bitcast(I32), in_=k_words[0].rearrange("p t b -> p (t b)").bitcast(I32))
+        for r in range(PACK):
+            nc.scalar.dma_start(
+                out=ks_pool[r:P:SECOND, :].bitcast(I32),
+                in_=k_scales[:, r::PACK, :].rearrange("o g t -> g o t").bitcast(I32),
+            )
+        nc.sync.dma_start(
+            out=q_codes[:].bitcast(I32).rearrange("p (o q) -> p o q", o=PASSES),
+            in_=q_words[0].rearrange("o p q b -> p o (q b)").bitcast(I32),
+        )
+        nc.sync.dma_start(
+            out=v_pool[:].bitcast(I32).rearrange("p (u e) -> p u e", u=POOL_PAGES),
+            in_=v_words.rearrange("u p e b -> p u (e b)").bitcast(I32),
+        )
+
+        vs_g = sb.tile([P, N], F32, name="vs_g")
+        nc.vector.tensor_copy(vs_g[:], vs_pool[:].indirect(offs_t[:]))
+        ks_g = sb.tile([P, N], U8, name="ks_g", align_bytes=64)
+        nc.vector.tensor_copy(ks_g[:], ks_pool[:].indirect(offs_t[:]))
+
+        nc.vector.memset(ks_second[:].bitcast(I32), 0)
+        nc.vector.memset(ident[:], 0.0)
+        for r in range(PACK):
+            nc.gpsimd.dma_start(
+                out=q_plane[r:P:QUAD, :].bitcast(I32).rearrange("g (o q) -> g o q", o=PASSES),
+                in_=q_scales[0][:, r::PACK, :].rearrange("o g q -> g o q").bitcast(I32),
+            )
+        for r in range(PACK):
+            nc.gpsimd.dma_start(
+                out=vsc_pool[r:P:QUAD, :].bitcast(I32).rearrange("g (u e) -> g u e", u=POOL_PAGES),
+                in_=v_scales[:, r::PACK, :].rearrange("u g e -> g u e").bitcast(I32),
+            )
+
+        make_identity(nc, ident[:], nomemset=True)
+
+        ks_first = sb.tile([P, N], U8, name="ks_first", align_bytes=64)
+        nc.vector.tensor_copy(
+            ks_first[:].rearrange("p (u r s) -> p u s r", u=PAGES, r=PACK),
+            ks_g[:].rearrange("p (u s r) -> p u s r", u=PAGES, r=PACK),
+        )
+        nc.scalar.dma_start(out=ks_second[0 : P - SECOND, :].bitcast(I32), in_=ks_first[SECOND:P, :].bitcast(I32))
+        k_planes = [ks_first, ks_second]
+
+        gate = sb.tile([P, Q_TILES, DV], F32, name="gate")
+        nc.scalar.activation(out=gate[:], in_=og_t[:], func=ACT.Sigmoid)
+
+        vs_col = []
+        for u in range(PAGES):
+            turned = ps.tile([P, PACK, P], F32, name="turned%d" % u)
+            for r in range(PACK):
+                nc.tensor.transpose(turned[:, r, :], vs_g[:, u * PAGE + r : (u + 1) * PAGE : PACK], ident[:])
+            col = sb.tile([P, PACK], F32, name="vs_col%d" % u)
+            nc.scalar.copy(col[:], turned[:, :, VS_ROW])
+            vs_col.append(col)
+
+        k_codes = []
+        for u in range(PAGES):
+            k_g = sb.tile([P, PAGE], U32, name="k_g%d" % u, align_bytes=64)
+            nc.vector.tensor_copy(k_g[:], k_pool[:].indirect(offs_t[:, u * PAGE // 16 : (u + 1) * PAGE // 16]))
+            codes = sb.tile([P, PASSES * PAGE], U16, name="k_codes%d" % u, align_bytes=64)
+            nc.vector.tensor_copy(
+                codes[:].rearrange("p (o r s) -> p o s r", o=PASSES, r=PACK),
+                k_g[:].bitcast(U16).rearrange("p (s r o) -> p o s r", o=PASSES, r=PACK),
+            )
+            k_codes.append(codes)
+
+        v_g = sb.tile([P, PAGES * DV], U32, name="v_g", align_bytes=64)
+        nc.vector.tensor_copy(v_g[:], v_pool[:].indirect(voffs_t[:]))
+        vsc_g = sb.tile([P, PAGES * DV], U8, name="vsc_g", align_bytes=64)
+        nc.vector.tensor_copy(vsc_g[:], vsc_pool[:].indirect(voffs_t[:]))
+
+        y = [ps.tile([P, DV], F32, name="y%d" % h) for h in range(Q_TILES)]
+        weights = {}
+        for u in range(PAGES):
+            for h in range(Q_TILES):
+                scores = ps.tile([P, PACK, P], F32, name="scores%d%d" % (u, h))
+                for r in range(PACK):
+                    for o in range(PASSES):
+                        k0 = o * PAGE + r * P
+                        s0 = u * PAGE + r * P
+                        q0 = o * NQ + h * P
+                        nc.tensor.matmul_mx(
+                            out=scores[:, r, :],
+                            lhsT=k_codes[u][:, k0 : k0 + P].bitcast(FP4X4),
+                            lhsT_scale=k_planes[o][:, s0 : s0 + P],
+                            rhs=q_codes[:, q0 : q0 + P].bitcast(FP8X4),
+                            rhs_scale=q_plane[:, q0 : q0 + P],
+                            start=(o == 0),
+                            stop=(o == PASSES - 1),
+                        )
+                silu = sb.tile([P, P, PACK], F32, name="silu%d%d" % (u, h))
+                nc.scalar.activation(out=silu[:], in_=scores[:].rearrange("p r q -> p q r"), func=ACT.Silu)
+                w = sb.tile([P, P, PACK], BF16, name="w%d%d" % (u, h), align_bytes=64)
+                nc.vector.tensor_tensor(w[:], silu[:], vs_col[u][:].unsqueeze(1).to_broadcast([P, P, PACK]), ALU.mult)
+                weights[(u, h)] = w
+
+        for u in range(PAGES):
+            for h in range(Q_TILES):
+                w_codes = sb.tile([P, P], U32, name="w_codes%d%d" % (u, h), align_bytes=64)
+                w_plane = sb.tile([P, P], U8, name="w_plane%d%d" % (u, h), align_bytes=64)
+                nc.vector.quantize_mx(
+                    out=w_codes[:].bitcast(FP8X4),
+                    scales=w_plane[:],
+                    in_=weights[(u, h)][:].rearrange("p q r -> p (q r)"),
+                )
+                nc.tensor.matmul_mx(
+                    out=y[h][:],
+                    lhsT=w_codes[:].bitcast(FP8X4),
+                    lhsT_scale=w_plane[:],
+                    rhs=v_g[:, u * DV : (u + 1) * DV].bitcast(FP8X4),
+                    rhs_scale=vsc_g[:, u * DV : (u + 1) * DV],
+                    start=(u == 0),
+                    stop=(u == PAGES - 1),
+                )
+
+        for h in range(Q_TILES):
+            res = sb.tile([P, DV], F32, name="res%d" % h)
+            nc.vector.scalar_tensor_tensor(res[:], y[h][:], 1.0 / 16.0, gate[:, h, :], ALU.mult, ALU.mult)
+            nc.sync.dma_start(out=out[0, h * P : (h + 1) * P, :], in_=res[:])

@@ -28,6 +28,7 @@ Q_TILES = NQ // P
 QUAD = 32
 SECOND = 16
 VS_ROW = P - 1
+WARM = (512, 512, 128)
 
 FLOPS = 2 * NQ * N * (PASSES * PAGE + DV)
 
@@ -38,72 +39,100 @@ def tile_attend_pkv4q_silu_gate_kernel(
     nc = tc.nc
     with ExitStack() as ctx:
         sb = ctx.enter_context(tc.tile_pool(name="sb", bufs=1))
+        shared = ctx.enter_context(tc.tile_pool(name="shared", bufs=1))
         ps = ctx.enter_context(tc.psum_pool(name="ps", bufs=1))
 
         offs_t = sb.tile([P, N // 16], U16, name="offs_t")
         voffs_t = sb.tile([P, PAGES * DV // 16], U16, name="voffs_t")
         k_pool = sb.tile([P, T], U32, name="k_pool", align_bytes=64)
-        ks_pool = sb.tile([P, T], U8, name="ks_pool", align_bytes=64)
-        vs_pool = sb.tile([P, T], F32, name="vs_pool", align_bytes=64)
-        v_pool = sb.tile([P, POOL_PAGES * DV], U32, name="v_pool", align_bytes=64)
-        vsc_pool = sb.tile([P, POOL_PAGES * DV], U8, name="vsc_pool", align_bytes=64)
+        ks_pool = shared.tile([P, T], U8, name="ks_pool", align_bytes=64, offset=4 * T)
+        vs_pool = shared.tile([P, T], F32, name="vs_pool", align_bytes=64, offset=0)
         q_codes = sb.tile([P, PASSES * NQ], U32, name="q_codes", align_bytes=64)
-        q_plane = sb.tile([P, PASSES * NQ], U8, name="q_plane", align_bytes=64)
-        ks_second = sb.tile([P, N], U8, name="ks_second", align_bytes=64)
+        planes = sb.tile([P, PASSES * NQ + N], U8, name="planes", align_bytes=64)
+        q_plane = planes[:, 0 : PASSES * NQ]
+        ks_second = planes[:, PASSES * NQ : PASSES * NQ + N]
         og_t = sb.tile([P, Q_TILES, DV], F32, name="og_t")
         ident = sb.tile([P, P], F32, name="ident")
 
-        nc.vector.memset(q_plane[:].bitcast(I32), 0)
+        make_identity(nc, ident[:])
         nc.vector.memset(ks_pool[:].bitcast(I32), 0)
-        nc.vector.memset(vsc_pool[:].bitcast(I32), 0)
         nc.vector.memset(vs_pool[0:VS_ROW, :], 0.0)
+        nc.vector.memset(planes[:].bitcast(I32), 0)
 
         nc.sync.dma_start(offs_t[:], offs)
         nc.scalar.dma_start(out=vs_pool[VS_ROW:P, :], in_=vs[0:1, :])
         nc.sync.dma_start(voffs_t[:], voffs)
         nc.scalar.dma_start(out=og_t[:], in_=og[0].rearrange("(h p) e -> p h e", p=P))
+        nc.sync.dma_start(
+            out=q_codes[:].bitcast(I32).rearrange("p (o q) -> p o q", o=PASSES),
+            in_=q_words[0].rearrange("o p q b -> p o (q b)").bitcast(I32),
+        )
         nc.sync.dma_start(out=k_pool[:].bitcast(I32), in_=k_words[0].rearrange("p t b -> p (t b)").bitcast(I32))
         for r in range(PACK):
             nc.scalar.dma_start(
                 out=ks_pool[r:P:SECOND, :].bitcast(I32),
                 in_=k_scales[:, r::PACK, :].rearrange("o g t -> g o t").bitcast(I32),
             )
-        nc.sync.dma_start(
-            out=q_codes[:].bitcast(I32).rearrange("p (o q) -> p o q", o=PASSES),
-            in_=q_words[0].rearrange("o p q b -> p o (q b)").bitcast(I32),
-        )
+        for r in range(PACK):
+            nc.sync.dma_start(
+                out=q_plane[r:P:QUAD, :].bitcast(I32).rearrange("g (o q) -> g o q", o=PASSES),
+                in_=q_scales[0][:, r::PACK, :].rearrange("o g q -> g o q").bitcast(I32),
+            )
+
+        page_offs = [offs_t[:, u * PAGE // 16 : (u + 1) * PAGE // 16] for u in range(PAGES)]
+        vs_g = sb.tile([P, N], F32, name="vs_g")
+        nc.vector.tensor_copy(vs_g[:], vs_pool[:].indirect(offs_t[:]))
+        vsc_pool = shared.tile([P, POOL_PAGES * DV], U8, name="vsc_pool", align_bytes=64, offset=3 * T)
+        nc.vector.memset(vsc_pool[:].bitcast(I32), 0)
+        for r in range(PACK):
+            nc.scalar.dma_start(
+                out=vsc_pool[r:P:QUAD, :].bitcast(I32).rearrange("g (u e) -> g u e", u=POOL_PAGES),
+                in_=v_scales[:, r::PACK, :].rearrange("u g e -> g u e").bitcast(I32),
+            )
+        ks_g = []
+        for u in range(PAGES):
+            gathered = shared.tile([P, PAGE], U8, name="ks_g%d" % u, align_bytes=64, offset=2 * T * u)
+            nc.vector.tensor_copy(gathered[:], ks_pool[:].indirect(page_offs[u]))
+            ks_g.append(gathered)
+
+        ks_first = [sb.tile([P, PAGE], U8, name="ks_first%d" % u, align_bytes=64) for u in range(PAGES)]
+        k_g = [shared.tile([P, PAGE], U32, name="k_g%d" % u, align_bytes=64, offset=4 * T + 4 * PAGE * u) for u in range(PAGES)]
+        k_codes = [sb.tile([P, PASSES * PAGE], U16, name="k_codes%d" % u, align_bytes=64) for u in range(PAGES)]
+
+        def deal_scales(u):
+            nc.vector.tensor_copy(
+                ks_first[u][:].rearrange("p (r s) -> p s r", r=PACK),
+                ks_g[u][:].rearrange("p (s r) -> p s r", r=PACK),
+            )
+            nc.sync.dma_start(
+                out=ks_second[0 : P - SECOND, u * PAGE : (u + 1) * PAGE].bitcast(I32),
+                in_=ks_first[u][SECOND:P, :].bitcast(I32),
+            )
+
+        def gather_keys(u):
+            nc.vector.tensor_copy(k_g[u][:], k_pool[:].indirect(page_offs[u]))
+
+        def part_keys(u):
+            nc.vector.tensor_copy(
+                k_codes[u][:].rearrange("p (o r s) -> p o s r", o=PASSES, r=PACK),
+                k_g[u][:].bitcast(U16).rearrange("p (s r o) -> p o s r", o=PASSES, r=PACK),
+            )
+
+        deal_scales(0)
+        v_pool = shared.tile([P, POOL_PAGES * DV], U32, name="v_pool", align_bytes=64, offset=0)
         nc.sync.dma_start(
             out=v_pool[:].bitcast(I32).rearrange("p (u e) -> p u e", u=POOL_PAGES),
             in_=v_words.rearrange("u p e b -> p u (e b)").bitcast(I32),
         )
-
-        vs_g = sb.tile([P, N], F32, name="vs_g")
-        nc.vector.tensor_copy(vs_g[:], vs_pool[:].indirect(offs_t[:]))
-        ks_g = sb.tile([P, N], U8, name="ks_g", align_bytes=64)
-        nc.vector.tensor_copy(ks_g[:], ks_pool[:].indirect(offs_t[:]))
-
-        nc.vector.memset(ks_second[:].bitcast(I32), 0)
-        nc.vector.memset(ident[:], 0.0)
-        for r in range(PACK):
-            nc.gpsimd.dma_start(
-                out=q_plane[r:P:QUAD, :].bitcast(I32).rearrange("g (o q) -> g o q", o=PASSES),
-                in_=q_scales[0][:, r::PACK, :].rearrange("o g q -> g o q").bitcast(I32),
-            )
-        for r in range(PACK):
-            nc.gpsimd.dma_start(
-                out=vsc_pool[r:P:QUAD, :].bitcast(I32).rearrange("g (u e) -> g u e", u=POOL_PAGES),
-                in_=v_scales[:, r::PACK, :].rearrange("u g e -> g u e").bitcast(I32),
-            )
-
-        make_identity(nc, ident[:], nomemset=True)
-
-        ks_first = sb.tile([P, N], U8, name="ks_first", align_bytes=64)
-        nc.vector.tensor_copy(
-            ks_first[:].rearrange("p (u r s) -> p u s r", u=PAGES, r=PACK),
-            ks_g[:].rearrange("p (u s r) -> p u s r", u=PAGES, r=PACK),
-        )
-        nc.scalar.dma_start(out=ks_second[0 : P - SECOND, :].bitcast(I32), in_=ks_first[SECOND:P, :].bitcast(I32))
-        k_planes = [ks_first, ks_second]
+        gather_keys(0)
+        deal_scales(1)
+        part_keys(0)
+        gather_keys(1)
+        v_g = shared.tile([P, PAGES * DV], U32, name="v_g", align_bytes=64, offset=4 * T)
+        nc.vector.tensor_copy(v_g[:], v_pool[:].indirect(voffs_t[:]))
+        part_keys(1)
+        vsc_g = shared.tile([P, PAGES * DV], U8, name="vsc_g", align_bytes=64, offset=4 * T + 4 * PAGES * DV)
+        nc.vector.tensor_copy(vsc_g[:], vsc_pool[:].indirect(voffs_t[:]))
 
         gate = sb.tile([P, Q_TILES, DV], F32, name="gate")
         nc.scalar.activation(out=gate[:], in_=og_t[:], func=ACT.Sigmoid)
@@ -117,23 +146,18 @@ def tile_attend_pkv4q_silu_gate_kernel(
             nc.scalar.copy(col[:], turned[:, :, VS_ROW])
             vs_col.append(col)
 
-        k_codes = []
-        for u in range(PAGES):
-            k_g = sb.tile([P, PAGE], U32, name="k_g%d" % u, align_bytes=64)
-            nc.vector.tensor_copy(k_g[:], k_pool[:].indirect(offs_t[:, u * PAGE // 16 : (u + 1) * PAGE // 16]))
-            codes = sb.tile([P, PASSES * PAGE], U16, name="k_codes%d" % u, align_bytes=64)
-            nc.vector.tensor_copy(
-                codes[:].rearrange("p (o r s) -> p o s r", o=PASSES, r=PACK),
-                k_g[:].bitcast(U16).rearrange("p (s r o) -> p o s r", o=PASSES, r=PACK),
+        warm = ps.tile([P, PASSES * NQ], F32, name="warm", tag="y0")
+        for width in WARM:
+            nc.tensor.matmul_mx(
+                out=warm[:, 0:width],
+                lhsT=q_codes[:, 0:P].bitcast(FP8X4),
+                lhsT_scale=ks_first[0][:, 0:P],
+                rhs=q_codes[:, 0:width].bitcast(FP8X4),
+                rhs_scale=ks_first[0][:, 0:width],
+                start=True,
+                stop=True,
             )
-            k_codes.append(codes)
-
-        v_g = sb.tile([P, PAGES * DV], U32, name="v_g", align_bytes=64)
-        nc.vector.tensor_copy(v_g[:], v_pool[:].indirect(voffs_t[:]))
-        vsc_g = sb.tile([P, PAGES * DV], U8, name="vsc_g", align_bytes=64)
-        nc.vector.tensor_copy(vsc_g[:], vsc_pool[:].indirect(voffs_t[:]))
-
-        y = [ps.tile([P, DV], F32, name="y%d" % h) for h in range(Q_TILES)]
+        y = [ps.tile([P, DV], F32, name="y%d" % h, tag="y%d" % h) for h in range(Q_TILES)]
         weights = {}
         for u in range(PAGES):
             for h in range(Q_TILES):
@@ -146,7 +170,7 @@ def tile_attend_pkv4q_silu_gate_kernel(
                         nc.tensor.matmul_mx(
                             out=scores[:, r, :],
                             lhsT=k_codes[u][:, k0 : k0 + P].bitcast(FP4X4),
-                            lhsT_scale=k_planes[o][:, s0 : s0 + P],
+                            lhsT_scale=ks_first[u][:, r * P : (r + 1) * P] if o == 0 else ks_second[:, s0 : s0 + P],
                             rhs=q_codes[:, q0 : q0 + P].bitcast(FP8X4),
                             rhs_scale=q_plane[:, q0 : q0 + P],
                             start=(o == 0),

@@ -29,6 +29,8 @@ QUAD = 32
 SECOND = 16
 VS_ROW = P - 1
 WARM = (512, 512, 128)
+VS_SPLIT = 2304
+K_SPLIT = 512
 
 FLOPS = 2 * NQ * N * (PASSES * PAGE + DV)
 
@@ -39,103 +41,87 @@ def tile_attend_pkv4q_silu_gate_kernel(
     nc = tc.nc
     with ExitStack() as ctx:
         sb = ctx.enter_context(tc.tile_pool(name="sb", bufs=1))
-        shared = ctx.enter_context(tc.tile_pool(name="shared", bufs=1))
         ps = ctx.enter_context(tc.psum_pool(name="ps", bufs=1))
 
         offs_t = sb.tile([P, N // 16], U16, name="offs_t")
         voffs_t = sb.tile([P, PAGES * DV // 16], U16, name="voffs_t")
         k_pool = sb.tile([P, T], U32, name="k_pool", align_bytes=64)
-        ks_pool = shared.tile([P, T], U8, name="ks_pool", align_bytes=64, offset=4 * T)
-        vs_pool = shared.tile([P, T], F32, name="vs_pool", align_bytes=64, offset=0)
-        q_codes = sb.tile([P, PASSES * NQ], U32, name="q_codes", align_bytes=64)
-        planes = sb.tile([P, PASSES * NQ + N], U8, name="planes", align_bytes=64)
-        q_plane = planes[:, 0 : PASSES * NQ]
-        ks_second = planes[:, PASSES * NQ : PASSES * NQ + N]
-        og_t = sb.tile([P, Q_TILES, DV], F32, name="og_t")
+        ks_pool = sb.tile([P, T], U8, name="ks_pool", align_bytes=64)
+        vs_pool = sb.tile([P, T], F32, name="vs_pool", align_bytes=64)
+        q_plane = sb.tile([P, PASSES * NQ], U8, name="q_plane", align_bytes=64)
+        ks_second = sb.tile([P, N], U8, name="ks_second", align_bytes=64)
+        vsc_pool = sb.tile([P, POOL_PAGES * DV], U8, name="vsc_pool", align_bytes=64)
         ident = sb.tile([P, P], F32, name="ident")
+        og_t = sb.tile([P, Q_TILES, DV], F32, name="og_t")
+        q_codes = [sb.tile([P, NQ], U32, name="q_codes%d" % o, align_bytes=64) for o in range(PASSES)]
+        v_pool = sb.tile([P, POOL_PAGES * DV], U32, name="v_pool", align_bytes=64)
 
+        nc.gpsimd.memset(ks_pool[:].bitcast(I32), 0)
+        nc.vector.memset(vs_pool[0:VS_ROW, 0 : VS_SPLIT - 1], 0.0)
+        nc.vector.memset(vs_pool[0:VS_ROW, VS_SPLIT - 1 : VS_SPLIT], 0.0)
+        nc.gpsimd.memset(vs_pool[0:VS_ROW, VS_SPLIT:T], 0.0)
+        nc.gpsimd.memset(q_plane[:].bitcast(I32), 0)
+        nc.gpsimd.memset(vsc_pool[:].bitcast(I32), 0)
         make_identity(nc, ident[:])
-        nc.vector.memset(ks_pool[:].bitcast(I32), 0)
-        nc.vector.memset(vs_pool[0:VS_ROW, :], 0.0)
-        nc.vector.memset(planes[:].bitcast(I32), 0)
+        nc.gpsimd.memset(ks_second[:].bitcast(I32), 0)
 
+        k_src = k_words[0].rearrange("p t b -> p (t b)").bitcast(I32)
         nc.sync.dma_start(offs_t[:], offs)
-        nc.scalar.dma_start(out=vs_pool[VS_ROW:P, :], in_=vs[0:1, :])
+        nc.sync.dma_start(out=vs_pool[VS_ROW:P, :], in_=vs[0:1, :])
         nc.sync.dma_start(voffs_t[:], voffs)
-        nc.scalar.dma_start(out=og_t[:], in_=og[0].rearrange("(h p) e -> p h e", p=P))
+        nc.sync.dma_start(out=og_t[:], in_=og[0].rearrange("(h p) e -> p h e", p=P))
+        for o in range(PASSES):
+            nc.sync.dma_start(out=q_codes[o][:].bitcast(I32), in_=q_words[0, o].rearrange("p q b -> p (q b)").bitcast(I32))
         nc.sync.dma_start(
-            out=q_codes[:].bitcast(I32).rearrange("p (o q) -> p o q", o=PASSES),
-            in_=q_words[0].rearrange("o p q b -> p o (q b)").bitcast(I32),
+            out=v_pool[:].bitcast(I32).rearrange("p (u e) -> p u e", u=POOL_PAGES),
+            in_=v_words.rearrange("u p e b -> p u (e b)").bitcast(I32),
         )
-        nc.sync.dma_start(out=k_pool[:].bitcast(I32), in_=k_words[0].rearrange("p t b -> p (t b)").bitcast(I32))
+        nc.sync.dma_start(out=k_pool[:, 0:K_SPLIT].bitcast(I32), in_=k_src[:, 0:K_SPLIT])
         for r in range(PACK):
-            nc.scalar.dma_start(
+            nc.sync.dma_start(
                 out=ks_pool[r:P:SECOND, :].bitcast(I32),
                 in_=k_scales[:, r::PACK, :].rearrange("o g t -> g o t").bitcast(I32),
             )
+        nc.sync.dma_start(out=k_pool[:, K_SPLIT:T].bitcast(I32), in_=k_src[:, K_SPLIT:T])
         for r in range(PACK):
             nc.sync.dma_start(
                 out=q_plane[r:P:QUAD, :].bitcast(I32).rearrange("g (o q) -> g o q", o=PASSES),
                 in_=q_scales[0][:, r::PACK, :].rearrange("o g q -> g o q").bitcast(I32),
             )
+        for r in range(PACK):
+            nc.sync.dma_start(
+                out=vsc_pool[r:P:QUAD, :].bitcast(I32).rearrange("g (u e) -> g u e", u=POOL_PAGES),
+                in_=v_scales[:, r::PACK, :].rearrange("u g e -> g u e").bitcast(I32),
+            )
 
         page_offs = [offs_t[:, u * PAGE // 16 : (u + 1) * PAGE // 16] for u in range(PAGES)]
         vs_g = sb.tile([P, N], F32, name="vs_g")
         nc.vector.tensor_copy(vs_g[:], vs_pool[:].indirect(offs_t[:]))
-        vsc_pool = shared.tile([P, POOL_PAGES * DV], U8, name="vsc_pool", align_bytes=64, offset=3 * T)
-        nc.vector.memset(vsc_pool[:].bitcast(I32), 0)
-        for r in range(PACK):
-            nc.scalar.dma_start(
-                out=vsc_pool[r:P:QUAD, :].bitcast(I32).rearrange("g (u e) -> g u e", u=POOL_PAGES),
-                in_=v_scales[:, r::PACK, :].rearrange("u g e -> g u e").bitcast(I32),
-            )
-        ks_g = []
+
+        ks_g = [sb.tile([P, PAGE], U8, name="ks_g%d" % u, align_bytes=64) for u in range(PAGES)]
         for u in range(PAGES):
-            gathered = shared.tile([P, PAGE], U8, name="ks_g%d" % u, align_bytes=64, offset=2 * T * u)
-            nc.vector.tensor_copy(gathered[:], ks_pool[:].indirect(page_offs[u]))
-            ks_g.append(gathered)
-
-        ks_first = [sb.tile([P, PAGE], U8, name="ks_first%d" % u, align_bytes=64) for u in range(PAGES)]
-        k_g = [shared.tile([P, PAGE], U32, name="k_g%d" % u, align_bytes=64, offset=4 * T + 4 * PAGE * u) for u in range(PAGES)]
-        k_codes = [sb.tile([P, PASSES * PAGE], U16, name="k_codes%d" % u, align_bytes=64) for u in range(PAGES)]
-
-        def deal_scales(u):
+            nc.vector.tensor_copy(ks_g[u][:], ks_pool[:].indirect(page_offs[u]))
+        ks_first = sb.tile([P, N], U8, name="ks_first", align_bytes=64)
+        for u in range(PAGES):
             nc.vector.tensor_copy(
-                ks_first[u][:].rearrange("p (r s) -> p s r", r=PACK),
-                ks_g[u][:].rearrange("p (s r) -> p s r", r=PACK),
+                ks_first[:, u * PAGE : (u + 1) * PAGE].rearrange("p (r s) -> p r s", r=PACK),
+                ks_g[u][:].rearrange("p (s r) -> p r s", r=PACK),
             )
-            nc.sync.dma_start(
-                out=ks_second[0 : P - SECOND, u * PAGE : (u + 1) * PAGE].bitcast(I32),
-                in_=ks_first[u][SECOND:P, :].bitcast(I32),
-            )
+        nc.scalar.dma_start(out=ks_second[0 : P - SECOND, :].bitcast(I32), in_=ks_first[SECOND:P, :].bitcast(I32))
 
-        def gather_keys(u):
+        k_g = [sb.tile([P, PAGE], U32, name="k_g%d" % u, align_bytes=64) for u in range(PAGES)]
+        k_codes = [sb.tile([P, PASSES * PAGE], U16, name="k_codes%d" % u, align_bytes=64) for u in range(PAGES)]
+        for u in range(PAGES):
             nc.vector.tensor_copy(k_g[u][:], k_pool[:].indirect(page_offs[u]))
-
-        def part_keys(u):
+        for u in range(PAGES):
             nc.vector.tensor_copy(
                 k_codes[u][:].rearrange("p (o r s) -> p o s r", o=PASSES, r=PACK),
                 k_g[u][:].bitcast(U16).rearrange("p (s r o) -> p o s r", o=PASSES, r=PACK),
             )
-
-        deal_scales(0)
-        v_pool = shared.tile([P, POOL_PAGES * DV], U32, name="v_pool", align_bytes=64, offset=0)
-        nc.sync.dma_start(
-            out=v_pool[:].bitcast(I32).rearrange("p (u e) -> p u e", u=POOL_PAGES),
-            in_=v_words.rearrange("u p e b -> p u (e b)").bitcast(I32),
-        )
-        gather_keys(0)
-        deal_scales(1)
-        part_keys(0)
-        gather_keys(1)
-        v_g = shared.tile([P, PAGES * DV], U32, name="v_g", align_bytes=64, offset=4 * T)
+        v_g = sb.tile([P, PAGES * DV], U32, name="v_g", align_bytes=64)
         nc.vector.tensor_copy(v_g[:], v_pool[:].indirect(voffs_t[:]))
-        part_keys(1)
-        vsc_g = shared.tile([P, PAGES * DV], U8, name="vsc_g", align_bytes=64, offset=4 * T + 4 * PAGES * DV)
+        vsc_g = sb.tile([P, PAGES * DV], U8, name="vsc_g", align_bytes=64)
         nc.vector.tensor_copy(vsc_g[:], vsc_pool[:].indirect(voffs_t[:]))
-
-        gate = sb.tile([P, Q_TILES, DV], F32, name="gate")
-        nc.scalar.activation(out=gate[:], in_=og_t[:], func=ACT.Sigmoid)
 
         vs_col = []
         for u in range(PAGES):
@@ -146,50 +132,58 @@ def tile_attend_pkv4q_silu_gate_kernel(
             nc.scalar.copy(col[:], turned[:, :, VS_ROW])
             vs_col.append(col)
 
+        half = sb.tile([P, Q_TILES, DV], F32, name="half")
+        gate = sb.tile([P, Q_TILES, DV], F32, name="gate")
+        nc.scalar.activation(out=half[:], in_=og_t[:], func=ACT.Tanh, scale=0.5)
+        nc.scalar.activation(out=gate[:], in_=half[:], func=ACT.Copy, scale=1.0 / 32.0, bias=1.0 / 32.0)
+
         warm = ps.tile([P, PASSES * NQ], F32, name="warm", tag="y0")
         for width in WARM:
             nc.tensor.matmul_mx(
                 out=warm[:, 0:width],
-                lhsT=q_codes[:, 0:P].bitcast(FP8X4),
-                lhsT_scale=ks_first[0][:, 0:P],
-                rhs=q_codes[:, 0:width].bitcast(FP8X4),
-                rhs_scale=ks_first[0][:, 0:width],
+                lhsT=q_codes[0][:, 0:P].bitcast(FP8X4),
+                lhsT_scale=ks_first[:, 0:P],
+                rhs=v_pool[:, 0:width].bitcast(FP8X4),
+                rhs_scale=ks_first[:, 0:width],
                 start=True,
                 stop=True,
             )
         y = [ps.tile([P, DV], F32, name="y%d" % h, tag="y%d" % h) for h in range(Q_TILES)]
-        weights = {}
+        silu = {}
         for u in range(PAGES):
             for h in range(Q_TILES):
                 scores = ps.tile([P, PACK, P], F32, name="scores%d%d" % (u, h))
                 for r in range(PACK):
-                    for o in range(PASSES):
+                    for o in (1, 0):
                         k0 = o * PAGE + r * P
                         s0 = u * PAGE + r * P
                         q0 = o * NQ + h * P
                         nc.tensor.matmul_mx(
                             out=scores[:, r, :],
                             lhsT=k_codes[u][:, k0 : k0 + P].bitcast(FP4X4),
-                            lhsT_scale=ks_first[u][:, r * P : (r + 1) * P] if o == 0 else ks_second[:, s0 : s0 + P],
-                            rhs=q_codes[:, q0 : q0 + P].bitcast(FP8X4),
+                            lhsT_scale=(ks_second if o else ks_first)[:, s0 : s0 + P],
+                            rhs=q_codes[o][:, h * P : (h + 1) * P].bitcast(FP8X4),
                             rhs_scale=q_plane[:, q0 : q0 + P],
-                            start=(o == 0),
-                            stop=(o == PASSES - 1),
+                            start=(o == 1),
+                            stop=(o == 0),
                         )
-                silu = sb.tile([P, P, PACK], F32, name="silu%d%d" % (u, h))
-                nc.scalar.activation(out=silu[:], in_=scores[:].rearrange("p r q -> p q r"), func=ACT.Silu)
-                w = sb.tile([P, P, PACK], BF16, name="w%d%d" % (u, h), align_bytes=64)
-                nc.vector.tensor_tensor(w[:], silu[:], vs_col[u][:].unsqueeze(1).to_broadcast([P, P, PACK]), ALU.mult)
-                weights[(u, h)] = w
+                act = sb.tile([P, P, PACK], F32, name="silu%d%d" % (u, h))
+                nc.scalar.activation(out=act[:], in_=scores[:].rearrange("p r q -> p q r"), func=ACT.Silu)
+                silu[(u, h)] = act
 
         for u in range(PAGES):
+            weights = []
+            for h in range(Q_TILES):
+                w = sb.tile([P, P, PACK], BF16, name="w%d%d" % (u, h), align_bytes=64)
+                nc.vector.tensor_tensor(w[:], silu[(u, h)][:], vs_col[u][:].unsqueeze(1).to_broadcast([P, P, PACK]), ALU.mult)
+                weights.append(w)
             for h in range(Q_TILES):
                 w_codes = sb.tile([P, P], U32, name="w_codes%d%d" % (u, h), align_bytes=64)
                 w_plane = sb.tile([P, P], U8, name="w_plane%d%d" % (u, h), align_bytes=64)
                 nc.vector.quantize_mx(
                     out=w_codes[:].bitcast(FP8X4),
                     scales=w_plane[:],
-                    in_=weights[(u, h)][:].rearrange("p q r -> p (q r)"),
+                    in_=weights[h][:].rearrange("p q r -> p (q r)"),
                 )
                 nc.tensor.matmul_mx(
                     out=y[h][:],
@@ -203,5 +197,5 @@ def tile_attend_pkv4q_silu_gate_kernel(
 
         for h in range(Q_TILES):
             res = sb.tile([P, DV], F32, name="res%d" % h)
-            nc.vector.scalar_tensor_tensor(res[:], y[h][:], 1.0 / 16.0, gate[:, h, :], ALU.mult, ALU.mult)
+            nc.vector.tensor_tensor(res[:], y[h][:], gate[:, h, :], ALU.mult)
             nc.sync.dma_start(out=out[0, h * P : (h + 1) * P, :], in_=res[:])

@@ -29,8 +29,8 @@ QUAD = 32
 SECOND = 16
 VS_ROW = P - 1
 WARM = (512, 512, 128)
-VS_SPLIT = 2304
-K_SPLIT = 512
+K_PIECE = 512
+K_SPLIT = 2 * K_PIECE
 
 FLOPS = 2 * NQ * N * (PASSES * PAGE + DV)
 
@@ -41,6 +41,7 @@ def tile_attend_pkv4q_silu_gate_kernel(
     nc = tc.nc
     with ExitStack() as ctx:
         sb = ctx.enter_context(tc.tile_pool(name="sb", bufs=1))
+        shared = ctx.enter_context(tc.tile_pool(name="shared", bufs=1))
         ps = ctx.enter_context(tc.psum_pool(name="ps", bufs=1))
 
         offs_t = sb.tile([P, N // 16], U16, name="offs_t")
@@ -53,17 +54,15 @@ def tile_attend_pkv4q_silu_gate_kernel(
         vsc_pool = sb.tile([P, POOL_PAGES * DV], U8, name="vsc_pool", align_bytes=64)
         ident = sb.tile([P, P], F32, name="ident")
         og_t = sb.tile([P, Q_TILES, DV], F32, name="og_t")
-        q_codes = [sb.tile([P, NQ], U32, name="q_codes%d" % o, align_bytes=64) for o in range(PASSES)]
+        q_codes = sb.tile([P, PASSES * NQ], U32, name="q_codes", align_bytes=64)
         v_pool = sb.tile([P, POOL_PAGES * DV], U32, name="v_pool", align_bytes=64)
 
-        nc.gpsimd.memset(ks_pool[:].bitcast(I32), 0)
-        nc.vector.memset(vs_pool[0:VS_ROW, 0 : VS_SPLIT - 1], 0.0)
-        nc.vector.memset(vs_pool[0:VS_ROW, VS_SPLIT - 1 : VS_SPLIT], 0.0)
-        nc.gpsimd.memset(vs_pool[0:VS_ROW, VS_SPLIT:T], 0.0)
-        nc.gpsimd.memset(q_plane[:].bitcast(I32), 0)
-        nc.gpsimd.memset(vsc_pool[:].bitcast(I32), 0)
         make_identity(nc, ident[:])
-        nc.gpsimd.memset(ks_second[:].bitcast(I32), 0)
+        nc.vector.memset(ks_pool[:].bitcast(I32), 0)
+        nc.vector.memset(vsc_pool[:].bitcast(I32), 0)
+        nc.vector.memset(q_plane[:].bitcast(I32), 0)
+        nc.vector.memset(vs_pool[0:VS_ROW, :], 0.0)
+        nc.vector.memset(ks_second[:].bitcast(I32), 0)
 
         k_src = k_words[0].rearrange("p t b -> p (t b)").bitcast(I32)
         nc.sync.dma_start(offs_t[:], offs)
@@ -71,12 +70,12 @@ def tile_attend_pkv4q_silu_gate_kernel(
         nc.sync.dma_start(voffs_t[:], voffs)
         nc.sync.dma_start(out=og_t[:], in_=og[0].rearrange("(h p) e -> p h e", p=P))
         for o in range(PASSES):
-            nc.sync.dma_start(out=q_codes[o][:].bitcast(I32), in_=q_words[0, o].rearrange("p q b -> p (q b)").bitcast(I32))
-        nc.sync.dma_start(
-            out=v_pool[:].bitcast(I32).rearrange("p (u e) -> p u e", u=POOL_PAGES),
-            in_=v_words.rearrange("u p e b -> p u (e b)").bitcast(I32),
-        )
-        nc.sync.dma_start(out=k_pool[:, 0:K_SPLIT].bitcast(I32), in_=k_src[:, 0:K_SPLIT])
+            nc.sync.dma_start(
+                out=q_codes[:, o * NQ : (o + 1) * NQ].bitcast(I32),
+                in_=q_words[0, o].rearrange("p q b -> p (q b)").bitcast(I32),
+            )
+        for c in range(0, K_SPLIT, K_PIECE):
+            nc.sync.dma_start(out=k_pool[:, c : c + K_PIECE].bitcast(I32), in_=k_src[:, c : c + K_PIECE])
         for r in range(PACK):
             nc.sync.dma_start(
                 out=ks_pool[r:P:SECOND, :].bitcast(I32),
@@ -88,8 +87,12 @@ def tile_attend_pkv4q_silu_gate_kernel(
                 out=q_plane[r:P:QUAD, :].bitcast(I32).rearrange("g (o q) -> g o q", o=PASSES),
                 in_=q_scales[0][:, r::PACK, :].rearrange("o g q -> g o q").bitcast(I32),
             )
+        nc.sync.dma_start(
+            out=v_pool[:].bitcast(I32).rearrange("p (u e) -> p u e", u=POOL_PAGES),
+            in_=v_words.rearrange("u p e b -> p u (e b)").bitcast(I32),
+        )
         for r in range(PACK):
-            nc.sync.dma_start(
+            nc.gpsimd.dma_start(
                 out=vsc_pool[r:P:QUAD, :].bitcast(I32).rearrange("g (u e) -> g u e", u=POOL_PAGES),
                 in_=v_scales[:, r::PACK, :].rearrange("u g e -> g u e").bitcast(I32),
             )
@@ -109,7 +112,7 @@ def tile_attend_pkv4q_silu_gate_kernel(
             )
         nc.scalar.dma_start(out=ks_second[0 : P - SECOND, :].bitcast(I32), in_=ks_first[SECOND:P, :].bitcast(I32))
 
-        k_g = [sb.tile([P, PAGE], U32, name="k_g%d" % u, align_bytes=64) for u in range(PAGES)]
+        k_g = [shared.tile([P, PAGE], U32, name="k_g%d" % u, align_bytes=64, offset=4 * PAGE * u) for u in range(PAGES)]
         k_codes = [sb.tile([P, PASSES * PAGE], U16, name="k_codes%d" % u, align_bytes=64) for u in range(PAGES)]
         for u in range(PAGES):
             nc.vector.tensor_copy(k_g[u][:], k_pool[:].indirect(page_offs[u]))
@@ -118,9 +121,9 @@ def tile_attend_pkv4q_silu_gate_kernel(
                 k_codes[u][:].rearrange("p (o r s) -> p o s r", o=PASSES, r=PACK),
                 k_g[u][:].bitcast(U16).rearrange("p (s r o) -> p o s r", o=PASSES, r=PACK),
             )
-        v_g = sb.tile([P, PAGES * DV], U32, name="v_g", align_bytes=64)
+        v_g = shared.tile([P, PAGES * DV], U32, name="v_g", align_bytes=64, offset=0)
         nc.vector.tensor_copy(v_g[:], v_pool[:].indirect(voffs_t[:]))
-        vsc_g = sb.tile([P, PAGES * DV], U8, name="vsc_g", align_bytes=64)
+        vsc_g = shared.tile([P, PAGES * DV], U8, name="vsc_g", align_bytes=64, offset=4 * PAGE)
         nc.vector.tensor_copy(vsc_g[:], vsc_pool[:].indirect(voffs_t[:]))
 
         vs_col = []
@@ -141,9 +144,9 @@ def tile_attend_pkv4q_silu_gate_kernel(
         for width in WARM:
             nc.tensor.matmul_mx(
                 out=warm[:, 0:width],
-                lhsT=q_codes[0][:, 0:P].bitcast(FP8X4),
+                lhsT=k_g[0][:].bitcast(U16)[:, 0:P].bitcast(FP4X4),
                 lhsT_scale=ks_first[:, 0:P],
-                rhs=v_pool[:, 0:width].bitcast(FP8X4),
+                rhs=q_codes[:, 0:width].bitcast(FP8X4),
                 rhs_scale=ks_first[:, 0:width],
                 start=True,
                 stop=True,
@@ -162,7 +165,7 @@ def tile_attend_pkv4q_silu_gate_kernel(
                             out=scores[:, r, :],
                             lhsT=k_codes[u][:, k0 : k0 + P].bitcast(FP4X4),
                             lhsT_scale=(ks_second if o else ks_first)[:, s0 : s0 + P],
-                            rhs=q_codes[o][:, h * P : (h + 1) * P].bitcast(FP8X4),
+                            rhs=q_codes[:, q0 : q0 + P].bitcast(FP8X4),
                             rhs_scale=q_plane[:, q0 : q0 + P],
                             start=(o == 1),
                             stop=(o == 0),

@@ -1,7 +1,6 @@
 from contextlib import ExitStack
 
 import concourse.mybir as mybir
-from concourse.masks import make_identity
 
 F32 = mybir.dt.float32
 BF16 = mybir.dt.bfloat16
@@ -29,8 +28,7 @@ QUAD = 32
 SECOND = 16
 VS_ROW = P - 1
 WARM = (512, 512, 128)
-K_PIECE = 512
-K_SPLIT = 2 * K_PIECE
+KS_ROW = 96
 
 FLOPS = 2 * NQ * N * (PASSES * PAGE + DV)
 
@@ -50,47 +48,32 @@ def tile_attend_pkv4q_silu_gate_kernel(
         ks_pool = sb.tile([P, T], U8, name="ks_pool", align_bytes=64)
         vs_pool = sb.tile([P, T], F32, name="vs_pool", align_bytes=64)
         q_plane = sb.tile([P, PASSES * NQ], U8, name="q_plane", align_bytes=64)
-        ks_second = sb.tile([P, N], U8, name="ks_second", align_bytes=64)
+        ks_planes = sb.tile([P, PASSES * N], U8, name="ks_planes", align_bytes=64)
         vsc_pool = sb.tile([P, POOL_PAGES * DV], U8, name="vsc_pool", align_bytes=64)
-        ident = sb.tile([P, P], F32, name="ident")
         og_t = sb.tile([P, Q_TILES, DV], F32, name="og_t")
         q_codes = sb.tile([P, PASSES * NQ], U32, name="q_codes", align_bytes=64)
-        v_pool = sb.tile([P, POOL_PAGES * DV], U32, name="v_pool", align_bytes=64)
 
-        make_identity(nc, ident[:])
-        nc.vector.memset(ks_pool[:].bitcast(I32), 0)
         nc.vector.memset(vsc_pool[:].bitcast(I32), 0)
+        nc.vector.memset(ks_pool[0:KS_ROW, :].bitcast(I32), 0)
         nc.vector.memset(q_plane[:].bitcast(I32), 0)
+        nc.vector.memset(ks_planes[:].bitcast(I32), 0)
         nc.vector.memset(vs_pool[0:VS_ROW, :], 0.0)
-        nc.vector.memset(ks_second[:].bitcast(I32), 0)
 
-        k_src = k_words[0].rearrange("p t b -> p (t b)").bitcast(I32)
         nc.sync.dma_start(offs_t[:], offs)
-        nc.sync.dma_start(out=vs_pool[VS_ROW:P, :], in_=vs[0:1, :])
+        nc.sync.dma_start(out=ks_pool[KS_ROW:P, :].bitcast(I32), in_=k_scales.rearrange("o f t -> (o f) t").bitcast(I32))
+        nc.scalar.dma_start(out=vs_pool[VS_ROW:P, :], in_=vs[0:1, :])
         nc.sync.dma_start(voffs_t[:], voffs)
         nc.sync.dma_start(out=og_t[:], in_=og[0].rearrange("(h p) e -> p h e", p=P))
-        for o in range(PASSES):
-            nc.sync.dma_start(
-                out=q_codes[:, o * NQ : (o + 1) * NQ].bitcast(I32),
-                in_=q_words[0, o].rearrange("p q b -> p (q b)").bitcast(I32),
-            )
-        for c in range(0, K_SPLIT, K_PIECE):
-            nc.sync.dma_start(out=k_pool[:, c : c + K_PIECE].bitcast(I32), in_=k_src[:, c : c + K_PIECE])
+        nc.sync.dma_start(out=k_pool[:].bitcast(I32), in_=k_words[0].rearrange("p t b -> p (t b)").bitcast(I32))
+        nc.sync.dma_start(
+            out=q_codes[:].bitcast(I32).rearrange("p (o q) -> p o q", o=PASSES),
+            in_=q_words[0].rearrange("o p q b -> p o (q b)").bitcast(I32),
+        )
         for r in range(PACK):
-            nc.sync.dma_start(
-                out=ks_pool[r:P:SECOND, :].bitcast(I32),
-                in_=k_scales[:, r::PACK, :].rearrange("o g t -> g o t").bitcast(I32),
-            )
-        nc.sync.dma_start(out=k_pool[:, K_SPLIT:T].bitcast(I32), in_=k_src[:, K_SPLIT:T])
-        for r in range(PACK):
-            nc.sync.dma_start(
+            nc.scalar.dma_start(
                 out=q_plane[r:P:QUAD, :].bitcast(I32).rearrange("g (o q) -> g o q", o=PASSES),
                 in_=q_scales[0][:, r::PACK, :].rearrange("o g q -> g o q").bitcast(I32),
             )
-        nc.sync.dma_start(
-            out=v_pool[:].bitcast(I32).rearrange("p (u e) -> p u e", u=POOL_PAGES),
-            in_=v_words.rearrange("u p e b -> p u (e b)").bitcast(I32),
-        )
         for r in range(PACK):
             nc.gpsimd.dma_start(
                 out=vsc_pool[r:P:QUAD, :].bitcast(I32).rearrange("g (u e) -> g u e", u=POOL_PAGES),
@@ -98,10 +81,8 @@ def tile_attend_pkv4q_silu_gate_kernel(
             )
 
         page_offs = [offs_t[:, u * PAGE // 16 : (u + 1) * PAGE // 16] for u in range(PAGES)]
-        vs_g = sb.tile([P, N], F32, name="vs_g")
-        nc.vector.tensor_copy(vs_g[:], vs_pool[:].indirect(offs_t[:]))
 
-        ks_g = [sb.tile([P, PAGE], U8, name="ks_g%d" % u, align_bytes=64) for u in range(PAGES)]
+        ks_g = [shared.tile([P, PAGE], U8, name="ks_g%d" % u, align_bytes=64, offset=8 * PAGE + PAGE * u) for u in range(PAGES)]
         for u in range(PAGES):
             nc.vector.tensor_copy(ks_g[u][:], ks_pool[:].indirect(page_offs[u]))
         ks_first = sb.tile([P, N], U8, name="ks_first", align_bytes=64)
@@ -110,8 +91,31 @@ def tile_attend_pkv4q_silu_gate_kernel(
                 ks_first[:, u * PAGE : (u + 1) * PAGE].rearrange("p (r s) -> p r s", r=PACK),
                 ks_g[u][:].rearrange("p (s r) -> p r s", r=PACK),
             )
-        nc.scalar.dma_start(out=ks_second[0 : P - SECOND, :].bitcast(I32), in_=ks_first[SECOND:P, :].bitcast(I32))
+        for g in range(PACK):
+            for o in range(PASSES):
+                row = KS_ROW + SECOND * o + PACK * g
+                (nc.scalar if o else nc.sync).dma_start(
+                    out=ks_planes[QUAD * g : QUAD * g + PACK, o * N : (o + 1) * N].bitcast(I32),
+                    in_=ks_first[row : row + PACK, :].bitcast(I32),
+                )
 
+        v_pool = shared.tile([P, POOL_PAGES * DV], U32, name="v_pool", align_bytes=64, offset=8 * PAGE)
+        nc.sync.dma_start(
+            out=v_pool[:].bitcast(I32).rearrange("p (u e) -> p u e", u=POOL_PAGES),
+            in_=v_words.rearrange("u p e b -> p u (e b)").bitcast(I32),
+        )
+
+        vs_col = []
+
+        def gather_vs(gathered):
+            u = len(vs_col)
+            nc.vector.tensor_copy(gathered[:], vs_pool[:].indirect(page_offs[u]))
+            col = sb.tile([P, PACK], F32, name="vs_col%d" % u)
+            nc.sync.dma_start(out=col[:], in_=gathered[VS_ROW:P, :].rearrange("o (p r) -> o p r", r=PACK))
+            vs_col.append(col)
+
+        vs_g0 = sb.tile([P, PAGE], F32, name="vs_g0")
+        gather_vs(vs_g0)
         k_g = [shared.tile([P, PAGE], U32, name="k_g%d" % u, align_bytes=64, offset=4 * PAGE * u) for u in range(PAGES)]
         k_codes = [sb.tile([P, PASSES * PAGE], U16, name="k_codes%d" % u, align_bytes=64) for u in range(PAGES)]
         for u in range(PAGES):
@@ -121,19 +125,12 @@ def tile_attend_pkv4q_silu_gate_kernel(
                 k_codes[u][:].rearrange("p (o r s) -> p o s r", o=PASSES, r=PACK),
                 k_g[u][:].bitcast(U16).rearrange("p (s r o) -> p o s r", o=PASSES, r=PACK),
             )
-        v_g = shared.tile([P, PAGES * DV], U32, name="v_g", align_bytes=64, offset=0)
+        vs_g1 = shared.tile([P, PAGE], F32, name="vs_g1", align_bytes=64, offset=0)
+        gather_vs(vs_g1)
+        v_g = shared.tile([P, PAGES * DV], U32, name="v_g", align_bytes=64, offset=4 * PAGE)
         nc.vector.tensor_copy(v_g[:], v_pool[:].indirect(voffs_t[:]))
-        vsc_g = shared.tile([P, PAGES * DV], U8, name="vsc_g", align_bytes=64, offset=4 * PAGE)
+        vsc_g = shared.tile([P, PAGES * DV], U8, name="vsc_g", align_bytes=64, offset=4 * PAGE + 4 * PAGES * DV)
         nc.vector.tensor_copy(vsc_g[:], vsc_pool[:].indirect(voffs_t[:]))
-
-        vs_col = []
-        for u in range(PAGES):
-            turned = ps.tile([P, PACK, P], F32, name="turned%d" % u)
-            for r in range(PACK):
-                nc.tensor.transpose(turned[:, r, :], vs_g[:, u * PAGE + r : (u + 1) * PAGE : PACK], ident[:])
-            col = sb.tile([P, PACK], F32, name="vs_col%d" % u)
-            nc.scalar.copy(col[:], turned[:, :, VS_ROW])
-            vs_col.append(col)
 
         half = sb.tile([P, Q_TILES, DV], F32, name="half")
         gate = sb.tile([P, Q_TILES, DV], F32, name="gate")
@@ -145,9 +142,9 @@ def tile_attend_pkv4q_silu_gate_kernel(
             nc.tensor.matmul_mx(
                 out=warm[:, 0:width],
                 lhsT=k_g[0][:].bitcast(U16)[:, 0:P].bitcast(FP4X4),
-                lhsT_scale=ks_first[:, 0:P],
+                lhsT_scale=q_plane[:, 0:P],
                 rhs=q_codes[:, 0:width].bitcast(FP8X4),
-                rhs_scale=ks_first[:, 0:width],
+                rhs_scale=q_plane[:, 0:width],
                 start=True,
                 stop=True,
             )
@@ -164,7 +161,7 @@ def tile_attend_pkv4q_silu_gate_kernel(
                         nc.tensor.matmul_mx(
                             out=scores[:, r, :],
                             lhsT=k_codes[u][:, k0 : k0 + P].bitcast(FP4X4),
-                            lhsT_scale=(ks_second if o else ks_first)[:, s0 : s0 + P],
+                            lhsT_scale=ks_planes[:, o * N + s0 : o * N + s0 + P],
                             rhs=q_codes[:, q0 : q0 + P].bitcast(FP8X4),
                             rhs_scale=q_plane[:, q0 : q0 + P],
                             start=(o == 1),

@@ -29,6 +29,7 @@ SECOND = 16
 VS_ROW = P - 1
 WARM = (512, 512, 128)
 KS_ROW = 96
+ODD = T // 8 + 1
 
 FLOPS = 2 * NQ * N * (PASSES * PAGE + DV)
 
@@ -47,42 +48,39 @@ def tile_attend_pkv4q_silu_gate_kernel(
         k_pool = sb.tile([P, T], U32, name="k_pool", align_bytes=64)
         ks_pool = sb.tile([P, T], U8, name="ks_pool", align_bytes=64)
         vs_pool = sb.tile([P, T], F32, name="vs_pool", align_bytes=64)
-        q_plane = sb.tile([P, PASSES * NQ], U8, name="q_plane", align_bytes=64)
-        ks_planes = sb.tile([P, PASSES * N], U8, name="ks_planes", align_bytes=64)
+        q_plane = sb.tile([P, PASSES * NQ + 4], U8, name="q_plane", align_bytes=64)
+        ks_planes = sb.tile([P, PASSES * N + 4], U8, name="ks_planes", align_bytes=64)
         vsc_pool = sb.tile([P, POOL_PAGES * DV], U8, name="vsc_pool", align_bytes=64)
-        og_t = sb.tile([P, Q_TILES, DV], F32, name="og_t")
         q_codes = sb.tile([P, PASSES * NQ], U32, name="q_codes", align_bytes=64)
 
-        nc.vector.memset(vsc_pool[:].bitcast(I32), 0)
-        nc.vector.memset(ks_pool[0:KS_ROW, :].bitcast(I32), 0)
+        nc.gpsimd.memset(vs_pool[0:VS_ROW, :], 0.0)
+        nc.gpsimd.memset(vsc_pool[:].bitcast(I32), 0)
+        one = sb.tile([P, 7], F32, name="one")
+        nc.vector.memset(one[:], 1.0)
         nc.vector.memset(q_plane[:].bitcast(I32), 0)
+        nc.vector.memset(ks_pool[0:KS_ROW, :].bitcast(I32)[:, 0:ODD], 0)
+        nc.vector.memset(ks_pool[0:KS_ROW, :].bitcast(I32)[:, ODD:], 0)
         nc.vector.memset(ks_planes[:].bitcast(I32), 0)
-        nc.vector.memset(vs_pool[0:VS_ROW, :], 0.0)
 
         nc.sync.dma_start(offs_t[:], offs)
         nc.sync.dma_start(out=ks_pool[KS_ROW:P, :].bitcast(I32), in_=k_scales.rearrange("o f t -> (o f) t").bitcast(I32))
         nc.scalar.dma_start(out=vs_pool[VS_ROW:P, :], in_=vs[0:1, :])
-        nc.sync.dma_start(voffs_t[:], voffs)
-        nc.sync.dma_start(out=og_t[:], in_=og[0].rearrange("(h p) e -> p h e", p=P))
+        table = sb.tile([P, 7], F32, name="table")
+        nc.scalar.activation(out=table[:], in_=one[:], func=ACT.Silu)
         nc.sync.dma_start(out=k_pool[:].bitcast(I32), in_=k_words[0].rearrange("p t b -> p (t b)").bitcast(I32))
+        nc.sync.dma_start(voffs_t[:], voffs)
         nc.sync.dma_start(
             out=q_codes[:].bitcast(I32).rearrange("p (o q) -> p o q", o=PASSES),
             in_=q_words[0].rearrange("o p q b -> p o (q b)").bitcast(I32),
         )
         for r in range(PACK):
             nc.scalar.dma_start(
-                out=q_plane[r:P:QUAD, :].bitcast(I32).rearrange("g (o q) -> g o q", o=PASSES),
+                out=q_plane[r:P:QUAD, 0 : PASSES * NQ].bitcast(I32).rearrange("g (o q) -> g o q", o=PASSES),
                 in_=q_scales[0][:, r::PACK, :].rearrange("o g q -> g o q").bitcast(I32),
             )
-        for r in range(PACK):
-            nc.gpsimd.dma_start(
-                out=vsc_pool[r:P:QUAD, :].bitcast(I32).rearrange("g (u e) -> g u e", u=POOL_PAGES),
-                in_=v_scales[:, r::PACK, :].rearrange("u g e -> g u e").bitcast(I32),
-            )
-
         page_offs = [offs_t[:, u * PAGE // 16 : (u + 1) * PAGE // 16] for u in range(PAGES)]
 
-        ks_g = [shared.tile([P, PAGE], U8, name="ks_g%d" % u, align_bytes=64, offset=8 * PAGE + PAGE * u) for u in range(PAGES)]
+        ks_g = [shared.tile([P, PAGE], U8, name="ks_g%d" % u, align_bytes=64, offset=9 * PAGE + PAGE * u) for u in range(PAGES)]
         for u in range(PAGES):
             nc.vector.tensor_copy(ks_g[u][:], ks_pool[:].indirect(page_offs[u]))
         ks_first = sb.tile([P, N], U8, name="ks_first", align_bytes=64)
@@ -99,7 +97,14 @@ def tile_attend_pkv4q_silu_gate_kernel(
                     in_=ks_first[row : row + PACK, :].bitcast(I32),
                 )
 
-        v_pool = shared.tile([P, POOL_PAGES * DV], U32, name="v_pool", align_bytes=64, offset=8 * PAGE)
+        for r in range(PACK):
+            nc.scalar.dma_start(
+                out=vsc_pool[r:P:QUAD, 0 : POOL_PAGES * DV].bitcast(I32).rearrange("g (u e) -> g u e", u=POOL_PAGES),
+                in_=v_scales[:, r::PACK, :].rearrange("u g e -> g u e").bitcast(I32),
+            )
+        og_t = shared.tile([P, Q_TILES, DV], F32, name="og_t", align_bytes=64, offset=8 * PAGE)
+        nc.sync.dma_start(out=og_t[:], in_=og[0].rearrange("(h p) e -> p h e", p=P))
+        v_pool = shared.tile([P, POOL_PAGES * DV], U32, name="v_pool", align_bytes=64, offset=10 * PAGE)
         nc.sync.dma_start(
             out=v_pool[:].bitcast(I32).rearrange("p (u e) -> p u e", u=POOL_PAGES),
             in_=v_words.rearrange("u p e b -> p u (e b)").bitcast(I32),

@@ -25,11 +25,14 @@ PAGES = N // PAGE
 POOL_PAGES = T // PAGE
 Q_TILES = NQ // P
 QUAD = 32
-SECOND = 16
+GROUP_ROWS = PASSES * 16
 VS_ROW = P - 1
-WARM = (512, 512, 128)
-KS_ROW = 96
-ODD = T // 8 + 1
+HALF = PAGE // 2
+REGION = PAGES * DV + N + NQ
+K_COL = (PAGES * DV, REGION + PAGES * DV)
+Q_COL = (K_COL[0] + N, K_COL[1] + N)
+PLANES = PASSES * REGION
+VS_SPLIT = 512
 
 FLOPS = 2 * NQ * N * (PASSES * PAGE + DV)
 
@@ -48,131 +51,124 @@ def tile_attend_pkv4q_silu_gate_kernel(
         k_pool = sb.tile([P, T], U32, name="k_pool", align_bytes=64)
         ks_pool = sb.tile([P, T], U8, name="ks_pool", align_bytes=64)
         vs_pool = sb.tile([P, T], F32, name="vs_pool", align_bytes=64)
-        q_plane = sb.tile([P, PASSES * NQ + 4], U8, name="q_plane", align_bytes=64)
-        ks_planes = sb.tile([P, PASSES * N + 4], U8, name="ks_planes", align_bytes=64)
+        planes = sb.tile([P, PLANES], U8, name="planes", align_bytes=64)
         vsc_pool = sb.tile([P, POOL_PAGES * DV], U8, name="vsc_pool", align_bytes=64)
         q_codes = sb.tile([P, PASSES * NQ], U32, name="q_codes", align_bytes=64)
 
-        nc.gpsimd.memset(vs_pool[0:VS_ROW, :], 0.0)
-        nc.gpsimd.memset(vsc_pool[:].bitcast(I32), 0)
+        def clear_odd(words, first):
+            nc.vector.memset(words[:, 0:first], 0)
+            nc.vector.memset(words[:, first:], 0)
+
+        for first, last in ((0, 16), (QUAD, 2 * QUAD), (2 * QUAD, P)):
+            nc.gpsimd.memset(vsc_pool[first:last, :].bitcast(I32), 0)
+        nc.gpsimd.memset(ks_pool[2 * QUAD : P, :].bitcast(I32), 0)
+        nc.gpsimd.memset(vs_pool[0:VS_ROW, VS_SPLIT:], 0.0)
         one = sb.tile([P, 7], F32, name="one")
         nc.vector.memset(one[:], 1.0)
-        nc.vector.memset(q_plane[:].bitcast(I32), 0)
-        nc.vector.memset(ks_pool[0:KS_ROW, :].bitcast(I32)[:, 0:ODD], 0)
-        nc.vector.memset(ks_pool[0:KS_ROW, :].bitcast(I32)[:, ODD:], 0)
-        nc.vector.memset(ks_planes[:].bitcast(I32), 0)
+        clear_odd(ks_pool[QUAD : 2 * QUAD, :].bitcast(I32), T // 8 + 1)
+        for first, last in ((QUAD, 2 * QUAD), (2 * QUAD, P)):
+            nc.vector.memset(planes[first:last, Q_COL[0] : REGION + 4].bitcast(I32), 0)
+        clear_odd(planes[:, REGION:].bitcast(I32), REGION // 8 + 1)
+        clear_odd(vs_pool[0:VS_ROW, 0:VS_SPLIT], VS_SPLIT // 2 + 1)
 
         nc.sync.dma_start(offs_t[:], offs)
-        nc.sync.dma_start(out=ks_pool[KS_ROW:P, :].bitcast(I32), in_=k_scales.rearrange("o f t -> (o f) t").bitcast(I32))
+        nc.sync.dma_start(out=ks_pool[0:GROUP_ROWS, :].bitcast(I32), in_=k_scales.rearrange("o f t -> (o f) t").bitcast(I32))
+        nc.sync.dma_start(voffs_t[:], voffs)
+        nc.scalar.dma_start(
+            out=vsc_pool[16:GROUP_ROWS, :].bitcast(I32).rearrange("f (u e) -> f u e", u=POOL_PAGES),
+            in_=v_scales.rearrange("u f e -> f u e").bitcast(I32),
+        )
+        nc.scalar.dma_start(
+            out=planes[0:GROUP_ROWS, Q_COL[0] : Q_COL[0] + NQ].bitcast(I32),
+            in_=q_scales[0].rearrange("o f q -> (o f) q").bitcast(I32),
+        )
         nc.scalar.dma_start(out=vs_pool[VS_ROW:P, :], in_=vs[0:1, :])
         table = sb.tile([P, 7], F32, name="table")
         nc.scalar.activation(out=table[:], in_=one[:], func=ACT.Silu)
         nc.sync.dma_start(out=k_pool[:].bitcast(I32), in_=k_words[0].rearrange("p t b -> p (t b)").bitcast(I32))
-        nc.sync.dma_start(voffs_t[:], voffs)
         nc.sync.dma_start(
             out=q_codes[:].bitcast(I32).rearrange("p (o q) -> p o q", o=PASSES),
             in_=q_words[0].rearrange("o p q b -> p o (q b)").bitcast(I32),
         )
-        for r in range(PACK):
-            nc.scalar.dma_start(
-                out=q_plane[r:P:QUAD, 0 : PASSES * NQ].bitcast(I32).rearrange("g (o q) -> g o q", o=PASSES),
-                in_=q_scales[0][:, r::PACK, :].rearrange("o g q -> g o q").bitcast(I32),
-            )
         page_offs = [offs_t[:, u * PAGE // 16 : (u + 1) * PAGE // 16] for u in range(PAGES)]
 
-        ks_g = [shared.tile([P, PAGE], U8, name="ks_g%d" % u, align_bytes=64, offset=9 * PAGE + PAGE * u) for u in range(PAGES)]
+        ks_g = [sb.tile([P, PAGE], U8, name="ks_g%d" % u, align_bytes=64) for u in range(PAGES)]
         for u in range(PAGES):
             nc.vector.tensor_copy(ks_g[u][:], ks_pool[:].indirect(page_offs[u]))
-        ks_first = sb.tile([P, N], U8, name="ks_first", align_bytes=64)
+        vsc_g = sb.tile([P, PAGES * DV], U8, name="vsc_g", align_bytes=64)
+        nc.vector.tensor_copy(vsc_g[:], vsc_pool[:].indirect(voffs_t[:]))
         for u in range(PAGES):
             nc.vector.tensor_copy(
-                ks_first[:, u * PAGE : (u + 1) * PAGE].rearrange("p (r s) -> p r s", r=PACK),
+                planes[:, K_COL[0] + u * PAGE : K_COL[0] + (u + 1) * PAGE].rearrange("p (r s) -> p r s", r=PACK),
                 ks_g[u][:].rearrange("p (s r) -> p r s", r=PACK),
             )
-        for g in range(PACK):
-            for o in range(PASSES):
-                row = KS_ROW + SECOND * o + PACK * g
-                (nc.scalar if o else nc.sync).dma_start(
-                    out=ks_planes[QUAD * g : QUAD * g + PACK, o * N : (o + 1) * N].bitcast(I32),
-                    in_=ks_first[row : row + PACK, :].bitcast(I32),
-                )
+        nc.vector.tensor_copy(planes[:, 0 : PAGES * DV].bitcast(I32), vsc_g[:].bitcast(I32))
+        moves = [(o, g) for o in (1, 0) for g in range(PACK) if (o, g) != (0, 0)]
 
-        for r in range(PACK):
-            nc.scalar.dma_start(
-                out=vsc_pool[r:P:QUAD, 0 : POOL_PAGES * DV].bitcast(I32).rearrange("g (u e) -> g u e", u=POOL_PAGES),
-                in_=v_scales[:, r::PACK, :].rearrange("u g e -> g u e").bitcast(I32),
+        def move(queue, o, g):
+            row = 16 * o + PACK * g
+            src = 0 if o else K_COL[0]
+            dst = REGION if o else K_COL[0]
+            width = REGION - src
+            queue.dma_start(
+                out=planes[QUAD * g : QUAD * g + PACK, dst : dst + width].bitcast(I32),
+                in_=planes[row : row + PACK, src : src + width].bitcast(I32),
             )
-        og_t = shared.tile([P, Q_TILES, DV], F32, name="og_t", align_bytes=64, offset=8 * PAGE)
-        nc.sync.dma_start(out=og_t[:], in_=og[0].rearrange("(h p) e -> p h e", p=P))
-        v_pool = shared.tile([P, POOL_PAGES * DV], U32, name="v_pool", align_bytes=64, offset=10 * PAGE)
+
+        for o, g in moves:
+            move(nc.sync if o else nc.scalar, o, g)
+
+        vs_col = []
+        for u in range(PAGES):
+            vs_g = sb.tile([P, PAGE], F32, name="vs_g%d" % u)
+            nc.scalar.activation(out=vs_g[:], in_=vs_pool[:].indirect(page_offs[u]), func=ACT.Copy)
+            col = sb.tile([P, PACK], F32, name="vs_col%d" % u)
+            nc.scalar.dma_start(out=col[:], in_=vs_g[VS_ROW:P, :].rearrange("o (p r) -> o p r", r=PACK))
+            vs_col.append(col)
+
+        k_codes = [sb.tile([P, PASSES * PAGE], U16, name="k_codes%d" % u, align_bytes=64) for u in range(PAGES)]
+        for u in range(PAGES):
+            k_g = []
+            for a in range(2):
+                part = shared.tile([P, HALF], U32, name="k_g%d%d" % (u, a), align_bytes=64, offset=(7 + 5 * a + (1 - 2 * a) * u) * PAGE)
+                first = (u * PAGE + a * HALF) // 16
+                nc.vector.tensor_copy(part[:], k_pool[:].indirect(offs_t[:, first : first + HALF // 16]))
+                k_g.append(part)
+            for a in range(2):
+                nc.vector.tensor_copy(
+                    k_codes[u][:].rearrange("p (o r s) -> p o s r", o=PASSES, r=PACK)[:, :, a * HALF // PACK : (a + 1) * HALF // PACK, :],
+                    k_g[a][:].bitcast(U16).rearrange("p (s r o) -> p o s r", o=PASSES, r=PACK),
+                )
+        v_pool = sb.tile([P, POOL_PAGES * DV], U32, name="v_pool", align_bytes=64)
         nc.sync.dma_start(
             out=v_pool[:].bitcast(I32).rearrange("p (u e) -> p u e", u=POOL_PAGES),
             in_=v_words.rearrange("u p e b -> p u (e b)").bitcast(I32),
         )
-
-        vs_col = []
-
-        def gather_vs(gathered):
-            u = len(vs_col)
-            nc.vector.tensor_copy(gathered[:], vs_pool[:].indirect(page_offs[u]))
-            col = sb.tile([P, PACK], F32, name="vs_col%d" % u)
-            nc.sync.dma_start(out=col[:], in_=gathered[VS_ROW:P, :].rearrange("o (p r) -> o p r", r=PACK))
-            vs_col.append(col)
-
-        vs_g0 = sb.tile([P, PAGE], F32, name="vs_g0")
-        gather_vs(vs_g0)
-        k_g = [shared.tile([P, PAGE], U32, name="k_g%d" % u, align_bytes=64, offset=4 * PAGE * u) for u in range(PAGES)]
-        k_codes = [sb.tile([P, PASSES * PAGE], U16, name="k_codes%d" % u, align_bytes=64) for u in range(PAGES)]
-        for u in range(PAGES):
-            nc.vector.tensor_copy(k_g[u][:], k_pool[:].indirect(page_offs[u]))
-        for u in range(PAGES):
-            nc.vector.tensor_copy(
-                k_codes[u][:].rearrange("p (o r s) -> p o s r", o=PASSES, r=PACK),
-                k_g[u][:].bitcast(U16).rearrange("p (s r o) -> p o s r", o=PASSES, r=PACK),
-            )
-        vs_g1 = shared.tile([P, PAGE], F32, name="vs_g1", align_bytes=64, offset=0)
-        gather_vs(vs_g1)
-        v_g = shared.tile([P, PAGES * DV], U32, name="v_g", align_bytes=64, offset=4 * PAGE)
+        v_g = shared.tile([P, PAGES * DV], U32, name="v_g", align_bytes=64, offset=8 * PAGE)
         nc.vector.tensor_copy(v_g[:], v_pool[:].indirect(voffs_t[:]))
-        vsc_g = shared.tile([P, PAGES * DV], U8, name="vsc_g", align_bytes=64, offset=4 * PAGE + 4 * PAGES * DV)
-        nc.vector.tensor_copy(vsc_g[:], vsc_pool[:].indirect(voffs_t[:]))
+        og_t = sb.tile([P, Q_TILES, DV], F32, name="og_t")
+        nc.sync.dma_start(out=og_t[:], in_=og[0].rearrange("(h p) e -> p h e", p=P))
 
-        half = sb.tile([P, Q_TILES, DV], F32, name="half")
-        gate = sb.tile([P, Q_TILES, DV], F32, name="gate")
-        nc.scalar.activation(out=half[:], in_=og_t[:], func=ACT.Tanh, scale=0.5)
-        nc.scalar.activation(out=gate[:], in_=half[:], func=ACT.Copy, scale=1.0 / 32.0, bias=1.0 / 32.0)
-
-        warm = ps.tile([P, PASSES * NQ], F32, name="warm", tag="y0")
-        for width in WARM:
-            nc.tensor.matmul_mx(
-                out=warm[:, 0:width],
-                lhsT=k_g[0][:].bitcast(U16)[:, 0:P].bitcast(FP4X4),
-                lhsT_scale=q_plane[:, 0:P],
-                rhs=q_codes[:, 0:width].bitcast(FP8X4),
-                rhs_scale=q_plane[:, 0:width],
-                start=True,
-                stop=True,
-            )
         y = [ps.tile([P, DV], F32, name="y%d" % h, tag="y%d" % h) for h in range(Q_TILES)]
         silu = {}
         for u in range(PAGES):
             for h in range(Q_TILES):
-                scores = ps.tile([P, PACK, P], F32, name="scores%d%d" % (u, h))
+                scores = ps.tile([P, PACK, P], F32, name="scores%d%d" % (u, h), tag="scores%d%d" % (u, h))
                 for r in range(PACK):
                     for o in (1, 0):
                         k0 = o * PAGE + r * P
-                        s0 = u * PAGE + r * P
+                        s0 = K_COL[o] + u * PAGE + r * P
                         q0 = o * NQ + h * P
                         nc.tensor.matmul_mx(
                             out=scores[:, r, :],
                             lhsT=k_codes[u][:, k0 : k0 + P].bitcast(FP4X4),
-                            lhsT_scale=ks_planes[:, o * N + s0 : o * N + s0 + P],
+                            lhsT_scale=planes[:, s0 : s0 + P],
                             rhs=q_codes[:, q0 : q0 + P].bitcast(FP8X4),
-                            rhs_scale=q_plane[:, q0 : q0 + P],
+                            rhs_scale=planes[:, Q_COL[o] + h * P : Q_COL[o] + (h + 1) * P],
                             start=(o == 1),
                             stop=(o == 0),
                         )
-                act = sb.tile([P, P, PACK], F32, name="silu%d%d" % (u, h))
+                act = shared.tile([P, P, PACK], F32, name="silu%d%d" % (u, h), align_bytes=64, offset=(24 + 8 * u + 4 * h) * PAGE)
                 nc.scalar.activation(out=act[:], in_=scores[:].rearrange("p r q -> p q r"), func=ACT.Silu)
                 silu[(u, h)] = act
 
@@ -182,6 +178,11 @@ def tile_attend_pkv4q_silu_gate_kernel(
                 w = sb.tile([P, P, PACK], BF16, name="w%d%d" % (u, h), align_bytes=64)
                 nc.vector.tensor_tensor(w[:], silu[(u, h)][:], vs_col[u][:].unsqueeze(1).to_broadcast([P, P, PACK]), ALU.mult)
                 weights.append(w)
+            if u == 0:
+                half = shared.tile([P, Q_TILES, DV], F32, name="half", align_bytes=64, offset=24 * PAGE)
+                gate = sb.tile([P, Q_TILES, DV], F32, name="gate")
+                nc.scalar.activation(out=half[:], in_=og_t[:], func=ACT.Tanh, scale=0.5)
+                nc.scalar.activation(out=gate[:], in_=half[:], func=ACT.Copy, scale=1.0 / 32.0, bias=1.0 / 32.0)
             for h in range(Q_TILES):
                 w_codes = sb.tile([P, P], U32, name="w_codes%d%d" % (u, h), align_bytes=64)
                 w_plane = sb.tile([P, P], U8, name="w_plane%d%d" % (u, h), align_bytes=64)
@@ -195,7 +196,7 @@ def tile_attend_pkv4q_silu_gate_kernel(
                     lhsT=w_codes[:].bitcast(FP8X4),
                     lhsT_scale=w_plane[:],
                     rhs=v_g[:, u * DV : (u + 1) * DV].bitcast(FP8X4),
-                    rhs_scale=vsc_g[:, u * DV : (u + 1) * DV],
+                    rhs_scale=planes[:, REGION + u * DV : REGION + (u + 1) * DV],
                     start=(u == 0),
                     stop=(u == PAGES - 1),
                 )

@@ -32,7 +32,8 @@ REGION = PAGES * DV + N + NQ
 K_COL = (PAGES * DV, REGION + PAGES * DV)
 Q_COL = (K_COL[0] + N, K_COL[1] + N)
 PLANES = PASSES * REGION
-VS_SPLIT = 512
+VS_SPLIT = 2688
+STAGE_ROW = P - GROUP_ROWS
 
 FLOPS = 2 * NQ * N * (PASSES * PAGE + DV)
 
@@ -55,31 +56,24 @@ def tile_attend_pkv4q_silu_gate_kernel(
         vsc_pool = sb.tile([P, POOL_PAGES * DV], U8, name="vsc_pool", align_bytes=64)
         q_codes = sb.tile([P, PASSES * NQ], U32, name="q_codes", align_bytes=64)
 
-        def clear_odd(words, first):
-            nc.vector.memset(words[:, 0:first], 0)
-            nc.vector.memset(words[:, first:], 0)
-
-        for first, last in ((0, 16), (QUAD, 2 * QUAD), (2 * QUAD, P)):
-            nc.gpsimd.memset(vsc_pool[first:last, :].bitcast(I32), 0)
-        nc.gpsimd.memset(ks_pool[2 * QUAD : P, :].bitcast(I32), 0)
-        nc.gpsimd.memset(vs_pool[0:VS_ROW, VS_SPLIT:], 0.0)
+        stage = sb.tile([P, REGION], U8, name="stage", align_bytes=64)
+        nc.gpsimd.memset(vsc_pool[0 : P - 16, :].bitcast(I32), 0)
+        nc.gpsimd.memset(planes[:, K_COL[0] : REGION].bitcast(I32), 0)
         one = sb.tile([P, 7], F32, name="one")
         nc.vector.memset(one[:], 1.0)
-        clear_odd(ks_pool[QUAD : 2 * QUAD, :].bitcast(I32), T // 8 + 1)
-        for first, last in ((QUAD, 2 * QUAD), (2 * QUAD, P)):
-            nc.vector.memset(planes[first:last, Q_COL[0] : REGION + 4].bitcast(I32), 0)
-        clear_odd(planes[:, REGION:].bitcast(I32), REGION // 8 + 1)
-        clear_odd(vs_pool[0:VS_ROW, 0:VS_SPLIT], VS_SPLIT // 2 + 1)
+        nc.vector.memset(ks_pool[0:STAGE_ROW, :].bitcast(I32), 0)
+        nc.vector.memset(planes[:, REGION:].bitcast(I32), 0)
+        nc.vector.memset(vs_pool[0:VS_ROW, 0:VS_SPLIT], 0.0)
 
         nc.sync.dma_start(offs_t[:], offs)
-        nc.sync.dma_start(out=ks_pool[0:GROUP_ROWS, :].bitcast(I32), in_=k_scales.rearrange("o f t -> (o f) t").bitcast(I32))
+        nc.sync.dma_start(out=ks_pool[STAGE_ROW:P, :].bitcast(I32), in_=k_scales.rearrange("o f t -> (o f) t").bitcast(I32))
         nc.sync.dma_start(voffs_t[:], voffs)
         nc.scalar.dma_start(
-            out=vsc_pool[16:GROUP_ROWS, :].bitcast(I32).rearrange("f (u e) -> f u e", u=POOL_PAGES),
+            out=vsc_pool[P - 16 : P, :].bitcast(I32).rearrange("f (u e) -> f u e", u=POOL_PAGES),
             in_=v_scales.rearrange("u f e -> f u e").bitcast(I32),
         )
         nc.scalar.dma_start(
-            out=planes[0:GROUP_ROWS, Q_COL[0] : Q_COL[0] + NQ].bitcast(I32),
+            out=stage[STAGE_ROW:P, Q_COL[0] : Q_COL[0] + NQ].bitcast(I32),
             in_=q_scales[0].rearrange("o f q -> (o f) q").bitcast(I32),
         )
         nc.scalar.dma_start(out=vs_pool[VS_ROW:P, :], in_=vs[0:1, :])
@@ -99,20 +93,21 @@ def tile_attend_pkv4q_silu_gate_kernel(
         nc.vector.tensor_copy(vsc_g[:], vsc_pool[:].indirect(voffs_t[:]))
         for u in range(PAGES):
             nc.vector.tensor_copy(
-                planes[:, K_COL[0] + u * PAGE : K_COL[0] + (u + 1) * PAGE].rearrange("p (r s) -> p r s", r=PACK),
+                stage[:, K_COL[0] + u * PAGE : K_COL[0] + (u + 1) * PAGE].rearrange("p (r s) -> p r s", r=PACK),
                 ks_g[u][:].rearrange("p (s r) -> p r s", r=PACK),
             )
-        nc.vector.tensor_copy(planes[:, 0 : PAGES * DV].bitcast(I32), vsc_g[:].bitcast(I32))
-        moves = [(o, g) for o in (1, 0) for g in range(PACK) if (o, g) != (0, 0)]
+        nc.vector.tensor_copy(stage[:, 0 : PAGES * DV].bitcast(I32), vsc_g[:].bitcast(I32))
+        nc.vector.memset(vs_pool[0:VS_ROW, VS_SPLIT:], 0.0)
+        moves = [(o, g) for o in range(PASSES) for g in range(PACK)]
 
         def move(queue, o, g):
-            row = 16 * o + PACK * g
+            row = STAGE_ROW + 16 * o + PACK * g
             src = 0 if o else K_COL[0]
             dst = REGION if o else K_COL[0]
             width = REGION - src
             queue.dma_start(
                 out=planes[QUAD * g : QUAD * g + PACK, dst : dst + width].bitcast(I32),
-                in_=planes[row : row + PACK, src : src + width].bitcast(I32),
+                in_=stage[row : row + PACK, src : src + width].bitcast(I32),
             )
 
         for o, g in moves:
@@ -154,8 +149,8 @@ def tile_attend_pkv4q_silu_gate_kernel(
         for u in range(PAGES):
             for h in range(Q_TILES):
                 scores = ps.tile([P, PACK, P], F32, name="scores%d%d" % (u, h), tag="scores%d%d" % (u, h))
-                for r in range(PACK):
-                    for o in (1, 0):
+                for o in range(PASSES):
+                    for r in range(PACK):
                         k0 = o * PAGE + r * P
                         s0 = K_COL[o] + u * PAGE + r * P
                         q0 = o * NQ + h * P
@@ -165,8 +160,8 @@ def tile_attend_pkv4q_silu_gate_kernel(
                             lhsT_scale=planes[:, s0 : s0 + P],
                             rhs=q_codes[:, q0 : q0 + P].bitcast(FP8X4),
                             rhs_scale=planes[:, Q_COL[o] + h * P : Q_COL[o] + (h + 1) * P],
-                            start=(o == 1),
-                            stop=(o == 0),
+                            start=(o == 0 and r == 0),
+                            stop=(o == PASSES - 1 and r == PACK - 1),
                         )
                 act = shared.tile([P, P, PACK], F32, name="silu%d%d" % (u, h), align_bytes=64, offset=(24 + 8 * u + 4 * h) * PAGE)
                 nc.scalar.activation(out=act[:], in_=scores[:].rearrange("p r q -> p q r"), func=ACT.Silu)

@@ -32,7 +32,6 @@ REGION = PAGES * DV + N + NQ
 K_COL = (PAGES * DV, REGION + PAGES * DV)
 Q_COL = (K_COL[0] + N, K_COL[1] + N)
 PLANES = PASSES * REGION
-VS_SPLIT = 2688
 STAGE_ROW = P - GROUP_ROWS
 
 FLOPS = 2 * NQ * N * (PASSES * PAGE + DV)
@@ -58,12 +57,13 @@ def tile_attend_pkv4q_silu_gate_kernel(
 
         stage = sb.tile([P, REGION], U8, name="stage", align_bytes=64)
         nc.gpsimd.memset(vsc_pool[0 : P - 16, :].bitcast(I32), 0)
-        nc.gpsimd.memset(planes[:, K_COL[0] : REGION].bitcast(I32), 0)
+        nc.gpsimd.memset(vs_pool[0:VS_ROW, :], 0.0)
         one = sb.tile([P, 7], F32, name="one")
         nc.vector.memset(one[:], 1.0)
-        nc.vector.memset(ks_pool[0:STAGE_ROW, :].bitcast(I32), 0)
-        nc.vector.memset(planes[:, REGION:].bitcast(I32), 0)
-        nc.vector.memset(vs_pool[0:VS_ROW, 0:VS_SPLIT], 0.0)
+        for words in (ks_pool[0:STAGE_ROW, :].bitcast(I32), planes[:, K_COL[0] :].bitcast(I32)):
+            odd = words.shape[1] // 2 + 1
+            nc.vector.memset(words[:, 0:odd], 0)
+            nc.vector.memset(words[:, odd:], 0)
 
         nc.sync.dma_start(offs_t[:], offs)
         nc.sync.dma_start(out=ks_pool[STAGE_ROW:P, :].bitcast(I32), in_=k_scales.rearrange("o f t -> (o f) t").bitcast(I32))
@@ -86,18 +86,17 @@ def tile_attend_pkv4q_silu_gate_kernel(
         )
         page_offs = [offs_t[:, u * PAGE // 16 : (u + 1) * PAGE // 16] for u in range(PAGES)]
 
-        ks_g = [sb.tile([P, PAGE], U8, name="ks_g%d" % u, align_bytes=64) for u in range(PAGES)]
+        ks_g = [shared.tile([P, PAGE], U8, name="ks_g%d" % u, align_bytes=64, offset=u * PAGE) for u in range(PAGES)]
         for u in range(PAGES):
             nc.vector.tensor_copy(ks_g[u][:], ks_pool[:].indirect(page_offs[u]))
-        vsc_g = sb.tile([P, PAGES * DV], U8, name="vsc_g", align_bytes=64)
-        nc.vector.tensor_copy(vsc_g[:], vsc_pool[:].indirect(voffs_t[:]))
         for u in range(PAGES):
             nc.vector.tensor_copy(
                 stage[:, K_COL[0] + u * PAGE : K_COL[0] + (u + 1) * PAGE].rearrange("p (r s) -> p r s", r=PACK),
                 ks_g[u][:].rearrange("p (s r) -> p r s", r=PACK),
             )
+        vsc_g = shared.tile([P, PAGES * DV], U8, name="vsc_g", align_bytes=64, offset=0)
+        nc.vector.tensor_copy(vsc_g[:], vsc_pool[:].indirect(voffs_t[:]))
         nc.vector.tensor_copy(stage[:, 0 : PAGES * DV].bitcast(I32), vsc_g[:].bitcast(I32))
-        nc.vector.memset(vs_pool[0:VS_ROW, VS_SPLIT:], 0.0)
         moves = [(o, g) for o in range(PASSES) for g in range(PACK)]
 
         def move(queue, o, g):
@@ -121,7 +120,7 @@ def tile_attend_pkv4q_silu_gate_kernel(
             nc.scalar.dma_start(out=col[:], in_=vs_g[VS_ROW:P, :].rearrange("o (p r) -> o p r", r=PACK))
             vs_col.append(col)
 
-        k_codes = [sb.tile([P, PASSES * PAGE], U16, name="k_codes%d" % u, align_bytes=64) for u in range(PAGES)]
+        k_codes = [shared.tile([P, PASSES * PAGE], U16, name="k_codes%d" % u, align_bytes=64, offset=(16 + 4 * u) * PAGE) for u in range(PAGES)]
         for u in range(PAGES):
             k_g = []
             for a in range(2):
@@ -129,10 +128,11 @@ def tile_attend_pkv4q_silu_gate_kernel(
                 first = (u * PAGE + a * HALF) // 16
                 nc.vector.tensor_copy(part[:], k_pool[:].indirect(offs_t[:, first : first + HALF // 16]))
                 k_g.append(part)
-            for a in range(2):
+            pieces = [(0, 0, PASSES), (1, 0, 1), (1, 1, PASSES)] if u == 0 else [(0, 0, PASSES), (1, 0, PASSES)]
+            for a, first, last in pieces:
                 nc.vector.tensor_copy(
-                    k_codes[u][:].rearrange("p (o r s) -> p o s r", o=PASSES, r=PACK)[:, :, a * HALF // PACK : (a + 1) * HALF // PACK, :],
-                    k_g[a][:].bitcast(U16).rearrange("p (s r o) -> p o s r", o=PASSES, r=PACK),
+                    k_codes[u][:].rearrange("p (o r s) -> p o s r", o=PASSES, r=PACK)[:, first:last, a * HALF // PACK : (a + 1) * HALF // PACK, :],
+                    k_g[a][:].bitcast(U16).rearrange("p (s r o) -> p o s r", o=PASSES, r=PACK)[:, first:last],
                 )
         v_pool = sb.tile([P, POOL_PAGES * DV], U32, name="v_pool", align_bytes=64)
         nc.sync.dma_start(
@@ -145,27 +145,36 @@ def tile_attend_pkv4q_silu_gate_kernel(
         nc.sync.dma_start(out=og_t[:], in_=og[0].rearrange("(h p) e -> p h e", p=P))
 
         y = [ps.tile([P, DV], F32, name="y%d" % h, tag="y%d" % h) for h in range(Q_TILES)]
+
+        def score_bank(u, h):
+            scores = ps.tile([P, PACK, P], F32, name="scores%d%d" % (u, h))
+            for o in range(PASSES):
+                for r in range(PACK):
+                    k0 = o * PAGE + r * P
+                    s0 = K_COL[o] + u * PAGE + r * P
+                    nc.tensor.matmul_mx(
+                        out=scores[:, r, :],
+                        lhsT=k_codes[u][:, k0 : k0 + P].bitcast(FP4X4),
+                        lhsT_scale=planes[:, s0 : s0 + P],
+                        rhs=q_codes[:, o * NQ + h * P : o * NQ + (h + 1) * P].bitcast(FP8X4),
+                        rhs_scale=planes[:, Q_COL[o] + h * P : Q_COL[o] + (h + 1) * P],
+                        start=(o == 0 and r == 0),
+                        stop=(o == PASSES - 1 and r == PACK - 1),
+                    )
+            return scores
+
         silu = {}
         for u in range(PAGES):
             for h in range(Q_TILES):
-                scores = ps.tile([P, PACK, P], F32, name="scores%d%d" % (u, h), tag="scores%d%d" % (u, h))
-                for o in range(PASSES):
-                    for r in range(PACK):
-                        k0 = o * PAGE + r * P
-                        s0 = K_COL[o] + u * PAGE + r * P
-                        q0 = o * NQ + h * P
-                        nc.tensor.matmul_mx(
-                            out=scores[:, r, :],
-                            lhsT=k_codes[u][:, k0 : k0 + P].bitcast(FP4X4),
-                            lhsT_scale=planes[:, s0 : s0 + P],
-                            rhs=q_codes[:, q0 : q0 + P].bitcast(FP8X4),
-                            rhs_scale=planes[:, Q_COL[o] + h * P : Q_COL[o] + (h + 1) * P],
-                            start=(o == 0 and r == 0),
-                            stop=(o == PASSES - 1 and r == PACK - 1),
-                        )
-                act = shared.tile([P, P, PACK], F32, name="silu%d%d" % (u, h), align_bytes=64, offset=(24 + 8 * u + 4 * h) * PAGE)
+                scores = score_bank(u, h)
+                act = sb.tile([P, P, PACK], F32, name="silu%d%d" % (u, h))
                 nc.scalar.activation(out=act[:], in_=scores[:].rearrange("p r q -> p q r"), func=ACT.Silu)
                 silu[(u, h)] = act
+
+        half = shared.tile([P, Q_TILES, DV], F32, name="half", align_bytes=64, offset=20 * PAGE)
+        gate = sb.tile([P, Q_TILES, DV], F32, name="gate")
+        nc.scalar.activation(out=half[:], in_=og_t[:], func=ACT.Tanh, scale=0.5)
+        nc.scalar.activation(out=gate[:], in_=half[:], func=ACT.Copy, scale=1.0 / 32.0, bias=1.0 / 32.0)
 
         for u in range(PAGES):
             weights = []
@@ -173,11 +182,6 @@ def tile_attend_pkv4q_silu_gate_kernel(
                 w = sb.tile([P, P, PACK], BF16, name="w%d%d" % (u, h), align_bytes=64)
                 nc.vector.tensor_tensor(w[:], silu[(u, h)][:], vs_col[u][:].unsqueeze(1).to_broadcast([P, P, PACK]), ALU.mult)
                 weights.append(w)
-            if u == 0:
-                half = shared.tile([P, Q_TILES, DV], F32, name="half", align_bytes=64, offset=24 * PAGE)
-                gate = sb.tile([P, Q_TILES, DV], F32, name="gate")
-                nc.scalar.activation(out=half[:], in_=og_t[:], func=ACT.Tanh, scale=0.5)
-                nc.scalar.activation(out=gate[:], in_=half[:], func=ACT.Copy, scale=1.0 / 32.0, bias=1.0 / 32.0)
             for h in range(Q_TILES):
                 w_codes = sb.tile([P, P], U32, name="w_codes%d%d" % (u, h), align_bytes=64)
                 w_plane = sb.tile([P, P], U8, name="w_plane%d%d" % (u, h), align_bytes=64)

@@ -27,12 +27,13 @@ Q_TILES = NQ // P
 QUAD = 32
 GROUP_ROWS = PASSES * 16
 VS_ROW = P - 1
+V_ROW = P - 16
 HALF = PAGE // 2
-REGION = PAGES * DV + N + NQ
-K_COL = (PAGES * DV, REGION + PAGES * DV)
+REGION = N + NQ
+KS_SPLIT = 3 * T // 4
+K_COL = (0, REGION)
 Q_COL = (K_COL[0] + N, K_COL[1] + N)
 PLANES = PASSES * REGION
-STAGE_ROW = P - GROUP_ROWS
 
 FLOPS = 2 * NQ * N * (PASSES * PAGE + DV)
 
@@ -55,35 +56,40 @@ def tile_attend_pkv4q_silu_gate_kernel(
         vsc_pool = sb.tile([P, POOL_PAGES * DV], U8, name="vsc_pool", align_bytes=64)
         q_codes = sb.tile([P, PASSES * NQ], U32, name="q_codes", align_bytes=64)
 
-        stage = sb.tile([P, REGION], U8, name="stage", align_bytes=64)
-        nc.gpsimd.memset(vsc_pool[0 : P - 16, :].bitcast(I32), 0)
+        v_plane = sb.tile([P, PAGES * DV], U8, name="v_plane", align_bytes=64)
+        nc.gpsimd.memset(vsc_pool[0:V_ROW, :].bitcast(I32), 0)
+        nc.gpsimd.memset(ks_pool[2 * QUAD : P, KS_SPLIT:].bitcast(I32), 0)
         nc.gpsimd.memset(vs_pool[0:VS_ROW, :], 0.0)
+        nc.gpsimd.memset(v_plane[:].bitcast(I32), 0)
         one = sb.tile([P, 7], F32, name="one")
         nc.vector.memset(one[:], 1.0)
-        for words in (ks_pool[0:STAGE_ROW, :].bitcast(I32), planes[:, K_COL[0] :].bitcast(I32)):
+
+        def clear_odd(words):
             odd = words.shape[1] // 2 + 1
             nc.vector.memset(words[:, 0:odd], 0)
             nc.vector.memset(words[:, odd:], 0)
 
+        clear_odd(ks_pool[QUAD : 2 * QUAD, :].bitcast(I32))
+        clear_odd(ks_pool[2 * QUAD : P, 0:KS_SPLIT].bitcast(I32))
+        for first, last in ((QUAD, 2 * QUAD), (2 * QUAD, P)):
+            nc.vector.memset(planes[first:last, Q_COL[0] : REGION + 4].bitcast(I32), 0)
+        clear_odd(planes[:, REGION:].bitcast(I32))
+
         nc.sync.dma_start(offs_t[:], offs)
-        nc.sync.dma_start(out=ks_pool[STAGE_ROW:P, :].bitcast(I32), in_=k_scales.rearrange("o f t -> (o f) t").bitcast(I32))
+        nc.sync.dma_start(out=ks_pool[0:GROUP_ROWS, :].bitcast(I32), in_=k_scales.rearrange("o f t -> (o f) t").bitcast(I32))
         nc.sync.dma_start(voffs_t[:], voffs)
         nc.scalar.dma_start(
-            out=vsc_pool[P - 16 : P, :].bitcast(I32).rearrange("f (u e) -> f u e", u=POOL_PAGES),
+            out=vsc_pool[V_ROW:P, :].bitcast(I32).rearrange("f (u e) -> f u e", u=POOL_PAGES),
             in_=v_scales.rearrange("u f e -> f u e").bitcast(I32),
         )
         nc.scalar.dma_start(
-            out=stage[STAGE_ROW:P, Q_COL[0] : Q_COL[0] + NQ].bitcast(I32),
+            out=planes[0:GROUP_ROWS, Q_COL[0] : Q_COL[0] + NQ].bitcast(I32),
             in_=q_scales[0].rearrange("o f q -> (o f) q").bitcast(I32),
         )
         nc.scalar.dma_start(out=vs_pool[VS_ROW:P, :], in_=vs[0:1, :])
         table = sb.tile([P, 7], F32, name="table")
         nc.scalar.activation(out=table[:], in_=one[:], func=ACT.Silu)
         nc.sync.dma_start(out=k_pool[:].bitcast(I32), in_=k_words[0].rearrange("p t b -> p (t b)").bitcast(I32))
-        nc.sync.dma_start(
-            out=q_codes[:].bitcast(I32).rearrange("p (o q) -> p o q", o=PASSES),
-            in_=q_words[0].rearrange("o p q b -> p o (q b)").bitcast(I32),
-        )
         page_offs = [offs_t[:, u * PAGE // 16 : (u + 1) * PAGE // 16] for u in range(PAGES)]
 
         ks_g = [shared.tile([P, PAGE], U8, name="ks_g%d" % u, align_bytes=64, offset=u * PAGE) for u in range(PAGES)]
@@ -91,26 +97,26 @@ def tile_attend_pkv4q_silu_gate_kernel(
             nc.vector.tensor_copy(ks_g[u][:], ks_pool[:].indirect(page_offs[u]))
         for u in range(PAGES):
             nc.vector.tensor_copy(
-                stage[:, K_COL[0] + u * PAGE : K_COL[0] + (u + 1) * PAGE].rearrange("p (r s) -> p r s", r=PACK),
+                planes[:, K_COL[0] + u * PAGE : K_COL[0] + (u + 1) * PAGE].rearrange("p (r s) -> p r s", r=PACK),
                 ks_g[u][:].rearrange("p (s r) -> p r s", r=PACK),
             )
         vsc_g = shared.tile([P, PAGES * DV], U8, name="vsc_g", align_bytes=64, offset=0)
         nc.vector.tensor_copy(vsc_g[:], vsc_pool[:].indirect(voffs_t[:]))
-        nc.vector.tensor_copy(stage[:, 0 : PAGES * DV].bitcast(I32), vsc_g[:].bitcast(I32))
-        moves = [(o, g) for o in range(PASSES) for g in range(PACK)]
+        moves = [(o, g) for o in range(PASSES) for g in range(PACK) if (o, g) != (0, 0)]
 
         def move(queue, o, g):
-            row = STAGE_ROW + 16 * o + PACK * g
-            src = 0 if o else K_COL[0]
-            dst = REGION if o else K_COL[0]
-            width = REGION - src
+            row = 16 * o + PACK * g
             queue.dma_start(
-                out=planes[QUAD * g : QUAD * g + PACK, dst : dst + width].bitcast(I32),
-                in_=stage[row : row + PACK, src : src + width].bitcast(I32),
+                out=planes[QUAD * g : QUAD * g + PACK, o * REGION : (o + 1) * REGION].bitcast(I32),
+                in_=planes[row : row + PACK, 0:REGION].bitcast(I32),
             )
 
         for o, g in moves:
             move(nc.sync if o else nc.scalar, o, g)
+        nc.sync.dma_start(
+            out=q_codes[:].bitcast(I32).rearrange("p (o q) -> p o q", o=PASSES),
+            in_=q_words[0].rearrange("o p q b -> p o (q b)").bitcast(I32),
+        )
 
         vs_col = []
         for u in range(PAGES):
@@ -141,6 +147,11 @@ def tile_attend_pkv4q_silu_gate_kernel(
         )
         v_g = shared.tile([P, PAGES * DV], U32, name="v_g", align_bytes=64, offset=8 * PAGE)
         nc.vector.tensor_copy(v_g[:], v_pool[:].indirect(voffs_t[:]))
+        for g in range(PACK):
+            nc.sync.dma_start(
+                out=v_plane[QUAD * g : QUAD * g + PACK, :].bitcast(I32),
+                in_=vsc_g[V_ROW + PACK * g : V_ROW + PACK * (g + 1), :].bitcast(I32),
+            )
         og_t = sb.tile([P, Q_TILES, DV], F32, name="og_t")
         nc.sync.dma_start(out=og_t[:], in_=og[0].rearrange("(h p) e -> p h e", p=P))
 
@@ -195,7 +206,7 @@ def tile_attend_pkv4q_silu_gate_kernel(
                     lhsT=w_codes[:].bitcast(FP8X4),
                     lhsT_scale=w_plane[:],
                     rhs=v_g[:, u * DV : (u + 1) * DV].bitcast(FP8X4),
-                    rhs_scale=planes[:, REGION + u * DV : REGION + (u + 1) * DV],
+                    rhs_scale=v_plane[:, u * DV : (u + 1) * DV],
                     start=(u == 0),
                     stop=(u == PAGES - 1),
                 )

@@ -28,6 +28,7 @@ QUAD = 32
 GROUP_ROWS = PASSES * 16
 VS_ROW = P - 1
 V_ROW = P - 16
+WARM = (256, 128)
 HALF = PAGE // 2
 REGION = N + NQ
 KS_SPLIT = 3 * T // 4
@@ -89,10 +90,14 @@ def tile_attend_pkv4q_silu_gate_kernel(
         nc.scalar.dma_start(out=vs_pool[VS_ROW:P, :], in_=vs[0:1, :])
         table = sb.tile([P, 7], F32, name="table")
         nc.scalar.activation(out=table[:], in_=one[:], func=ACT.Silu)
+        nc.sync.dma_start(
+            out=q_codes[:].bitcast(I32).rearrange("p (o q) -> p o q", o=PASSES),
+            in_=q_words[0].rearrange("o p q b -> p o (q b)").bitcast(I32),
+        )
         nc.sync.dma_start(out=k_pool[:].bitcast(I32), in_=k_words[0].rearrange("p t b -> p (t b)").bitcast(I32))
         page_offs = [offs_t[:, u * PAGE // 16 : (u + 1) * PAGE // 16] for u in range(PAGES)]
 
-        ks_g = [shared.tile([P, PAGE], U8, name="ks_g%d" % u, align_bytes=64, offset=u * PAGE) for u in range(PAGES)]
+        ks_g = [shared.tile([P, PAGE], U8, name="ks_g%d" % u, align_bytes=64, offset=(40 + u) * PAGE) for u in range(PAGES)]
         for u in range(PAGES):
             nc.vector.tensor_copy(ks_g[u][:], ks_pool[:].indirect(page_offs[u]))
         for u in range(PAGES):
@@ -100,7 +105,7 @@ def tile_attend_pkv4q_silu_gate_kernel(
                 planes[:, K_COL[0] + u * PAGE : K_COL[0] + (u + 1) * PAGE].rearrange("p (r s) -> p r s", r=PACK),
                 ks_g[u][:].rearrange("p (s r) -> p r s", r=PACK),
             )
-        vsc_g = shared.tile([P, PAGES * DV], U8, name="vsc_g", align_bytes=64, offset=0)
+        vsc_g = shared.tile([P, PAGES * DV], U8, name="vsc_g", align_bytes=64, offset=40 * PAGE)
         nc.vector.tensor_copy(vsc_g[:], vsc_pool[:].indirect(voffs_t[:]))
         moves = [(o, g) for o in range(PASSES) for g in range(PACK) if (o, g) != (0, 0)]
 
@@ -113,17 +118,22 @@ def tile_attend_pkv4q_silu_gate_kernel(
 
         for o, g in moves:
             move(nc.sync if o else nc.scalar, o, g)
+
+        v_pool = sb.tile([P, POOL_PAGES * DV], U32, name="v_pool", align_bytes=64)
         nc.sync.dma_start(
-            out=q_codes[:].bitcast(I32).rearrange("p (o q) -> p o q", o=PASSES),
-            in_=q_words[0].rearrange("o p q b -> p o (q b)").bitcast(I32),
+            out=v_pool[:].bitcast(I32).rearrange("p (u e) -> p u e", u=POOL_PAGES),
+            in_=v_words.rearrange("u p e b -> p u (e b)").bitcast(I32),
         )
 
         vs_col = []
+        vs_rows = []
         for u in range(PAGES):
             vs_g = sb.tile([P, PAGE], F32, name="vs_g%d" % u)
             nc.scalar.activation(out=vs_g[:], in_=vs_pool[:].indirect(page_offs[u]), func=ACT.Copy)
+            vs_rows.append(vs_g)
+        for u, vs_g in enumerate(vs_rows):
             col = sb.tile([P, PACK], F32, name="vs_col%d" % u)
-            nc.scalar.dma_start(out=col[:], in_=vs_g[VS_ROW:P, :].rearrange("o (p r) -> o p r", r=PACK))
+            nc.sync.dma_start(out=col[:], in_=vs_g[VS_ROW:P, :].rearrange("o (p r) -> o p r", r=PACK))
             vs_col.append(col)
 
         k_codes = [shared.tile([P, PASSES * PAGE], U16, name="k_codes%d" % u, align_bytes=64, offset=(16 + 4 * u) * PAGE) for u in range(PAGES)]
@@ -134,17 +144,24 @@ def tile_attend_pkv4q_silu_gate_kernel(
                 first = (u * PAGE + a * HALF) // 16
                 nc.vector.tensor_copy(part[:], k_pool[:].indirect(offs_t[:, first : first + HALF // 16]))
                 k_g.append(part)
-            pieces = [(0, 0, PASSES), (1, 0, 1), (1, 1, PASSES)] if u == 0 else [(0, 0, PASSES), (1, 0, PASSES)]
+            if u == 0:
+                warm = ps.tile([P, NQ], F32, name="warm", tag="y0")
+                for width in WARM:
+                    nc.tensor.matmul_mx(
+                        out=warm[:, 0:width],
+                        lhsT=k_g[1][:].bitcast(U16)[:, 0:P].bitcast(FP4X4),
+                        lhsT_scale=planes[:, Q_COL[0] : Q_COL[0] + P],
+                        rhs=q_codes[:, 0:width].bitcast(FP8X4),
+                        rhs_scale=planes[:, Q_COL[0] : Q_COL[0] + width],
+                        start=True,
+                        stop=True,
+                    )
+            pieces = [(0, 0, PASSES), (1, 1, PASSES), (1, 0, 1)] if u == 0 else [(0, 0, PASSES), (1, 0, PASSES)]
             for a, first, last in pieces:
                 nc.vector.tensor_copy(
                     k_codes[u][:].rearrange("p (o r s) -> p o s r", o=PASSES, r=PACK)[:, first:last, a * HALF // PACK : (a + 1) * HALF // PACK, :],
                     k_g[a][:].bitcast(U16).rearrange("p (s r o) -> p o s r", o=PASSES, r=PACK)[:, first:last],
                 )
-        v_pool = sb.tile([P, POOL_PAGES * DV], U32, name="v_pool", align_bytes=64)
-        nc.sync.dma_start(
-            out=v_pool[:].bitcast(I32).rearrange("p (u e) -> p u e", u=POOL_PAGES),
-            in_=v_words.rearrange("u p e b -> p u (e b)").bitcast(I32),
-        )
         v_g = shared.tile([P, PAGES * DV], U32, name="v_g", align_bytes=64, offset=8 * PAGE)
         nc.vector.tensor_copy(v_g[:], v_pool[:].indirect(voffs_t[:]))
         for g in range(PACK):
@@ -159,7 +176,7 @@ def tile_attend_pkv4q_silu_gate_kernel(
 
         def score_bank(u, h):
             scores = ps.tile([P, PACK, P], F32, name="scores%d%d" % (u, h))
-            for o in range(PASSES):
+            for o in (1, 0):
                 for r in range(PACK):
                     k0 = o * PAGE + r * P
                     s0 = K_COL[o] + u * PAGE + r * P
@@ -169,8 +186,8 @@ def tile_attend_pkv4q_silu_gate_kernel(
                         lhsT_scale=planes[:, s0 : s0 + P],
                         rhs=q_codes[:, o * NQ + h * P : o * NQ + (h + 1) * P].bitcast(FP8X4),
                         rhs_scale=planes[:, Q_COL[o] + h * P : Q_COL[o] + (h + 1) * P],
-                        start=(o == 0 and r == 0),
-                        stop=(o == PASSES - 1 and r == PACK - 1),
+                        start=(o == 1 and r == 0),
+                        stop=(o == 0 and r == PACK - 1),
                     )
             return scores
 

@@ -55,7 +55,7 @@ def tile_attend_pkv4q_silu_gate_kernel(
         vs_pool = sb.tile([P, T], F32, name="vs_pool", align_bytes=64)
         planes = sb.tile([P, PLANES], U8, name="planes", align_bytes=64)
         vsc_pool = sb.tile([P, POOL_PAGES * DV], U8, name="vsc_pool", align_bytes=64)
-        q_codes = sb.tile([P, PASSES * NQ], U32, name="q_codes", align_bytes=64)
+        q_codes = [sb.tile([P, PASSES * P], U32, name="q_codes%d" % h, align_bytes=64) for h in range(Q_TILES)]
 
         v_plane = sb.tile([P, PAGES * DV], U8, name="v_plane", align_bytes=64)
         nc.gpsimd.memset(vsc_pool[0:V_ROW, :].bitcast(I32), 0)
@@ -91,8 +91,8 @@ def tile_attend_pkv4q_silu_gate_kernel(
         table = sb.tile([P, 7], F32, name="table")
         nc.scalar.activation(out=table[:], in_=one[:], func=ACT.Silu)
         nc.sync.dma_start(
-            out=q_codes[:].bitcast(I32).rearrange("p (o q) -> p o q", o=PASSES),
-            in_=q_words[0].rearrange("o p q b -> p o (q b)").bitcast(I32),
+            out=q_codes[0][:].bitcast(I32).rearrange("p (o q) -> p o q", o=PASSES),
+            in_=q_words[0][:, :, 0 * P : (0 + 1) * P, :].rearrange("o p q b -> p o (q b)").bitcast(I32),
         )
         nc.sync.dma_start(out=k_pool[:].bitcast(I32), in_=k_words[0].rearrange("p t b -> p (t b)").bitcast(I32))
         page_offs = [offs_t[:, u * PAGE // 16 : (u + 1) * PAGE // 16] for u in range(PAGES)]
@@ -118,6 +118,10 @@ def tile_attend_pkv4q_silu_gate_kernel(
 
         for o, g in moves:
             move(nc.sync if o else nc.scalar, o, g)
+        nc.sync.dma_start(
+            out=q_codes[1][:].bitcast(I32).rearrange("p (o q) -> p o q", o=PASSES),
+            in_=q_words[0][:, :, 1 * P : (1 + 1) * P, :].rearrange("o p q b -> p o (q b)").bitcast(I32),
+        )
 
         v_pool = sb.tile([P, POOL_PAGES * DV], U32, name="v_pool", align_bytes=64)
         nc.sync.dma_start(
@@ -151,7 +155,7 @@ def tile_attend_pkv4q_silu_gate_kernel(
                         out=warm[:, 0:width],
                         lhsT=k_g[1][:].bitcast(U16)[:, 0:P].bitcast(FP4X4),
                         lhsT_scale=planes[:, Q_COL[0] : Q_COL[0] + P],
-                        rhs=q_codes[:, 0:width].bitcast(FP8X4),
+                        rhs=q_codes[0][:, 0:width].bitcast(FP8X4),
                         rhs_scale=planes[:, Q_COL[0] : Q_COL[0] + width],
                         start=True,
                         stop=True,
@@ -184,7 +188,7 @@ def tile_attend_pkv4q_silu_gate_kernel(
                         out=scores[:, r, :],
                         lhsT=k_codes[u][:, k0 : k0 + P].bitcast(FP4X4),
                         lhsT_scale=planes[:, s0 : s0 + P],
-                        rhs=q_codes[:, o * NQ + h * P : o * NQ + (h + 1) * P].bitcast(FP8X4),
+                        rhs=q_codes[h][:, o * P : (o + 1) * P].bitcast(FP8X4),
                         rhs_scale=planes[:, Q_COL[o] + h * P : Q_COL[o] + (h + 1) * P],
                         start=(o == 1 and r == 0),
                         stop=(o == 0 and r == PACK - 1),

@@ -1,6 +1,7 @@
 from contextlib import ExitStack
 
 import concourse.mybir as mybir
+from concourse.masks import make_identity
 
 F32 = mybir.dt.float32
 BF16 = mybir.dt.bfloat16
@@ -16,6 +17,7 @@ ALU = mybir.AluOpType
 P = 128
 PACK = 4
 PAGE = P * PACK
+HALF = PAGE // 2
 T = 4096
 N = 1024
 NQ = 256
@@ -25,16 +27,11 @@ PAGES = N // PAGE
 POOL_PAGES = T // PAGE
 Q_TILES = NQ // P
 QUAD = 32
-GROUP_ROWS = PASSES * 16
-VS_ROW = P - 1
+SCALE_ROWS = PASSES * 16
 V_ROW = P - 16
-WARM = (256, 128)
-HALF = PAGE // 2
+VS_ROW = P - POOL_PAGES * PACK
+VS_BASE = PAGE - P
 REGION = N + NQ
-KS_SPLIT = 3 * T // 4
-K_COL = (0, REGION)
-Q_COL = (K_COL[0] + N, K_COL[1] + N)
-PLANES = PASSES * REGION
 
 FLOPS = 2 * NQ * N * (PASSES * PAGE + DV)
 
@@ -50,131 +47,157 @@ def tile_attend_pkv4q_silu_gate_kernel(
 
         offs_t = sb.tile([P, N // 16], U16, name="offs_t")
         voffs_t = sb.tile([P, PAGES * DV // 16], U16, name="voffs_t")
-        k_pool = sb.tile([P, T], U32, name="k_pool", align_bytes=64)
+        k_half = [
+            shared.tile([P, T], U32, name="k_half0", align_bytes=64, offset=40 * PAGE),
+            sb.tile([P, T], U32, name="k_half1", align_bytes=64),
+        ]
         ks_pool = sb.tile([P, T], U8, name="ks_pool", align_bytes=64)
-        vs_pool = sb.tile([P, T], F32, name="vs_pool", align_bytes=64)
-        planes = sb.tile([P, PLANES], U8, name="planes", align_bytes=64)
+        planes = sb.tile([P, PASSES * REGION], U8, name="planes", align_bytes=64)
         vsc_pool = sb.tile([P, POOL_PAGES * DV], U8, name="vsc_pool", align_bytes=64)
-        q_codes = [sb.tile([P, PASSES * P], U32, name="q_codes%d" % h, align_bytes=64) for h in range(Q_TILES)]
-
         v_plane = sb.tile([P, PAGES * DV], U8, name="v_plane", align_bytes=64)
-        nc.gpsimd.memset(vsc_pool[0:V_ROW, :].bitcast(I32), 0)
-        nc.gpsimd.memset(ks_pool[2 * QUAD : P, KS_SPLIT:].bitcast(I32), 0)
-        nc.gpsimd.memset(vs_pool[0:VS_ROW, :], 0.0)
-        nc.gpsimd.memset(v_plane[:].bitcast(I32), 0)
-        one = sb.tile([P, 7], F32, name="one")
-        nc.vector.memset(one[:], 1.0)
+        q_codes = [
+            sb.tile([P, PASSES * P], U32, name="q_codes0", align_bytes=64),
+            shared.tile([P, PASSES * P], U32, name="q_codes1", align_bytes=64, offset=40 * PAGE),
+        ]
+        vs_rows = sb.tile([P, PAGE], F32, name="vs_rows")
+        vs_pool = sb.tile([P, VS_BASE + T], F32, name="vs_pool", align_bytes=64)
+        ident = sb.tile([P, P], F32, name="ident")
 
         def clear_odd(words):
             odd = words.shape[1] // 2 + 1
             nc.vector.memset(words[:, 0:odd], 0)
             nc.vector.memset(words[:, odd:], 0)
 
+        one = sb.tile([P, 7], F32, name="one")
+        nc.vector.memset(one[:], 1.0)
         clear_odd(ks_pool[QUAD : 2 * QUAD, :].bitcast(I32))
-        clear_odd(ks_pool[2 * QUAD : P, 0:KS_SPLIT].bitcast(I32))
+        clear_odd(ks_pool[2 * QUAD : P, :].bitcast(I32))
+
+        vs_pages = vs_pool[:, VS_BASE:].rearrange("p (u j) -> p u j", u=POOL_PAGES)
         for first, last in ((QUAD, 2 * QUAD), (2 * QUAD, P)):
-            nc.vector.memset(planes[first:last, Q_COL[0] : REGION + 4].bitcast(I32), 0)
-        clear_odd(planes[:, REGION:].bitcast(I32))
+            nc.gpsimd.memset(planes[first:last, N:REGION].bitcast(I32), 0)
+        nc.gpsimd.memset(planes[:, REGION:].bitcast(I32), 0)
+        nc.gpsimd.memset(vsc_pool[0:V_ROW, :].bitcast(I32), 0)
+        nc.gpsimd.memset(vs_rows[0:VS_ROW, :], 0.0)
+        make_identity(nc, ident[:])
+        nc.gpsimd.memset(vs_pages[:, :, PACK:P], 0.0)
+        nc.gpsimd.memset(v_plane[:].bitcast(I32), 0)
+
+        def load_keys(a):
+            halves = "p (u a t) -> p u a t"
+            nc.sync.dma_start(
+                out=k_half[a][:].bitcast(I32).rearrange(halves, a=2, t=HALF)[:, :, a, :],
+                in_=k_words[0].rearrange("p t b -> p (t b)").bitcast(I32).rearrange(halves, a=2, t=HALF)[:, :, a, :],
+            )
+
+        def load_queries(queue, h):
+            queue.dma_start(
+                out=q_codes[h][:].bitcast(I32).rearrange("p (o q) -> p o q", o=PASSES),
+                in_=q_words[0][:, :, h * P : (h + 1) * P, :].rearrange("o p q b -> p o (q b)").bitcast(I32),
+            )
 
         nc.sync.dma_start(offs_t[:], offs)
-        nc.sync.dma_start(out=ks_pool[0:GROUP_ROWS, :].bitcast(I32), in_=k_scales.rearrange("o f t -> (o f) t").bitcast(I32))
+        nc.sync.dma_start(out=ks_pool[0:SCALE_ROWS, :].bitcast(I32), in_=k_scales.rearrange("o f t -> (o f) t").bitcast(I32))
         nc.sync.dma_start(voffs_t[:], voffs)
+        nc.scalar.dma_start(
+            out=planes[0:SCALE_ROWS, N:REGION].bitcast(I32),
+            in_=q_scales[0].rearrange("o f q -> (o f) q").bitcast(I32),
+        )
+        skew = vs.rearrange("a t -> (a t)")[0 : PACK * (T + 1)].rearrange("(r t) -> r t", r=PACK)[:, 0:T]
+        nc.scalar.dma_start(out=vs_rows[VS_ROW:P, :], in_=skew.rearrange("r (u j) -> u r j", u=POOL_PAGES))
         nc.scalar.dma_start(
             out=vsc_pool[V_ROW:P, :].bitcast(I32).rearrange("f (u e) -> f u e", u=POOL_PAGES),
             in_=v_scales.rearrange("u f e -> f u e").bitcast(I32),
         )
-        nc.scalar.dma_start(
-            out=planes[0:GROUP_ROWS, Q_COL[0] : Q_COL[0] + NQ].bitcast(I32),
-            in_=q_scales[0].rearrange("o f q -> (o f) q").bitcast(I32),
-        )
-        nc.scalar.dma_start(out=vs_pool[VS_ROW:P, :], in_=vs[0:1, :])
+        load_keys(0)
+        load_queries(nc.scalar, 0)
         table = sb.tile([P, 7], F32, name="table")
         nc.scalar.activation(out=table[:], in_=one[:], func=ACT.Silu)
-        nc.sync.dma_start(
-            out=q_codes[0][:].bitcast(I32).rearrange("p (o q) -> p o q", o=PASSES),
-            in_=q_words[0][:, :, 0 * P : (0 + 1) * P, :].rearrange("o p q b -> p o (q b)").bitcast(I32),
-        )
-        nc.sync.dma_start(out=k_pool[:].bitcast(I32), in_=k_words[0].rearrange("p t b -> p (t b)").bitcast(I32))
-        page_offs = [offs_t[:, u * PAGE // 16 : (u + 1) * PAGE // 16] for u in range(PAGES)]
+        load_keys(1)
 
-        ks_g = [shared.tile([P, PAGE], U8, name="ks_g%d" % u, align_bytes=64, offset=(40 + u) * PAGE) for u in range(PAGES)]
+        ks_g = [sb.tile([P, PAGE], U8, name="ks_g%d" % u, align_bytes=64) for u in range(PAGES)]
         for u in range(PAGES):
-            nc.vector.tensor_copy(ks_g[u][:], ks_pool[:].indirect(page_offs[u]))
+            nc.vector.tensor_copy(ks_g[u][:], ks_pool[:].indirect(offs_t[:, u * PAGE // 16 : (u + 1) * PAGE // 16]))
         for u in range(PAGES):
             nc.vector.tensor_copy(
-                planes[:, K_COL[0] + u * PAGE : K_COL[0] + (u + 1) * PAGE].rearrange("p (r s) -> p r s", r=PACK),
+                planes[:, u * PAGE : (u + 1) * PAGE].rearrange("p (r s) -> p r s", r=PACK),
                 ks_g[u][:].rearrange("p (s r) -> p r s", r=PACK),
             )
-        vsc_g = shared.tile([P, PAGES * DV], U8, name="vsc_g", align_bytes=64, offset=40 * PAGE)
-        nc.vector.tensor_copy(vsc_g[:], vsc_pool[:].indirect(voffs_t[:]))
-        moves = [(o, g) for o in range(PASSES) for g in range(PACK) if (o, g) != (0, 0)]
 
-        def move(queue, o, g):
-            row = 16 * o + PACK * g
-            queue.dma_start(
-                out=planes[QUAD * g : QUAD * g + PACK, o * REGION : (o + 1) * REGION].bitcast(I32),
-                in_=planes[row : row + PACK, 0:REGION].bitcast(I32),
+        def move_scales(queue, o):
+            for g in range(PACK):
+                row = 16 * o + PACK * g
+                if row:
+                    queue.dma_start(
+                        out=planes[QUAD * g : QUAD * g + PACK, o * REGION : (o + 1) * REGION].bitcast(I32),
+                        in_=planes[row : row + PACK, 0:REGION].bitcast(I32),
+                    )
+
+        move_scales(nc.sync, 0)
+        move_scales(nc.sync, 1)
+
+        turned = ps.tile([P, P], F32, name="turned")
+        nc.tensor.transpose(turned[:], vs_rows[:, 0:PAGE:PACK], ident[:])
+        nc.scalar.activation(
+            out=vs_pages[:, :, 0:PACK],
+            in_=turned[:, VS_ROW:P].rearrange("p (u r) -> p u r", r=PACK),
+            func=ACT.Copy,
+        )
+        vs_g = [
+            sb.tile([P, PAGE + PACK], F32, name="vs_g0"),
+            sb.tile([P, PAGE + PACK], F32, name="vs_g1"),
+        ]
+
+        def gather_vs(u):
+            for r in range(PACK):
+                first = (u * PAGE + r * P) // 16
+                nc.scalar.activation(
+                    out=vs_g[u][:, r * P : (r + 1) * P],
+                    in_=vs_pool[:, VS_BASE - r * P : VS_BASE - r * P + T].indirect(offs_t[:, first : first + P // 16]),
+                    func=ACT.Copy,
+                )
+
+        gather_vs(0)
+        gather_vs(1)
+        vs_col = [vs_g[u][:].rearrange("p (r j) -> p r j", r=PACK)[:, :, 0] for u in range(PAGES)]
+
+        k_codes = [shared.tile([P, PASSES * PAGE], U16, name="k_codes%d" % u, align_bytes=64, offset=(16 - 7 * u) * PAGE) for u in range(PAGES)]
+
+        def gather_keys(u, a, place):
+            part = shared.tile([P, HALF], U32, name="k_g%d%d" % (u, a), align_bytes=64, offset=place * PAGE)
+            first = (u * PAGE + a * HALF) // 16
+            nc.vector.tensor_copy(part[:], k_half[a][:].indirect(offs_t[:, first : first + HALF // 16]))
+            return part
+
+        def part_keys(u, a, part, first, last):
+            nc.vector.tensor_copy(
+                k_codes[u][:].rearrange("p (o r s) -> p o s r", o=PASSES, r=PACK)[:, first:last, a * HALF // PACK : (a + 1) * HALF // PACK, :],
+                part[:].bitcast(U16).rearrange("p (s r o) -> p o s r", o=PASSES, r=PACK)[:, first:last],
             )
 
-        for o, g in moves:
-            move(nc.sync if o else nc.scalar, o, g)
-        nc.sync.dma_start(
-            out=q_codes[1][:].bitcast(I32).rearrange("p (o q) -> p o q", o=PASSES),
-            in_=q_words[0][:, :, 1 * P : (1 + 1) * P, :].rearrange("o p q b -> p o (q b)").bitcast(I32),
-        )
-
-        v_pool = sb.tile([P, POOL_PAGES * DV], U32, name="v_pool", align_bytes=64)
+        early = [gather_keys(u, 0, 2 * u) for u in range(PAGES)]
+        part_keys(0, 0, early[0], 0, PASSES)
+        load_queries(nc.sync, 1)
+        v_pool = shared.tile([P, POOL_PAGES * DV], U32, name="v_pool", align_bytes=64, offset=42 * PAGE)
         nc.sync.dma_start(
             out=v_pool[:].bitcast(I32).rearrange("p (u e) -> p u e", u=POOL_PAGES),
             in_=v_words.rearrange("u p e b -> p u (e b)").bitcast(I32),
         )
-
-        vs_col = []
-        vs_rows = []
-        for u in range(PAGES):
-            vs_g = sb.tile([P, PAGE], F32, name="vs_g%d" % u)
-            nc.scalar.activation(out=vs_g[:], in_=vs_pool[:].indirect(page_offs[u]), func=ACT.Copy)
-            vs_rows.append(vs_g)
-        for u, vs_g in enumerate(vs_rows):
-            col = sb.tile([P, PACK], F32, name="vs_col%d" % u)
-            nc.sync.dma_start(out=col[:], in_=vs_g[VS_ROW:P, :].rearrange("o (p r) -> o p r", r=PACK))
-            vs_col.append(col)
-
-        k_codes = [shared.tile([P, PASSES * PAGE], U16, name="k_codes%d" % u, align_bytes=64, offset=(16 + 4 * u) * PAGE) for u in range(PAGES)]
-        for u in range(PAGES):
-            k_g = []
-            for a in range(2):
-                part = shared.tile([P, HALF], U32, name="k_g%d%d" % (u, a), align_bytes=64, offset=(7 + 5 * a + (1 - 2 * a) * u) * PAGE)
-                first = (u * PAGE + a * HALF) // 16
-                nc.vector.tensor_copy(part[:], k_pool[:].indirect(offs_t[:, first : first + HALF // 16]))
-                k_g.append(part)
-            if u == 0:
-                warm = ps.tile([P, NQ], F32, name="warm", tag="y0")
-                for width in WARM:
-                    nc.tensor.matmul_mx(
-                        out=warm[:, 0:width],
-                        lhsT=k_g[1][:].bitcast(U16)[:, 0:P].bitcast(FP4X4),
-                        lhsT_scale=planes[:, Q_COL[0] : Q_COL[0] + P],
-                        rhs=q_codes[0][:, 0:width].bitcast(FP8X4),
-                        rhs_scale=planes[:, Q_COL[0] : Q_COL[0] + width],
-                        start=True,
-                        stop=True,
-                    )
-            pieces = [(0, 0, PASSES), (1, 1, PASSES), (1, 0, 1)] if u == 0 else [(0, 0, PASSES), (1, 0, PASSES)]
-            for a, first, last in pieces:
-                nc.vector.tensor_copy(
-                    k_codes[u][:].rearrange("p (o r s) -> p o s r", o=PASSES, r=PACK)[:, first:last, a * HALF // PACK : (a + 1) * HALF // PACK, :],
-                    k_g[a][:].bitcast(U16).rearrange("p (s r o) -> p o s r", o=PASSES, r=PACK)[:, first:last],
-                )
-        v_g = shared.tile([P, PAGES * DV], U32, name="v_g", align_bytes=64, offset=8 * PAGE)
-        nc.vector.tensor_copy(v_g[:], v_pool[:].indirect(voffs_t[:]))
+        og_t = shared.tile([P, Q_TILES, DV], F32, name="og_t", align_bytes=64, offset=56 * PAGE)
+        nc.sync.dma_start(out=og_t[:], in_=og[0].rearrange("(h p) e -> p h e", p=P))
+        late = gather_keys(0, 1, 8)
+        part_keys(0, 1, late, 1, PASSES)
+        part_keys(0, 1, late, 0, 1)
+        late = gather_keys(1, 1, 7)
+        part_keys(1, 0, early[1], 0, PASSES)
+        part_keys(1, 1, late, 0, PASSES)
+        vsc_g = shared.tile([P, PAGES * DV], U8, name="vsc_g", align_bytes=64, offset=8 * PAGE)
+        nc.vector.tensor_copy(vsc_g[:], vsc_pool[:].indirect(voffs_t[:]))
         for g in range(PACK):
             nc.sync.dma_start(
                 out=v_plane[QUAD * g : QUAD * g + PACK, :].bitcast(I32),
                 in_=vsc_g[V_ROW + PACK * g : V_ROW + PACK * (g + 1), :].bitcast(I32),
             )
-        og_t = sb.tile([P, Q_TILES, DV], F32, name="og_t")
-        nc.sync.dma_start(out=og_t[:], in_=og[0].rearrange("(h p) e -> p h e", p=P))
 
         y = [ps.tile([P, DV], F32, name="y%d" % h, tag="y%d" % h) for h in range(Q_TILES)]
 
@@ -183,13 +206,14 @@ def tile_attend_pkv4q_silu_gate_kernel(
             for o in (1, 0):
                 for r in range(PACK):
                     k0 = o * PAGE + r * P
-                    s0 = K_COL[o] + u * PAGE + r * P
+                    s0 = o * REGION + u * PAGE + r * P
+                    q0 = o * REGION + N + h * P
                     nc.tensor.matmul_mx(
                         out=scores[:, r, :],
                         lhsT=k_codes[u][:, k0 : k0 + P].bitcast(FP4X4),
                         lhsT_scale=planes[:, s0 : s0 + P],
                         rhs=q_codes[h][:, o * P : (o + 1) * P].bitcast(FP8X4),
-                        rhs_scale=planes[:, Q_COL[o] + h * P : Q_COL[o] + (h + 1) * P],
+                        rhs_scale=planes[:, q0 : q0 + P],
                         start=(o == 1 and r == 0),
                         stop=(o == 0 and r == PACK - 1),
                     )
@@ -199,11 +223,11 @@ def tile_attend_pkv4q_silu_gate_kernel(
         for u in range(PAGES):
             for h in range(Q_TILES):
                 scores = score_bank(u, h)
-                act = sb.tile([P, P, PACK], F32, name="silu%d%d" % (u, h))
+                act = shared.tile([P, P, PACK], F32, name="silu%d%d" % (u, h), align_bytes=64, offset=(80 + 8 * u + 4 * h) * PAGE)
                 nc.scalar.activation(out=act[:], in_=scores[:].rearrange("p r q -> p q r"), func=ACT.Silu)
                 silu[(u, h)] = act
 
-        half = shared.tile([P, Q_TILES, DV], F32, name="half", align_bytes=64, offset=20 * PAGE)
+        half = shared.tile([P, Q_TILES, DV], F32, name="half", align_bytes=64, offset=11 * PAGE)
         gate = sb.tile([P, Q_TILES, DV], F32, name="gate")
         nc.scalar.activation(out=half[:], in_=og_t[:], func=ACT.Tanh, scale=0.5)
         nc.scalar.activation(out=gate[:], in_=half[:], func=ACT.Copy, scale=1.0 / 32.0, bias=1.0 / 32.0)
@@ -212,8 +236,11 @@ def tile_attend_pkv4q_silu_gate_kernel(
             weights = []
             for h in range(Q_TILES):
                 w = sb.tile([P, P, PACK], BF16, name="w%d%d" % (u, h), align_bytes=64)
-                nc.vector.tensor_tensor(w[:], silu[(u, h)][:], vs_col[u][:].unsqueeze(1).to_broadcast([P, P, PACK]), ALU.mult)
+                nc.vector.tensor_tensor(w[:], silu[(u, h)][:], vs_col[u].unsqueeze(1).to_broadcast([P, P, PACK]), ALU.mult)
                 weights.append(w)
+                if (u, h) == (0, 0):
+                    v_g = shared.tile([P, PAGES * DV], U32, name="v_g", align_bytes=64, offset=80 * PAGE)
+                    nc.vector.tensor_copy(v_g[:], v_pool[:].indirect(voffs_t[:]))
             for h in range(Q_TILES):
                 w_codes = sb.tile([P, P], U32, name="w_codes%d%d" % (u, h), align_bytes=64)
                 w_plane = sb.tile([P, P], U8, name="w_plane%d%d" % (u, h), align_bytes=64)

@@ -32,6 +32,7 @@ V_ROW = P - 16
 VS_ROW = P - POOL_PAGES * PACK
 VS_BASE = PAGE - P
 REGION = N + NQ
+WARM = (256, 128)
 
 FLOPS = 2 * NQ * N * (PASSES * PAGE + DV)
 
@@ -47,18 +48,12 @@ def tile_attend_pkv4q_silu_gate_kernel(
 
         offs_t = sb.tile([P, N // 16], U16, name="offs_t")
         voffs_t = sb.tile([P, PAGES * DV // 16], U16, name="voffs_t")
-        k_half = [
-            shared.tile([P, T], U32, name="k_half0", align_bytes=64, offset=40 * PAGE),
-            sb.tile([P, T], U32, name="k_half1", align_bytes=64),
-        ]
+        k_pool = sb.tile([P, T], U32, name="k_pool", align_bytes=64)
         ks_pool = sb.tile([P, T], U8, name="ks_pool", align_bytes=64)
         planes = sb.tile([P, PASSES * REGION], U8, name="planes", align_bytes=64)
         vsc_pool = sb.tile([P, POOL_PAGES * DV], U8, name="vsc_pool", align_bytes=64)
         v_plane = sb.tile([P, PAGES * DV], U8, name="v_plane", align_bytes=64)
-        q_codes = [
-            sb.tile([P, PASSES * P], U32, name="q_codes0", align_bytes=64),
-            shared.tile([P, PASSES * P], U32, name="q_codes1", align_bytes=64, offset=40 * PAGE),
-        ]
+        q_codes = sb.tile([P, PASSES * NQ], U32, name="q_codes", align_bytes=64)
         vs_rows = sb.tile([P, PAGE], F32, name="vs_rows")
         vs_pool = sb.tile([P, VS_BASE + T], F32, name="vs_pool", align_bytes=64)
         ident = sb.tile([P, P], F32, name="ident")
@@ -83,19 +78,6 @@ def tile_attend_pkv4q_silu_gate_kernel(
         nc.gpsimd.memset(vs_pages[:, :, PACK:P], 0.0)
         nc.gpsimd.memset(v_plane[:].bitcast(I32), 0)
 
-        def load_keys(a):
-            halves = "p (u a t) -> p u a t"
-            nc.sync.dma_start(
-                out=k_half[a][:].bitcast(I32).rearrange(halves, a=2, t=HALF)[:, :, a, :],
-                in_=k_words[0].rearrange("p t b -> p (t b)").bitcast(I32).rearrange(halves, a=2, t=HALF)[:, :, a, :],
-            )
-
-        def load_queries(queue, h):
-            queue.dma_start(
-                out=q_codes[h][:].bitcast(I32).rearrange("p (o q) -> p o q", o=PASSES),
-                in_=q_words[0][:, :, h * P : (h + 1) * P, :].rearrange("o p q b -> p o (q b)").bitcast(I32),
-            )
-
         nc.sync.dma_start(offs_t[:], offs)
         nc.sync.dma_start(out=ks_pool[0:SCALE_ROWS, :].bitcast(I32), in_=k_scales.rearrange("o f t -> (o f) t").bitcast(I32))
         nc.sync.dma_start(voffs_t[:], voffs)
@@ -109,13 +91,15 @@ def tile_attend_pkv4q_silu_gate_kernel(
             out=vsc_pool[V_ROW:P, :].bitcast(I32).rearrange("f (u e) -> f u e", u=POOL_PAGES),
             in_=v_scales.rearrange("u f e -> f u e").bitcast(I32),
         )
-        load_keys(0)
-        load_queries(nc.scalar, 0)
+        nc.sync.dma_start(out=k_pool[:].bitcast(I32), in_=k_words[0].rearrange("p t b -> p (t b)").bitcast(I32))
+        nc.sync.dma_start(
+            out=q_codes[:].bitcast(I32).rearrange("p (o q) -> p o q", o=PASSES),
+            in_=q_words[0].rearrange("o p q b -> p o (q b)").bitcast(I32),
+        )
         table = sb.tile([P, 7], F32, name="table")
         nc.scalar.activation(out=table[:], in_=one[:], func=ACT.Silu)
-        load_keys(1)
 
-        ks_g = [sb.tile([P, PAGE], U8, name="ks_g%d" % u, align_bytes=64) for u in range(PAGES)]
+        ks_g = [shared.tile([P, PAGE], U8, name="ks_g%d" % u, align_bytes=64, offset=(30 + u) * PAGE) for u in range(PAGES)]
         for u in range(PAGES):
             nc.vector.tensor_copy(ks_g[u][:], ks_pool[:].indirect(offs_t[:, u * PAGE // 16 : (u + 1) * PAGE // 16]))
         for u in range(PAGES):
@@ -135,6 +119,20 @@ def tile_attend_pkv4q_silu_gate_kernel(
 
         move_scales(nc.sync, 0)
         move_scales(nc.sync, 1)
+        v_pool = sb.tile([P, POOL_PAGES * DV], U32, name="v_pool", align_bytes=64)
+        nc.sync.dma_start(
+            out=v_pool[:].bitcast(I32).rearrange("p (u e) -> p u e", u=POOL_PAGES),
+            in_=v_words.rearrange("u p e b -> p u (e b)").bitcast(I32),
+        )
+        vsc_g = shared.tile([P, PAGES * DV], U8, name="vsc_g", align_bytes=64, offset=30 * PAGE)
+        nc.vector.tensor_copy(vsc_g[:], vsc_pool[:].indirect(voffs_t[:]))
+        for g in range(PACK):
+            nc.sync.dma_start(
+                out=v_plane[QUAD * g : QUAD * g + PACK, :].bitcast(I32),
+                in_=vsc_g[V_ROW + PACK * g : V_ROW + PACK * (g + 1), :].bitcast(I32),
+            )
+        og_t = sb.tile([P, Q_TILES, DV], F32, name="og_t")
+        nc.sync.dma_start(out=og_t[:], in_=og[0].rearrange("(h p) e -> p h e", p=P))
 
         turned = ps.tile([P, P], F32, name="turned")
         nc.tensor.transpose(turned[:], vs_rows[:, 0:PAGE:PACK], ident[:])
@@ -166,7 +164,7 @@ def tile_attend_pkv4q_silu_gate_kernel(
         def gather_keys(u, a, place):
             part = shared.tile([P, HALF], U32, name="k_g%d%d" % (u, a), align_bytes=64, offset=place * PAGE)
             first = (u * PAGE + a * HALF) // 16
-            nc.vector.tensor_copy(part[:], k_half[a][:].indirect(offs_t[:, first : first + HALF // 16]))
+            nc.vector.tensor_copy(part[:], k_pool[:].indirect(offs_t[:, first : first + HALF // 16]))
             return part
 
         def part_keys(u, a, part, first, last):
@@ -175,35 +173,31 @@ def tile_attend_pkv4q_silu_gate_kernel(
                 part[:].bitcast(U16).rearrange("p (s r o) -> p o s r", o=PASSES, r=PACK)[:, first:last],
             )
 
-        early = [gather_keys(u, 0, 2 * u) for u in range(PAGES)]
-        part_keys(0, 0, early[0], 0, PASSES)
-        load_queries(nc.sync, 1)
-        v_pool = shared.tile([P, POOL_PAGES * DV], U32, name="v_pool", align_bytes=64, offset=42 * PAGE)
-        nc.sync.dma_start(
-            out=v_pool[:].bitcast(I32).rearrange("p (u e) -> p u e", u=POOL_PAGES),
-            in_=v_words.rearrange("u p e b -> p u (e b)").bitcast(I32),
-        )
-        og_t = shared.tile([P, Q_TILES, DV], F32, name="og_t", align_bytes=64, offset=56 * PAGE)
-        nc.sync.dma_start(out=og_t[:], in_=og[0].rearrange("(h p) e -> p h e", p=P))
-        late = gather_keys(0, 1, 8)
-        part_keys(0, 1, late, 1, PASSES)
-        part_keys(0, 1, late, 0, 1)
-        late = gather_keys(1, 1, 7)
-        part_keys(1, 0, early[1], 0, PASSES)
-        part_keys(1, 1, late, 0, PASSES)
-        vsc_g = shared.tile([P, PAGES * DV], U8, name="vsc_g", align_bytes=64, offset=8 * PAGE)
-        nc.vector.tensor_copy(vsc_g[:], vsc_pool[:].indirect(voffs_t[:]))
-        for g in range(PACK):
-            nc.sync.dma_start(
-                out=v_plane[QUAD * g : QUAD * g + PACK, :].bitcast(I32),
-                in_=vsc_g[V_ROW + PACK * g : V_ROW + PACK * (g + 1), :].bitcast(I32),
+        halves = [gather_keys(0, a, 2 + 4 * a) for a in range(2)]
+        warm = ps.tile([P, NQ], F32, name="warm", tag="y0")
+        for width in WARM:
+            nc.tensor.matmul_mx(
+                out=warm[:, 0:width],
+                lhsT=halves[1][:].bitcast(U16)[:, 0:P].bitcast(FP4X4),
+                lhsT_scale=planes[:, N : N + P],
+                rhs=q_codes[:, 0:width].bitcast(FP8X4),
+                rhs_scale=planes[:, N : N + width],
+                start=True,
+                stop=True,
             )
+        part_keys(0, 0, halves[0], 0, PASSES)
+        part_keys(0, 1, halves[1], 0, 1)
+        part_keys(0, 1, halves[1], 1, PASSES)
+        halves = [gather_keys(1, a, 5 + 2 * a) for a in range(2)]
+        for a in range(2):
+            part_keys(1, a, halves[a], 0, PASSES)
 
         y = [ps.tile([P, DV], F32, name="y%d" % h, tag="y%d" % h) for h in range(Q_TILES)]
 
         def score_bank(u, h):
             scores = ps.tile([P, PACK, P], F32, name="scores%d%d" % (u, h))
-            for o in (1, 0):
+            order = (0, 1) if (u, h) == (0, 0) else (1, 0)
+            for o in order:
                 for r in range(PACK):
                     k0 = o * PAGE + r * P
                     s0 = o * REGION + u * PAGE + r * P
@@ -212,10 +206,10 @@ def tile_attend_pkv4q_silu_gate_kernel(
                         out=scores[:, r, :],
                         lhsT=k_codes[u][:, k0 : k0 + P].bitcast(FP4X4),
                         lhsT_scale=planes[:, s0 : s0 + P],
-                        rhs=q_codes[h][:, o * P : (o + 1) * P].bitcast(FP8X4),
+                        rhs=q_codes[:, o * NQ + h * P : o * NQ + (h + 1) * P].bitcast(FP8X4),
                         rhs_scale=planes[:, q0 : q0 + P],
-                        start=(o == 1 and r == 0),
-                        stop=(o == 0 and r == PACK - 1),
+                        start=(o == order[0] and r == 0),
+                        stop=(o == order[1] and r == PACK - 1),
                     )
             return scores
 

@@ -29,9 +29,10 @@ Q_TILES = NQ // P
 QUAD = 32
 SCALE_ROWS = PASSES * 16
 V_ROW = P - 16
-VS_ROW = P - POOL_PAGES * PACK
+VS_ROW = P - POOL_PAGES
 VS_BASE = PAGE - P
 REGION = N + NQ
+KS_SPLIT = 5 * T // 8
 WARM = (256, 128)
 
 FLOPS = 2 * NQ * N * (PASSES * PAGE + DV)
@@ -66,31 +67,32 @@ def tile_attend_pkv4q_silu_gate_kernel(
         one = sb.tile([P, 7], F32, name="one")
         nc.vector.memset(one[:], 1.0)
         clear_odd(ks_pool[QUAD : 2 * QUAD, :].bitcast(I32))
-        clear_odd(ks_pool[2 * QUAD : P, :].bitcast(I32))
+        clear_odd(ks_pool[2 * QUAD : P, 0:KS_SPLIT].bitcast(I32))
 
         vs_pages = vs_pool[:, VS_BASE:].rearrange("p (u j) -> p u j", u=POOL_PAGES)
+        nc.gpsimd.memset(vsc_pool[0:V_ROW, :].bitcast(I32), 0)
+        nc.gpsimd.memset(ks_pool[2 * QUAD : P, KS_SPLIT:].bitcast(I32), 0)
         for first, last in ((QUAD, 2 * QUAD), (2 * QUAD, P)):
             nc.gpsimd.memset(planes[first:last, N:REGION].bitcast(I32), 0)
         nc.gpsimd.memset(planes[:, REGION:].bitcast(I32), 0)
-        nc.gpsimd.memset(vsc_pool[0:V_ROW, :].bitcast(I32), 0)
+        nc.gpsimd.memset(ident[:], 0.0)
         nc.gpsimd.memset(vs_rows[0:VS_ROW, :], 0.0)
-        make_identity(nc, ident[:])
+        make_identity(nc, ident[:], nomemset=True)
         nc.gpsimd.memset(vs_pages[:, :, PACK:P], 0.0)
         nc.gpsimd.memset(v_plane[:].bitcast(I32), 0)
 
+        nc.sync.dma_start(voffs_t[:], voffs)
         nc.sync.dma_start(offs_t[:], offs)
         nc.sync.dma_start(out=ks_pool[0:SCALE_ROWS, :].bitcast(I32), in_=k_scales.rearrange("o f t -> (o f) t").bitcast(I32))
-        nc.sync.dma_start(voffs_t[:], voffs)
-        nc.scalar.dma_start(
-            out=planes[0:SCALE_ROWS, N:REGION].bitcast(I32),
-            in_=q_scales[0].rearrange("o f q -> (o f) q").bitcast(I32),
-        )
-        skew = vs.rearrange("a t -> (a t)")[0 : PACK * (T + 1)].rearrange("(r t) -> r t", r=PACK)[:, 0:T]
-        nc.scalar.dma_start(out=vs_rows[VS_ROW:P, :], in_=skew.rearrange("r (u j) -> u r j", u=POOL_PAGES))
         nc.scalar.dma_start(
             out=vsc_pool[V_ROW:P, :].bitcast(I32).rearrange("f (u e) -> f u e", u=POOL_PAGES),
             in_=v_scales.rearrange("u f e -> f u e").bitcast(I32),
         )
+        nc.scalar.dma_start(
+            out=planes[0:SCALE_ROWS, N:REGION].bitcast(I32),
+            in_=q_scales[0].rearrange("o f q -> (o f) q").bitcast(I32),
+        )
+        nc.scalar.dma_start(out=vs_rows[VS_ROW:P, :], in_=vs[0].rearrange("(u j) -> u j", u=POOL_PAGES))
         nc.sync.dma_start(out=k_pool[:].bitcast(I32), in_=k_words[0].rearrange("p t b -> p (t b)").bitcast(I32))
         nc.sync.dma_start(
             out=q_codes[:].bitcast(I32).rearrange("p (o q) -> p o q", o=PASSES),
@@ -99,6 +101,8 @@ def tile_attend_pkv4q_silu_gate_kernel(
         table = sb.tile([P, 7], F32, name="table")
         nc.scalar.activation(out=table[:], in_=one[:], func=ACT.Silu)
 
+        vsc_g = sb.tile([P, PAGES * DV], U8, name="vsc_g", align_bytes=64)
+        nc.vector.tensor_copy(vsc_g[:], vsc_pool[:].indirect(voffs_t[:]))
         ks_g = [shared.tile([P, PAGE], U8, name="ks_g%d" % u, align_bytes=64, offset=(30 + u) * PAGE) for u in range(PAGES)]
         for u in range(PAGES):
             nc.vector.tensor_copy(ks_g[u][:], ks_pool[:].indirect(offs_t[:, u * PAGE // 16 : (u + 1) * PAGE // 16]))
@@ -124,8 +128,6 @@ def tile_attend_pkv4q_silu_gate_kernel(
             out=v_pool[:].bitcast(I32).rearrange("p (u e) -> p u e", u=POOL_PAGES),
             in_=v_words.rearrange("u p e b -> p u (e b)").bitcast(I32),
         )
-        vsc_g = shared.tile([P, PAGES * DV], U8, name="vsc_g", align_bytes=64, offset=30 * PAGE)
-        nc.vector.tensor_copy(vsc_g[:], vsc_pool[:].indirect(voffs_t[:]))
         for g in range(PACK):
             nc.sync.dma_start(
                 out=v_plane[QUAD * g : QUAD * g + PACK, :].bitcast(I32),
@@ -134,11 +136,12 @@ def tile_attend_pkv4q_silu_gate_kernel(
         og_t = sb.tile([P, Q_TILES, DV], F32, name="og_t")
         nc.sync.dma_start(out=og_t[:], in_=og[0].rearrange("(h p) e -> p h e", p=P))
 
-        turned = ps.tile([P, P], F32, name="turned")
-        nc.tensor.transpose(turned[:], vs_rows[:, 0:PAGE:PACK], ident[:])
+        turned = ps.tile([P, PACK, P], F32, name="turned")
+        for r in range(PACK):
+            nc.tensor.transpose(turned[:, r, :], vs_rows[:, r:PAGE:PACK], ident[:])
         nc.scalar.activation(
             out=vs_pages[:, :, 0:PACK],
-            in_=turned[:, VS_ROW:P].rearrange("p (u r) -> p u r", r=PACK),
+            in_=turned[:, :, VS_ROW:P].rearrange("p r u -> p u r"),
             func=ACT.Copy,
         )
         vs_g = [

@@ -33,7 +33,6 @@ VS_ROW = P - POOL_PAGES
 VS_BASE = PAGE - P
 REGION = N + NQ
 KS_SPLIT = 5 * T // 8
-WARM = (256, 128)
 
 FLOPS = 2 * NQ * N * (PASSES * PAGE + DV)
 
@@ -177,17 +176,6 @@ def tile_attend_pkv4q_silu_gate_kernel(
             )
 
         halves = [gather_keys(0, a, 2 + 4 * a) for a in range(2)]
-        warm = ps.tile([P, NQ], F32, name="warm", tag="y0")
-        for width in WARM:
-            nc.tensor.matmul_mx(
-                out=warm[:, 0:width],
-                lhsT=halves[1][:].bitcast(U16)[:, 0:P].bitcast(FP4X4),
-                lhsT_scale=planes[:, N : N + P],
-                rhs=q_codes[:, 0:width].bitcast(FP8X4),
-                rhs_scale=planes[:, N : N + width],
-                start=True,
-                stop=True,
-            )
         part_keys(0, 0, halves[0], 0, PASSES)
         part_keys(0, 1, halves[1], 0, 1)
         part_keys(0, 1, halves[1], 1, PASSES)

@@ -122,7 +122,7 @@ def tile_attend_pkv4q_silu_gate_kernel(
 
         move_scales(nc.sync, 0)
         move_scales(nc.sync, 1)
-        v_pool = sb.tile([P, POOL_PAGES * DV], U32, name="v_pool", align_bytes=64)
+        v_pool = shared.tile([P, POOL_PAGES * DV], U32, name="v_pool", align_bytes=64, offset=40 * PAGE)
         nc.sync.dma_start(
             out=v_pool[:].bitcast(I32).rearrange("p (u e) -> p u e", u=POOL_PAGES),
             in_=v_words.rearrange("u p e b -> p u (e b)").bitcast(I32),
@@ -217,32 +217,35 @@ def tile_attend_pkv4q_silu_gate_kernel(
         nc.scalar.activation(out=half[:], in_=og_t[:], func=ACT.Tanh, scale=0.5)
         nc.scalar.activation(out=gate[:], in_=half[:], func=ACT.Copy, scale=1.0 / 32.0, bias=1.0 / 32.0)
 
-        for u in range(PAGES):
-            weights = []
-            for h in range(Q_TILES):
-                w = sb.tile([P, P, PACK], BF16, name="w%d%d" % (u, h), align_bytes=64)
-                nc.vector.tensor_tensor(w[:], silu[(u, h)][:], vs_col[u].unsqueeze(1).to_broadcast([P, P, PACK]), ALU.mult)
-                weights.append(w)
-                if (u, h) == (0, 0):
-                    v_g = shared.tile([P, PAGES * DV], U32, name="v_g", align_bytes=64, offset=80 * PAGE)
-                    nc.vector.tensor_copy(v_g[:], v_pool[:].indirect(voffs_t[:]))
-            for h in range(Q_TILES):
-                w_codes = sb.tile([P, P], U32, name="w_codes%d%d" % (u, h), align_bytes=64)
-                w_plane = sb.tile([P, P], U8, name="w_plane%d%d" % (u, h), align_bytes=64)
-                nc.vector.quantize_mx(
-                    out=w_codes[:].bitcast(FP8X4),
-                    scales=w_plane[:],
-                    in_=weights[h][:].rearrange("p q r -> p (q r)"),
-                )
-                nc.tensor.matmul_mx(
-                    out=y[h][:],
-                    lhsT=w_codes[:].bitcast(FP8X4),
-                    lhsT_scale=w_plane[:],
-                    rhs=v_g[:, u * DV : (u + 1) * DV].bitcast(FP8X4),
-                    rhs_scale=v_plane[:, u * DV : (u + 1) * DV],
-                    start=(u == 0),
-                    stop=(u == PAGES - 1),
-                )
+        def weigh(u, h):
+            w = shared.tile([P, P, PACK], BF16, name="w%d%d" % (u, h), align_bytes=64, offset=(38 + 4 * u + 2 * h) * PAGE)
+            nc.vector.tensor_tensor(w[:], silu[(u, h)][:], vs_col[u].unsqueeze(1).to_broadcast([P, P, PACK]), ALU.mult)
+            return w
+
+        def accumulate(u, h, w):
+            w_codes = sb.tile([P, P], U32, name="w_codes%d%d" % (u, h), align_bytes=64)
+            w_plane = sb.tile([P, P], U8, name="w_plane%d%d" % (u, h), align_bytes=64)
+            nc.vector.quantize_mx(out=w_codes[:].bitcast(FP8X4), scales=w_plane[:], in_=w[:].rearrange("p q r -> p (q r)"))
+            nc.tensor.matmul_mx(
+                out=y[h][:],
+                lhsT=w_codes[:].bitcast(FP8X4),
+                lhsT_scale=w_plane[:],
+                rhs=v_g[:, u * DV : (u + 1) * DV].bitcast(FP8X4),
+                rhs_scale=v_plane[:, u * DV : (u + 1) * DV],
+                start=(u == 0),
+                stop=(u == PAGES - 1),
+            )
+
+        tiles = [(u, h) for u in range(PAGES) for h in range(Q_TILES)]
+        weights = [weigh(*tiles[0])]
+        v_g = shared.tile([P, PAGES * DV], U32, name="v_g", align_bytes=64, offset=80 * PAGE)
+        nc.vector.tensor_copy(v_g[:], v_pool[:].indirect(voffs_t[:]))
+        accumulate(*tiles[0], weights[0])
+        weights.append(weigh(*tiles[1]))
+        for i in range(1, len(tiles)):
+            if i + 1 < len(tiles):
+                weights.append(weigh(*tiles[i + 1]))
+            accumulate(*tiles[i], weights[i])
 
         for h in range(Q_TILES):
             res = sb.tile([P, DV], F32, name="res%d" % h)

@@ -102,7 +102,7 @@ def tile_attend_pkv4q_silu_gate_kernel(
 
         vsc_g = sb.tile([P, PAGES * DV], U8, name="vsc_g", align_bytes=64)
         nc.vector.tensor_copy(vsc_g[:], vsc_pool[:].indirect(voffs_t[:]))
-        ks_g = [shared.tile([P, PAGE], U8, name="ks_g%d" % u, align_bytes=64, offset=(30 + u) * PAGE) for u in range(PAGES)]
+        ks_g = [sb.tile([P, PAGE], U8, name="ks_g%d" % u, align_bytes=64) for u in range(PAGES)]
         for u in range(PAGES):
             nc.vector.tensor_copy(ks_g[u][:], ks_pool[:].indirect(offs_t[:, u * PAGE // 16 : (u + 1) * PAGE // 16]))
         for u in range(PAGES):
@@ -122,7 +122,7 @@ def tile_attend_pkv4q_silu_gate_kernel(
 
         move_scales(nc.sync, 0)
         move_scales(nc.sync, 1)
-        v_pool = shared.tile([P, POOL_PAGES * DV], U32, name="v_pool", align_bytes=64, offset=40 * PAGE)
+        v_pool = sb.tile([P, POOL_PAGES * DV], U32, name="v_pool", align_bytes=64)
         nc.sync.dma_start(
             out=v_pool[:].bitcast(I32).rearrange("p (u e) -> p u e", u=POOL_PAGES),
             in_=v_words.rearrange("u p e b -> p u (e b)").bitcast(I32),
@@ -143,23 +143,19 @@ def tile_attend_pkv4q_silu_gate_kernel(
             in_=turned[:, :, VS_ROW:P].rearrange("p r u -> p u r"),
             func=ACT.Copy,
         )
-        vs_g = [
-            sb.tile([P, PAGE + PACK], F32, name="vs_g0"),
-            sb.tile([P, PAGE + PACK], F32, name="vs_g1"),
-        ]
-
-        def gather_vs(u):
+        vs_col = []
+        for u in range(PAGES):
+            vs_g = sb.tile([P, PAGE + PACK], F32, name="vs_g%d" % u)
             for r in range(PACK):
                 first = (u * PAGE + r * P) // 16
                 nc.scalar.activation(
-                    out=vs_g[u][:, r * P : (r + 1) * P],
+                    out=vs_g[:, r * P : (r + 1) * P],
                     in_=vs_pool[:, VS_BASE - r * P : VS_BASE - r * P + T].indirect(offs_t[:, first : first + P // 16]),
                     func=ACT.Copy,
                 )
-
-        gather_vs(0)
-        gather_vs(1)
-        vs_col = [vs_g[u][:].rearrange("p (r j) -> p r j", r=PACK)[:, :, 0] for u in range(PAGES)]
+            col = sb.tile([P, PACK], F32, name="vs_col%d" % u)
+            nc.scalar.activation(out=col[:], in_=vs_g[:].rearrange("p (r j) -> p r j", r=PACK)[:, :, 0], func=ACT.Copy)
+            vs_col.append(col[:])
 
         k_codes = [shared.tile([P, PASSES * PAGE], U16, name="k_codes%d" % u, align_bytes=64, offset=(16 - 7 * u) * PAGE) for u in range(PAGES)]
 
@@ -179,7 +175,7 @@ def tile_attend_pkv4q_silu_gate_kernel(
         part_keys(0, 0, halves[0], 0, PASSES)
         part_keys(0, 1, halves[1], 0, 1)
         part_keys(0, 1, halves[1], 1, PASSES)
-        halves = [gather_keys(1, a, 5 + 2 * a) for a in range(2)]
+        halves = [gather_keys(1, a, 3 + 4 * a) for a in range(2)]
         for a in range(2):
             part_keys(1, a, halves[a], 0, PASSES)
 
@@ -208,7 +204,7 @@ def tile_attend_pkv4q_silu_gate_kernel(
         for u in range(PAGES):
             for h in range(Q_TILES):
                 scores = score_bank(u, h)
-                act = shared.tile([P, P, PACK], F32, name="silu%d%d" % (u, h), align_bytes=64, offset=(80 + 8 * u + 4 * h) * PAGE)
+                act = sb.tile([P, P, PACK], F32, name="silu%d%d" % (u, h))
                 nc.scalar.activation(out=act[:], in_=scores[:].rearrange("p r q -> p q r"), func=ACT.Silu)
                 silu[(u, h)] = act
 
@@ -218,14 +214,17 @@ def tile_attend_pkv4q_silu_gate_kernel(
         nc.scalar.activation(out=gate[:], in_=half[:], func=ACT.Copy, scale=1.0 / 32.0, bias=1.0 / 32.0)
 
         def weigh(u, h):
-            w = shared.tile([P, P, PACK], BF16, name="w%d%d" % (u, h), align_bytes=64, offset=(38 + 4 * u + 2 * h) * PAGE)
+            w = sb.tile([P, P, PACK], BF16, name="w%d%d" % (u, h), align_bytes=64)
             nc.vector.tensor_tensor(w[:], silu[(u, h)][:], vs_col[u].unsqueeze(1).to_broadcast([P, P, PACK]), ALU.mult)
             return w
 
-        def accumulate(u, h, w):
+        def quantise(u, h, w):
             w_codes = sb.tile([P, P], U32, name="w_codes%d%d" % (u, h), align_bytes=64)
             w_plane = sb.tile([P, P], U8, name="w_plane%d%d" % (u, h), align_bytes=64)
             nc.vector.quantize_mx(out=w_codes[:].bitcast(FP8X4), scales=w_plane[:], in_=w[:].rearrange("p q r -> p (q r)"))
+            return w_codes, w_plane
+
+        def accumulate(u, h, w_codes, w_plane):
             nc.tensor.matmul_mx(
                 out=y[h][:],
                 lhsT=w_codes[:].bitcast(FP8X4),
@@ -237,15 +236,16 @@ def tile_attend_pkv4q_silu_gate_kernel(
             )
 
         tiles = [(u, h) for u in range(PAGES) for h in range(Q_TILES)]
-        weights = [weigh(*tiles[0])]
-        v_g = shared.tile([P, PAGES * DV], U32, name="v_g", align_bytes=64, offset=80 * PAGE)
+        weights = weigh(*tiles[0])
+        v_g = sb.tile([P, PAGES * DV], U32, name="v_g", align_bytes=64)
         nc.vector.tensor_copy(v_g[:], v_pool[:].indirect(voffs_t[:]))
-        accumulate(*tiles[0], weights[0])
-        weights.append(weigh(*tiles[1]))
-        for i in range(1, len(tiles)):
-            if i + 1 < len(tiles):
-                weights.append(weigh(*tiles[i + 1]))
-            accumulate(*tiles[i], weights[i])
+        codes = []
+        for i in range(len(tiles)):
+            ahead = weigh(*tiles[i + 1]) if i + 1 < len(tiles) else None
+            codes.append(quantise(*tiles[i], weights))
+            weights = ahead
+        for tile, made in zip(tiles, codes):
+            accumulate(*tile, *made)
 
         for h in range(Q_TILES):
             res = sb.tile([P, DV], F32, name="res%d" % h)

@@ -63,8 +63,6 @@ def tile_attend_pkv4q_silu_gate_kernel(
             nc.vector.memset(words[:, 0:odd], 0)
             nc.vector.memset(words[:, odd:], 0)
 
-        one = sb.tile([P, 7], F32, name="one")
-        nc.vector.memset(one[:], 1.0)
         clear_odd(ks_pool[QUAD : 2 * QUAD, :].bitcast(I32))
         clear_odd(ks_pool[2 * QUAD : P, 0:KS_SPLIT].bitcast(I32))
 
@@ -97,8 +95,6 @@ def tile_attend_pkv4q_silu_gate_kernel(
             out=q_codes[:].bitcast(I32).rearrange("p (o q) -> p o q", o=PASSES),
             in_=q_words[0].rearrange("o p q b -> p o (q b)").bitcast(I32),
         )
-        table = sb.tile([P, 7], F32, name="table")
-        nc.scalar.activation(out=table[:], in_=one[:], func=ACT.Silu)
 
         vsc_g = sb.tile([P, PAGES * DV], U8, name="vsc_g", align_bytes=64)
         nc.vector.tensor_copy(vsc_g[:], vsc_pool[:].indirect(voffs_t[:]))

@@ -27,8 +27,9 @@ PAGES = N // PAGE
 POOL_PAGES = T // PAGE
 Q_TILES = NQ // P
 QUAD = 32
-SCALE_ROWS = PASSES * 16
-V_ROW = P - 16
+BLOCKS = 16
+SCALE_ROWS = PASSES * BLOCKS
+V_ROW = P - BLOCKS
 VS_ROW = P - POOL_PAGES
 VS_BASE = PAGE - P
 REGION = N + NQ
@@ -107,27 +108,22 @@ def tile_attend_pkv4q_silu_gate_kernel(
                 ks_g[u][:].rearrange("p (s r) -> p r s", r=PACK),
             )
 
-        def move_scales(queue, o):
-            for g in range(PACK):
-                row = 16 * o + PACK * g
-                if row:
-                    queue.dma_start(
-                        out=planes[QUAD * g : QUAD * g + PACK, o * REGION : (o + 1) * REGION].bitcast(I32),
-                        in_=planes[row : row + PACK, 0:REGION].bitcast(I32),
-                    )
+        def move_rows(plane, rows, first):
+            for j in range(PACK):
+                nc.sync.dma_start(out=plane[j:P:QUAD, :].bitcast(I32), in_=rows[first + j : first + BLOCKS : PACK, :].bitcast(I32))
 
-        move_scales(nc.sync, 0)
-        move_scales(nc.sync, 1)
+        for g in range(1, PACK):
+            nc.sync.dma_start(
+                out=planes[QUAD * g : QUAD * g + PACK, 0:REGION].bitcast(I32),
+                in_=planes[PACK * g : PACK * (g + 1), 0:REGION].bitcast(I32),
+            )
+        move_rows(planes[:, REGION:], planes[:, 0:REGION], BLOCKS)
         v_pool = sb.tile([P, POOL_PAGES * DV], U32, name="v_pool", align_bytes=64)
         nc.sync.dma_start(
             out=v_pool[:].bitcast(I32).rearrange("p (u e) -> p u e", u=POOL_PAGES),
             in_=v_words.rearrange("u p e b -> p u (e b)").bitcast(I32),
         )
-        for g in range(PACK):
-            nc.sync.dma_start(
-                out=v_plane[QUAD * g : QUAD * g + PACK, :].bitcast(I32),
-                in_=vsc_g[V_ROW + PACK * g : V_ROW + PACK * (g + 1), :].bitcast(I32),
-            )
+        move_rows(v_plane[:], vsc_g[:], V_ROW)
         og_t = sb.tile([P, Q_TILES, DV], F32, name="og_t")
         nc.sync.dma_start(out=og_t[:], in_=og[0].rearrange("(h p) e -> p h e", p=P))
 
@@ -168,9 +164,9 @@ def tile_attend_pkv4q_silu_gate_kernel(
             )
 
         halves = [gather_keys(0, a, 2 + 4 * a) for a in range(2)]
-        part_keys(0, 0, halves[0], 0, PASSES)
-        part_keys(0, 1, halves[1], 0, 1)
-        part_keys(0, 1, halves[1], 1, PASSES)
+        for o in range(PASSES):
+            for a in range(2):
+                part_keys(0, a, halves[a], o, o + 1)
         halves = [gather_keys(1, a, 3 + 4 * a) for a in range(2)]
         for a in range(2):
             part_keys(1, a, halves[a], 0, PASSES)
@@ -209,9 +205,9 @@ def tile_attend_pkv4q_silu_gate_kernel(
         nc.scalar.activation(out=half[:], in_=og_t[:], func=ACT.Tanh, scale=0.5)
         nc.scalar.activation(out=gate[:], in_=half[:], func=ACT.Copy, scale=1.0 / 32.0, bias=1.0 / 32.0)
 
-        def weigh(u, h):
+        def weigh(engine, u, h):
             w = sb.tile([P, P, PACK], BF16, name="w%d%d" % (u, h), align_bytes=64)
-            nc.vector.tensor_tensor(w[:], silu[(u, h)][:], vs_col[u].unsqueeze(1).to_broadcast([P, P, PACK]), ALU.mult)
+            engine.tensor_tensor(w[:], silu[(u, h)][:], vs_col[u].unsqueeze(1).to_broadcast([P, P, PACK]), ALU.mult)
             return w
 
         def quantise(u, h, w):
@@ -232,12 +228,12 @@ def tile_attend_pkv4q_silu_gate_kernel(
             )
 
         tiles = [(u, h) for u in range(PAGES) for h in range(Q_TILES)]
-        weights = weigh(*tiles[0])
+        weights = weigh(nc.gpsimd, *tiles[0])
         v_g = sb.tile([P, PAGES * DV], U32, name="v_g", align_bytes=64)
         nc.vector.tensor_copy(v_g[:], v_pool[:].indirect(voffs_t[:]))
         codes = []
         for i in range(len(tiles)):
-            ahead = weigh(*tiles[i + 1]) if i + 1 < len(tiles) else None
+            ahead = weigh(nc.vector, *tiles[i + 1]) if i + 1 < len(tiles) else None
             codes.append(quantise(*tiles[i], weights))
             weights = ahead
         for tile, made in zip(tiles, codes):

@@ -228,7 +228,7 @@ def tile_attend_pkv4q_silu_gate_kernel(
             )
 
         tiles = [(u, h) for u in range(PAGES) for h in range(Q_TILES)]
-        weights = weigh(nc.gpsimd, *tiles[0])
+        weights = weigh(nc.vector, *tiles[0])
         v_g = sb.tile([P, PAGES * DV], U32, name="v_g", align_bytes=64)
         nc.vector.tensor_copy(v_g[:], v_pool[:].indirect(voffs_t[:]))
         codes = []

@@ -112,12 +112,12 @@ def tile_attend_pkv4q_silu_gate_kernel(
             for j in range(PACK):
                 nc.sync.dma_start(out=plane[j:P:QUAD, :].bitcast(I32), in_=rows[first + j : first + BLOCKS : PACK, :].bitcast(I32))
 
+        move_rows(planes[:, REGION:], planes[:, 0:REGION], BLOCKS)
         for g in range(1, PACK):
             nc.sync.dma_start(
                 out=planes[QUAD * g : QUAD * g + PACK, 0:REGION].bitcast(I32),
                 in_=planes[PACK * g : PACK * (g + 1), 0:REGION].bitcast(I32),
             )
-        move_rows(planes[:, REGION:], planes[:, 0:REGION], BLOCKS)
         v_pool = sb.tile([P, POOL_PAGES * DV], U32, name="v_pool", align_bytes=64)
         nc.sync.dma_start(
             out=v_pool[:].bitcast(I32).rearrange("p (u e) -> p u e", u=POOL_PAGES),
@@ -157,25 +157,27 @@ def tile_attend_pkv4q_silu_gate_kernel(
             nc.vector.tensor_copy(part[:], k_pool[:].indirect(offs_t[:, first : first + HALF // 16]))
             return part
 
-        def part_keys(u, a, part, first, last):
+        def part_keys(u, a, part, passes, places=slice(0, PACK)):
             nc.vector.tensor_copy(
-                k_codes[u][:].rearrange("p (o r s) -> p o s r", o=PASSES, r=PACK)[:, first:last, a * HALF // PACK : (a + 1) * HALF // PACK, :],
-                part[:].bitcast(U16).rearrange("p (s r o) -> p o s r", o=PASSES, r=PACK)[:, first:last],
+                k_codes[u][:].rearrange("p (o r s) -> p o s r", o=PASSES, r=PACK)[:, passes, a * HALF // PACK : (a + 1) * HALF // PACK, places],
+                part[:].bitcast(U16).rearrange("p (s r o) -> p o s r", o=PASSES, r=PACK)[:, passes, :, places],
             )
 
         halves = [gather_keys(0, a, 2 + 4 * a) for a in range(2)]
-        for o in range(PASSES):
-            for a in range(2):
-                part_keys(0, a, halves[a], o, o + 1)
+        part_keys(0, 0, halves[0], slice(1, 2))
+        part_keys(0, 1, halves[1], slice(1, 2), slice(0, 2))
+        part_keys(0, 1, halves[1], slice(1, 2), slice(2, 4))
+        for a in range(2):
+            part_keys(0, a, halves[a], slice(0, 1))
         halves = [gather_keys(1, a, 3 + 4 * a) for a in range(2)]
         for a in range(2):
-            part_keys(1, a, halves[a], 0, PASSES)
+            part_keys(1, a, halves[a], slice(0, PASSES))
 
         y = [ps.tile([P, DV], F32, name="y%d" % h, tag="y%d" % h) for h in range(Q_TILES)]
 
         def score_bank(u, h):
             scores = ps.tile([P, PACK, P], F32, name="scores%d%d" % (u, h))
-            order = (0, 1) if (u, h) == (0, 0) else (1, 0)
+            order = (1, 0) if (u, h) == (0, 0) else (0, 1)
             for o in order:
                 for r in range(PACK):
                     k0 = o * PAGE + r * P
@@ -231,8 +233,9 @@ def tile_attend_pkv4q_silu_gate_kernel(
         weights = weigh(nc.vector, *tiles[0])
         v_g = sb.tile([P, PAGES * DV], U32, name="v_g", align_bytes=64)
         nc.vector.tensor_copy(v_g[:], v_pool[:].indirect(voffs_t[:]))
-        codes = []
-        for i in range(len(tiles)):
+        codes = [quantise(*tiles[0], weights)]
+        weights = weigh(nc.vector, *tiles[1])
+        for i in range(1, len(tiles)):
             ahead = weigh(nc.vector, *tiles[i + 1]) if i + 1 < len(tiles) else None
             codes.append(quantise(*tiles[i], weights))
             weights = ahead

@@ -34,6 +34,7 @@ VS_ROW = P - POOL_PAGES
 VS_BASE = PAGE - P
 REGION = N + NQ
 KS_SPLIT = 5 * T // 8
+Q_PARTS = (slice(0, P // 2), slice(P // 2, P))
 
 FLOPS = 2 * NQ * N * (PASSES * PAGE + DV)
 
@@ -199,7 +200,8 @@ def tile_attend_pkv4q_silu_gate_kernel(
             for h in range(Q_TILES):
                 scores = score_bank(u, h)
                 act = sb.tile([P, P, PACK], F32, name="silu%d%d" % (u, h))
-                nc.scalar.activation(out=act[:], in_=scores[:].rearrange("p r q -> p q r"), func=ACT.Silu)
+                for part in Q_PARTS:
+                    nc.scalar.activation(out=act[:, part, :], in_=scores[:].rearrange("p r q -> p q r")[:, part, :], func=ACT.Silu)
                 silu[(u, h)] = act
 
         half = shared.tile([P, Q_TILES, DV], F32, name="half", align_bytes=64, offset=11 * PAGE)
@@ -209,7 +211,8 @@ def tile_attend_pkv4q_silu_gate_kernel(
 
         def weigh(engine, u, h):
             w = sb.tile([P, P, PACK], BF16, name="w%d%d" % (u, h), align_bytes=64)
-            engine.tensor_tensor(w[:], silu[(u, h)][:], vs_col[u].unsqueeze(1).to_broadcast([P, P, PACK]), ALU.mult)
+            for part in Q_PARTS:
+                engine.tensor_tensor(w[:, part, :], silu[(u, h)][:, part, :], vs_col[u].unsqueeze(1).to_broadcast([P, P // 2, PACK]), ALU.mult)
             return w
 
         def quantise(u, h, w):

@@ -34,6 +34,7 @@ VS_ROW = P - POOL_PAGES
 VS_BASE = PAGE - P
 REGION = N + NQ
 KS_SPLIT = 5 * T // 8
+WARM_WIDTHS = (256, 128, 64)
 Q_PARTS = (slice(0, P // 2), slice(P // 2, P))
 
 FLOPS = 2 * NQ * N * (PASSES * PAGE + DV)
@@ -51,12 +52,11 @@ def tile_attend_pkv4q_silu_gate_kernel(
         offs_t = sb.tile([P, N // 16], U16, name="offs_t")
         voffs_t = sb.tile([P, PAGES * DV // 16], U16, name="voffs_t")
         k_pool = sb.tile([P, T], U32, name="k_pool", align_bytes=64)
-        ks_pool = sb.tile([P, T], U8, name="ks_pool", align_bytes=64)
-        planes = sb.tile([P, PASSES * REGION], U8, name="planes", align_bytes=64)
+        ks_pool = shared.tile([P, T], U8, name="ks_pool", align_bytes=64, offset=32 * PAGE)
+        staged = sb.tile([P, REGION], U8, name="staged", align_bytes=64)
         vsc_pool = sb.tile([P, POOL_PAGES * DV], U8, name="vsc_pool", align_bytes=64)
-        v_plane = sb.tile([P, PAGES * DV], U8, name="v_plane", align_bytes=64)
         q_codes = sb.tile([P, PASSES * NQ], U32, name="q_codes", align_bytes=64)
-        vs_rows = sb.tile([P, PAGE], F32, name="vs_rows")
+        vs_rows = shared.tile([P, PAGE], F32, name="vs_rows", align_bytes=64, offset=3 * PAGE)
         vs_pool = sb.tile([P, VS_BASE + T], F32, name="vs_pool", align_bytes=64)
         ident = sb.tile([P, P], F32, name="ident")
 
@@ -72,13 +72,11 @@ def tile_attend_pkv4q_silu_gate_kernel(
         nc.gpsimd.memset(vsc_pool[0:V_ROW, :].bitcast(I32), 0)
         nc.gpsimd.memset(ks_pool[2 * QUAD : P, KS_SPLIT:].bitcast(I32), 0)
         for first, last in ((QUAD, 2 * QUAD), (2 * QUAD, P)):
-            nc.gpsimd.memset(planes[first:last, N:REGION].bitcast(I32), 0)
-        nc.gpsimd.memset(planes[:, REGION:].bitcast(I32), 0)
+            nc.gpsimd.memset(staged[first:last, N:REGION].bitcast(I32), 0)
         nc.gpsimd.memset(ident[:], 0.0)
         nc.gpsimd.memset(vs_rows[0:VS_ROW, :], 0.0)
         make_identity(nc, ident[:], nomemset=True)
         nc.gpsimd.memset(vs_pages[:, :, PACK:P], 0.0)
-        nc.gpsimd.memset(v_plane[:].bitcast(I32), 0)
 
         nc.sync.dma_start(voffs_t[:], voffs)
         nc.sync.dma_start(offs_t[:], offs)
@@ -88,7 +86,7 @@ def tile_attend_pkv4q_silu_gate_kernel(
             in_=v_scales.rearrange("u f e -> f u e").bitcast(I32),
         )
         nc.scalar.dma_start(
-            out=planes[0:SCALE_ROWS, N:REGION].bitcast(I32),
+            out=staged[0:SCALE_ROWS, N:REGION].bitcast(I32),
             in_=q_scales[0].rearrange("o f q -> (o f) q").bitcast(I32),
         )
         nc.scalar.dma_start(out=vs_rows[VS_ROW:P, :], in_=vs[0].rearrange("(u j) -> u j", u=POOL_PAGES))
@@ -105,7 +103,7 @@ def tile_attend_pkv4q_silu_gate_kernel(
             nc.vector.tensor_copy(ks_g[u][:], ks_pool[:].indirect(offs_t[:, u * PAGE // 16 : (u + 1) * PAGE // 16]))
         for u in range(PAGES):
             nc.vector.tensor_copy(
-                planes[:, u * PAGE : (u + 1) * PAGE].rearrange("p (r s) -> p r s", r=PACK),
+                staged[:, u * PAGE : (u + 1) * PAGE].rearrange("p (r s) -> p r s", r=PACK),
                 ks_g[u][:].rearrange("p (s r) -> p r s", r=PACK),
             )
 
@@ -113,17 +111,19 @@ def tile_attend_pkv4q_silu_gate_kernel(
             for j in range(PACK):
                 nc.sync.dma_start(out=plane[j:P:QUAD, :].bitcast(I32), in_=rows[first + j : first + BLOCKS : PACK, :].bitcast(I32))
 
-        move_rows(planes[:, REGION:], planes[:, 0:REGION], BLOCKS)
+        planes = [staged, shared.tile([P, REGION], U8, name="plane1", align_bytes=64, offset=32 * PAGE)]
+        move_rows(planes[1][:], staged[:], BLOCKS)
         for g in range(1, PACK):
             nc.sync.dma_start(
-                out=planes[QUAD * g : QUAD * g + PACK, 0:REGION].bitcast(I32),
-                in_=planes[PACK * g : PACK * (g + 1), 0:REGION].bitcast(I32),
+                out=staged[QUAD * g : QUAD * g + PACK, :].bitcast(I32),
+                in_=staged[PACK * g : PACK * (g + 1), :].bitcast(I32),
             )
         v_pool = sb.tile([P, POOL_PAGES * DV], U32, name="v_pool", align_bytes=64)
         nc.sync.dma_start(
             out=v_pool[:].bitcast(I32).rearrange("p (u e) -> p u e", u=POOL_PAGES),
             in_=v_words.rearrange("u p e b -> p u (e b)").bitcast(I32),
         )
+        v_plane = shared.tile([P, PAGES * DV], U8, name="v_plane", align_bytes=64, offset=36 * PAGE)
         move_rows(v_plane[:], vsc_g[:], V_ROW)
         og_t = sb.tile([P, Q_TILES, DV], F32, name="og_t")
         nc.sync.dma_start(out=og_t[:], in_=og[0].rearrange("(h p) e -> p h e", p=P))
@@ -165,6 +165,19 @@ def tile_attend_pkv4q_silu_gate_kernel(
             )
 
         halves = [gather_keys(0, a, 2 + 4 * a) for a in range(2)]
+        warm = ps.tile([P, PAGE], F32, name="warm")
+        first = 0
+        for width in WARM_WIDTHS:
+            nc.tensor.matmul_mx(
+                out=warm[:, first : first + width],
+                lhsT=q_codes[:, 0:P].bitcast(FP8X4),
+                lhsT_scale=ks_g[0][:, 0:P],
+                rhs=halves[0][:].bitcast(U16)[:, 0:width].bitcast(FP4X4),
+                rhs_scale=ks_g[0][:, 0:width],
+                start=True,
+                stop=True,
+            )
+            first = first + width
         part_keys(0, 0, halves[0], slice(1, 2))
         part_keys(0, 1, halves[1], slice(1, 2), slice(0, 2))
         part_keys(0, 1, halves[1], slice(1, 2), slice(2, 4))
@@ -182,14 +195,14 @@ def tile_attend_pkv4q_silu_gate_kernel(
             for o in order:
                 for r in range(PACK):
                     k0 = o * PAGE + r * P
-                    s0 = o * REGION + u * PAGE + r * P
-                    q0 = o * REGION + N + h * P
+                    s0 = u * PAGE + r * P
+                    q0 = N + h * P
                     nc.tensor.matmul_mx(
                         out=scores[:, r, :],
                         lhsT=k_codes[u][:, k0 : k0 + P].bitcast(FP4X4),
-                        lhsT_scale=planes[:, s0 : s0 + P],
+                        lhsT_scale=planes[o][:, s0 : s0 + P],
                         rhs=q_codes[:, o * NQ + h * P : o * NQ + (h + 1) * P].bitcast(FP8X4),
-                        rhs_scale=planes[:, q0 : q0 + P],
+                        rhs_scale=planes[o][:, q0 : q0 + P],
                         start=(o == order[0] and r == 0),
                         stop=(o == order[1] and r == PACK - 1),
                     )

@@ -35,6 +35,7 @@ VS_BASE = PAGE - P
 REGION = N + NQ
 KS_SPLIT = 5 * T // 8
 WARM_WIDTHS = (256, 128, 64)
+WARM_PAD = 64
 Q_PARTS = (slice(0, P // 2), slice(P // 2, P))
 
 FLOPS = 2 * NQ * N * (PASSES * PAGE + DV)
@@ -56,7 +57,7 @@ def tile_attend_pkv4q_silu_gate_kernel(
         staged = sb.tile([P, REGION], U8, name="staged", align_bytes=64)
         vsc_pool = sb.tile([P, POOL_PAGES * DV], U8, name="vsc_pool", align_bytes=64)
         q_codes = sb.tile([P, PASSES * NQ], U32, name="q_codes", align_bytes=64)
-        vs_rows = shared.tile([P, PAGE], F32, name="vs_rows", align_bytes=64, offset=3 * PAGE)
+        vs_rows = sb.tile([P, PAGE], F32, name="vs_rows")
         vs_pool = sb.tile([P, VS_BASE + T], F32, name="vs_pool", align_bytes=64)
         ident = sb.tile([P, P], F32, name="ident")
 
@@ -76,6 +77,8 @@ def tile_attend_pkv4q_silu_gate_kernel(
         nc.gpsimd.memset(ident[:], 0.0)
         nc.gpsimd.memset(vs_rows[0:VS_ROW, :], 0.0)
         make_identity(nc, ident[:], nomemset=True)
+        ks_g = [sb.tile([P, PAGE + (1 - u) * WARM_PAD], U8, name="ks_g%d" % u, align_bytes=64) for u in range(PAGES)]
+        nc.gpsimd.memset(ks_g[0][:, PAGE:].bitcast(I32), 0)
         nc.gpsimd.memset(vs_pages[:, :, PACK:P], 0.0)
 
         nc.sync.dma_start(voffs_t[:], voffs)
@@ -98,13 +101,12 @@ def tile_attend_pkv4q_silu_gate_kernel(
 
         vsc_g = sb.tile([P, PAGES * DV], U8, name="vsc_g", align_bytes=64)
         nc.vector.tensor_copy(vsc_g[:], vsc_pool[:].indirect(voffs_t[:]))
-        ks_g = [sb.tile([P, PAGE], U8, name="ks_g%d" % u, align_bytes=64) for u in range(PAGES)]
         for u in range(PAGES):
-            nc.vector.tensor_copy(ks_g[u][:], ks_pool[:].indirect(offs_t[:, u * PAGE // 16 : (u + 1) * PAGE // 16]))
+            nc.vector.tensor_copy(ks_g[u][:, 0:PAGE], ks_pool[:].indirect(offs_t[:, u * PAGE // 16 : (u + 1) * PAGE // 16]))
         for u in range(PAGES):
             nc.vector.tensor_copy(
                 staged[:, u * PAGE : (u + 1) * PAGE].rearrange("p (r s) -> p r s", r=PACK),
-                ks_g[u][:].rearrange("p (s r) -> p r s", r=PACK),
+                ks_g[u][:, 0:PAGE].rearrange("p (s r) -> p r s", r=PACK),
             )
 
         def move_rows(plane, rows, first):
@@ -171,7 +173,7 @@ def tile_attend_pkv4q_silu_gate_kernel(
             nc.tensor.matmul_mx(
                 out=warm[:, first : first + width],
                 lhsT=q_codes[:, 0:P].bitcast(FP8X4),
-                lhsT_scale=ks_g[0][:, 0:P],
+                lhsT_scale=ks_g[0][:, PAGE + WARM_PAD - P :],
                 rhs=halves[0][:].bitcast(U16)[:, 0:width].bitcast(FP4X4),
                 rhs_scale=ks_g[0][:, 0:width],
                 start=True,
@@ -181,9 +183,9 @@ def tile_attend_pkv4q_silu_gate_kernel(
         part_keys(0, 0, halves[0], slice(1, 2))
         part_keys(0, 1, halves[1], slice(1, 2), slice(0, 2))
         part_keys(0, 1, halves[1], slice(1, 2), slice(2, 4))
-        for a in range(2):
+        for a in (1, 0):
             part_keys(0, a, halves[a], slice(0, 1))
-        halves = [gather_keys(1, a, 3 + 4 * a) for a in range(2)]
+        halves = [gather_keys(1, a, 5 + 2 * a) for a in range(2)]
         for a in range(2):
             part_keys(1, a, halves[a], slice(0, PASSES))
 

@@ -35,7 +35,6 @@ VS_BASE = PAGE - P
 REGION = N + NQ
 KS_SPLIT = 5 * T // 8
 WARM_WIDTHS = (256, 128, 64)
-WARM_PAD = 64
 Q_PARTS = (slice(0, P // 2), slice(P // 2, P))
 
 FLOPS = 2 * NQ * N * (PASSES * PAGE + DV)
@@ -77,9 +76,6 @@ def tile_attend_pkv4q_silu_gate_kernel(
         nc.gpsimd.memset(ident[:], 0.0)
         nc.gpsimd.memset(vs_rows[0:VS_ROW, :], 0.0)
         make_identity(nc, ident[:], nomemset=True)
-        ks_g = [sb.tile([P, PAGE + (1 - u) * WARM_PAD], U8, name="ks_g%d" % u, align_bytes=64) for u in range(PAGES)]
-        nc.gpsimd.memset(ks_g[0][:, PAGE:].bitcast(I32), 0)
-        nc.gpsimd.memset(vs_pages[:, :, PACK:P], 0.0)
 
         nc.sync.dma_start(voffs_t[:], voffs)
         nc.sync.dma_start(offs_t[:], offs)
@@ -92,6 +88,9 @@ def tile_attend_pkv4q_silu_gate_kernel(
             out=staged[0:SCALE_ROWS, N:REGION].bitcast(I32),
             in_=q_scales[0].rearrange("o f q -> (o f) q").bitcast(I32),
         )
+        warm_plane = sb.tile([P, P], U8, name="warm_plane", align_bytes=64)
+        nc.gpsimd.tensor_copy(warm_plane[:].bitcast(I32), staged[:, N : N + P].bitcast(I32))
+        nc.gpsimd.memset(vs_pages[:, :, PACK:P], 0.0)
         nc.scalar.dma_start(out=vs_rows[VS_ROW:P, :], in_=vs[0].rearrange("(u j) -> u j", u=POOL_PAGES))
         nc.sync.dma_start(out=k_pool[:].bitcast(I32), in_=k_words[0].rearrange("p t b -> p (t b)").bitcast(I32))
         nc.sync.dma_start(
@@ -101,12 +100,13 @@ def tile_attend_pkv4q_silu_gate_kernel(
 
         vsc_g = sb.tile([P, PAGES * DV], U8, name="vsc_g", align_bytes=64)
         nc.vector.tensor_copy(vsc_g[:], vsc_pool[:].indirect(voffs_t[:]))
+        ks_g = [sb.tile([P, PAGE], U8, name="ks_g%d" % u, align_bytes=64) for u in range(PAGES)]
         for u in range(PAGES):
-            nc.vector.tensor_copy(ks_g[u][:, 0:PAGE], ks_pool[:].indirect(offs_t[:, u * PAGE // 16 : (u + 1) * PAGE // 16]))
+            nc.vector.tensor_copy(ks_g[u][:], ks_pool[:].indirect(offs_t[:, u * PAGE // 16 : (u + 1) * PAGE // 16]))
         for u in range(PAGES):
             nc.vector.tensor_copy(
                 staged[:, u * PAGE : (u + 1) * PAGE].rearrange("p (r s) -> p r s", r=PACK),
-                ks_g[u][:, 0:PAGE].rearrange("p (s r) -> p r s", r=PACK),
+                ks_g[u][:].rearrange("p (s r) -> p r s", r=PACK),
             )
 
         def move_rows(plane, rows, first):
@@ -173,7 +173,7 @@ def tile_attend_pkv4q_silu_gate_kernel(
             nc.tensor.matmul_mx(
                 out=warm[:, first : first + width],
                 lhsT=q_codes[:, 0:P].bitcast(FP8X4),
-                lhsT_scale=ks_g[0][:, PAGE + WARM_PAD - P :],
+                lhsT_scale=warm_plane[:],
                 rhs=halves[0][:].bitcast(U16)[:, 0:width].bitcast(FP4X4),
                 rhs_scale=ks_g[0][:, 0:width],
                 start=True,

from contextlib import ExitStack

import concourse.mybir as mybir
from concourse.masks import make_identity

F32 = mybir.dt.float32
BF16 = mybir.dt.bfloat16
I32 = mybir.dt.int32
U32 = mybir.dt.uint32
U16 = mybir.dt.uint16
U8 = mybir.dt.uint8
FP8X4 = mybir.dt.float8_e4m3fn_x4
FP4X4 = mybir.dt.float4_e2m1fn_x4
ACT = mybir.ActivationFunctionType
ALU = mybir.AluOpType

P = 128
PACK = 4
PAGE = P * PACK
HALF = PAGE // 2
T = 4096
N = 1024
NQ = 256
DV = 128
PASSES = 2
PAGES = N // PAGE
POOL_PAGES = T // PAGE
Q_TILES = NQ // P
QUAD = 32
BLOCKS = 16
SCALE_ROWS = PASSES * BLOCKS
V_ROW = P - BLOCKS
VS_ROW = P - POOL_PAGES
VS_BASE = PAGE - P
REGION = N + NQ
KS_SPLIT = 5 * T // 8
WARM_WIDTHS = (256, 128, 64)
Q_PARTS = (slice(0, P // 2), slice(P // 2, P))

FLOPS = 2 * NQ * N * (PASSES * PAGE + DV)


def tile_attend_pkv4q_silu_gate_kernel(
    tc, q_words, q_scales, k_words, k_scales, v_words, v_scales, vs, og, offs, voffs, out
):
    nc = tc.nc
    with ExitStack() as ctx:
        sb = ctx.enter_context(tc.tile_pool(name="sb", bufs=1))
        shared = ctx.enter_context(tc.tile_pool(name="shared", bufs=1))
        ps = ctx.enter_context(tc.psum_pool(name="ps", bufs=1))

        offs_t = sb.tile([P, N // 16], U16, name="offs_t")
        voffs_t = sb.tile([P, PAGES * DV // 16], U16, name="voffs_t")
        k_pool = sb.tile([P, T], U32, name="k_pool", align_bytes=64)
        ks_pool = shared.tile([P, T], U8, name="ks_pool", align_bytes=64, offset=32 * PAGE)
        staged = sb.tile([P, REGION], U8, name="staged", align_bytes=64)
        vsc_pool = sb.tile([P, POOL_PAGES * DV], U8, name="vsc_pool", align_bytes=64)
        q_codes = sb.tile([P, PASSES * NQ], U32, name="q_codes", align_bytes=64)
        vs_rows = sb.tile([P, PAGE], F32, name="vs_rows")
        vs_pool = sb.tile([P, VS_BASE + T], F32, name="vs_pool", align_bytes=64)
        ident = sb.tile([P, P], F32, name="ident")

        def clear_odd(words):
            odd = words.shape[1] // 2 + 1
            nc.vector.memset(words[:, 0:odd], 0)
            nc.vector.memset(words[:, odd:], 0)

        clear_odd(ks_pool[QUAD : 2 * QUAD, :].bitcast(I32))
        clear_odd(ks_pool[2 * QUAD : P, 0:KS_SPLIT].bitcast(I32))

        vs_pages = vs_pool[:, VS_BASE:].rearrange("p (u j) -> p u j", u=POOL_PAGES)
        nc.gpsimd.memset(vsc_pool[0:V_ROW, :].bitcast(I32), 0)
        nc.gpsimd.memset(ks_pool[2 * QUAD : P, KS_SPLIT:].bitcast(I32), 0)
        for first, last in ((QUAD, 2 * QUAD), (2 * QUAD, P)):
            nc.gpsimd.memset(staged[first:last, N:REGION].bitcast(I32), 0)
        nc.gpsimd.memset(ident[:], 0.0)
        nc.gpsimd.memset(vs_rows[0:VS_ROW, :], 0.0)
        make_identity(nc, ident[:], nomemset=True)

        nc.sync.dma_start(voffs_t[:], voffs)
        nc.sync.dma_start(offs_t[:], offs)
        nc.sync.dma_start(out=ks_pool[0:SCALE_ROWS, :].bitcast(I32), in_=k_scales.rearrange("o f t -> (o f) t").bitcast(I32))
        nc.scalar.dma_start(
            out=vsc_pool[V_ROW:P, :].bitcast(I32).rearrange("f (u e) -> f u e", u=POOL_PAGES),
            in_=v_scales.rearrange("u f e -> f u e").bitcast(I32),
        )
        nc.scalar.dma_start(
            out=staged[0:SCALE_ROWS, N:REGION].bitcast(I32),
            in_=q_scales[0].rearrange("o f q -> (o f) q").bitcast(I32),
        )
        warm_plane = sb.tile([P, P], U8, name="warm_plane", align_bytes=64)
        nc.gpsimd.tensor_copy(warm_plane[:].bitcast(I32), staged[:, N : N + P].bitcast(I32))
        nc.gpsimd.memset(vs_pages[:, :, PACK:P], 0.0)
        nc.scalar.dma_start(out=vs_rows[VS_ROW:P, :], in_=vs[0].rearrange("(u j) -> u j", u=POOL_PAGES))
        nc.sync.dma_start(out=k_pool[:].bitcast(I32), in_=k_words[0].rearrange("p t b -> p (t b)").bitcast(I32))
        nc.sync.dma_start(
            out=q_codes[:].bitcast(I32).rearrange("p (o q) -> p o q", o=PASSES),
            in_=q_words[0].rearrange("o p q b -> p o (q b)").bitcast(I32),
        )

        vsc_g = sb.tile([P, PAGES * DV], U8, name="vsc_g", align_bytes=64)
        nc.vector.tensor_copy(vsc_g[:], vsc_pool[:].indirect(voffs_t[:]))
        ks_g = [sb.tile([P, PAGE], U8, name="ks_g%d" % u, align_bytes=64) for u in range(PAGES)]
        for u in range(PAGES):
            nc.vector.tensor_copy(ks_g[u][:], ks_pool[:].indirect(offs_t[:, u * PAGE // 16 : (u + 1) * PAGE // 16]))
        for u in range(PAGES):
            nc.vector.tensor_copy(
                staged[:, u * PAGE : (u + 1) * PAGE].rearrange("p (r s) -> p r s", r=PACK),
                ks_g[u][:].rearrange("p (s r) -> p r s", r=PACK),
            )

        def move_rows(plane, rows, first):
            for j in range(PACK):
                nc.sync.dma_start(out=plane[j:P:QUAD, :].bitcast(I32), in_=rows[first + j : first + BLOCKS : PACK, :].bitcast(I32))

        planes = [staged, shared.tile([P, REGION], U8, name="plane1", align_bytes=64, offset=32 * PAGE)]
        move_rows(planes[1][:], staged[:], BLOCKS)
        for g in range(1, PACK):
            nc.sync.dma_start(
                out=staged[QUAD * g : QUAD * g + PACK, :].bitcast(I32),
                in_=staged[PACK * g : PACK * (g + 1), :].bitcast(I32),
            )
        v_pool = sb.tile([P, POOL_PAGES * DV], U32, name="v_pool", align_bytes=64)
        nc.sync.dma_start(
            out=v_pool[:].bitcast(I32).rearrange("p (u e) -> p u e", u=POOL_PAGES),
            in_=v_words.rearrange("u p e b -> p u (e b)").bitcast(I32),
        )
        v_plane = shared.tile([P, PAGES * DV], U8, name="v_plane", align_bytes=64, offset=36 * PAGE)
        move_rows(v_plane[:], vsc_g[:], V_ROW)
        og_t = sb.tile([P, Q_TILES, DV], F32, name="og_t")
        nc.sync.dma_start(out=og_t[:], in_=og[0].rearrange("(h p) e -> p h e", p=P))

        turned = ps.tile([P, PACK, P], F32, name="turned")
        for r in range(PACK):
            nc.tensor.transpose(turned[:, r, :], vs_rows[:, r:PAGE:PACK], ident[:])
        nc.scalar.activation(
            out=vs_pages[:, :, 0:PACK],
            in_=turned[:, :, VS_ROW:P].rearrange("p r u -> p u r"),
            func=ACT.Copy,
        )
        vs_col = []
        for u in range(PAGES):
            vs_g = sb.tile([P, PAGE + PACK], F32, name="vs_g%d" % u)
            for r in range(PACK):
                first = (u * PAGE + r * P) // 16
                nc.scalar.activation(
                    out=vs_g[:, r * P : (r + 1) * P],
                    in_=vs_pool[:, VS_BASE - r * P : VS_BASE - r * P + T].indirect(offs_t[:, first : first + P // 16]),
                    func=ACT.Copy,
                )
            col = sb.tile([P, PACK], F32, name="vs_col%d" % u)
            nc.scalar.activation(out=col[:], in_=vs_g[:].rearrange("p (r j) -> p r j", r=PACK)[:, :, 0], func=ACT.Copy)
            vs_col.append(col[:])

        k_codes = [shared.tile([P, PASSES * PAGE], U16, name="k_codes%d" % u, align_bytes=64, offset=(16 - 7 * u) * PAGE) for u in range(PAGES)]

        def gather_keys(u, a, place):
            part = shared.tile([P, HALF], U32, name="k_g%d%d" % (u, a), align_bytes=64, offset=place * PAGE)
            first = (u * PAGE + a * HALF) // 16
            nc.vector.tensor_copy(part[:], k_pool[:].indirect(offs_t[:, first : first + HALF // 16]))
            return part

        def part_keys(u, a, part, passes, places=slice(0, PACK)):
            nc.vector.tensor_copy(
                k_codes[u][:].rearrange("p (o r s) -> p o s r", o=PASSES, r=PACK)[:, passes, a * HALF // PACK : (a + 1) * HALF // PACK, places],
                part[:].bitcast(U16).rearrange("p (s r o) -> p o s r", o=PASSES, r=PACK)[:, passes, :, places],
            )

        halves = [gather_keys(0, a, 2 + 4 * a) for a in range(2)]
        warm = ps.tile([P, PAGE], F32, name="warm")
        first = 0
        for width in WARM_WIDTHS:
            nc.tensor.matmul_mx(
                out=warm[:, first : first + width],
                lhsT=q_codes[:, 0:P].bitcast(FP8X4),
                lhsT_scale=warm_plane[:],
                rhs=halves[0][:].bitcast(U16)[:, 0:width].bitcast(FP4X4),
                rhs_scale=ks_g[0][:, 0:width],
                start=True,
                stop=True,
            )
            first = first + width
        part_keys(0, 0, halves[0], slice(1, 2))
        part_keys(0, 1, halves[1], slice(1, 2), slice(0, 2))
        part_keys(0, 1, halves[1], slice(1, 2), slice(2, 4))
        for a in (1, 0):
            part_keys(0, a, halves[a], slice(0, 1))
        halves = [gather_keys(1, a, 5 + 2 * a) for a in range(2)]
        for a in range(2):
            part_keys(1, a, halves[a], slice(0, PASSES))

        y = [ps.tile([P, DV], F32, name="y%d" % h, tag="y%d" % h) for h in range(Q_TILES)]

        def score_bank(u, h):
            scores = ps.tile([P, PACK, P], F32, name="scores%d%d" % (u, h))
            order = (1, 0) if (u, h) == (0, 0) else (0, 1)
            for o in order:
                for r in range(PACK):
                    k0 = o * PAGE + r * P
                    s0 = u * PAGE + r * P
                    q0 = N + h * P
                    nc.tensor.matmul_mx(
                        out=scores[:, r, :],
                        lhsT=k_codes[u][:, k0 : k0 + P].bitcast(FP4X4),
                        lhsT_scale=planes[o][:, s0 : s0 + P],
                        rhs=q_codes[:, o * NQ + h * P : o * NQ + (h + 1) * P].bitcast(FP8X4),
                        rhs_scale=planes[o][:, q0 : q0 + P],
                        start=(o == order[0] and r == 0),
                        stop=(o == order[1] and r == PACK - 1),
                    )
            return scores

        silu = {}
        for u in range(PAGES):
            for h in range(Q_TILES):
                scores = score_bank(u, h)
                act = sb.tile([P, P, PACK], F32, name="silu%d%d" % (u, h))
                for part in Q_PARTS:
                    nc.scalar.activation(out=act[:, part, :], in_=scores[:].rearrange("p r q -> p q r")[:, part, :], func=ACT.Silu)
                silu[(u, h)] = act

        half = shared.tile([P, Q_TILES, DV], F32, name="half", align_bytes=64, offset=11 * PAGE)
        gate = sb.tile([P, Q_TILES, DV], F32, name="gate")
        nc.scalar.activation(out=half[:], in_=og_t[:], func=ACT.Tanh, scale=0.5)
        nc.scalar.activation(out=gate[:], in_=half[:], func=ACT.Copy, scale=1.0 / 32.0, bias=1.0 / 32.0)

        def weigh(engine, u, h):
            w = sb.tile([P, P, PACK], BF16, name="w%d%d" % (u, h), align_bytes=64)
            for part in Q_PARTS:
                engine.tensor_tensor(w[:, part, :], silu[(u, h)][:, part, :], vs_col[u].unsqueeze(1).to_broadcast([P, P // 2, PACK]), ALU.mult)
            return w

        def quantise(u, h, w):
            w_codes = sb.tile([P, P], U32, name="w_codes%d%d" % (u, h), align_bytes=64)
            w_plane = sb.tile([P, P], U8, name="w_plane%d%d" % (u, h), align_bytes=64)
            nc.vector.quantize_mx(out=w_codes[:].bitcast(FP8X4), scales=w_plane[:], in_=w[:].rearrange("p q r -> p (q r)"))
            return w_codes, w_plane

        def accumulate(u, h, w_codes, w_plane):
            nc.tensor.matmul_mx(
                out=y[h][:],
                lhsT=w_codes[:].bitcast(FP8X4),
                lhsT_scale=w_plane[:],
                rhs=v_g[:, u * DV : (u + 1) * DV].bitcast(FP8X4),
                rhs_scale=v_plane[:, u * DV : (u + 1) * DV],
                start=(u == 0),
                stop=(u == PAGES - 1),
            )

        tiles = [(u, h) for u in range(PAGES) for h in range(Q_TILES)]
        weights = weigh(nc.vector, *tiles[0])
        v_g = sb.tile([P, PAGES * DV], U32, name="v_g", align_bytes=64)
        nc.vector.tensor_copy(v_g[:], v_pool[:].indirect(voffs_t[:]))
        codes = [quantise(*tiles[0], weights)]
        weights = weigh(nc.vector, *tiles[1])
        for i in range(1, len(tiles)):
            ahead = weigh(nc.vector, *tiles[i + 1]) if i + 1 < len(tiles) else None
            codes.append(quantise(*tiles[i], weights))
            weights = ahead
        for tile, made in zip(tiles, codes):
            accumulate(*tile, *made)

        for h in range(Q_TILES):
            res = sb.tile([P, DV], F32, name="res%d" % h)
            nc.vector.tensor_tensor(res[:], y[h][:], gate[:, h, :], ALU.mult)
            nc.sync.dma_start(out=out[0, h * P : (h + 1) * P, :], in_=res[:])
